import numpy as np
import ml_dtypes


def mxq(x, axis, fmt="e4m3"):
    dtype, down = {"e4m3": (ml_dtypes.float8_e4m3fn, 7), "e5m2": (ml_dtypes.float8_e5m2, 14)}[fmt]
    v = np.moveaxis(np.asarray(x, np.float32).astype(ml_dtypes.bfloat16).astype(np.float64), axis, -1)
    blocks = v.reshape(v.shape[:-1] + (-1, 32))
    amax = np.abs(blocks).max(-1, keepdims=True)
    byte = np.maximum(np.where(amax > 0, np.frexp(amax)[1] - 1 + 127, 0) - down, 1)
    scale = np.exp2(byte - 127.0)
    codes = (blocks / scale).astype(np.float32).astype(dtype).astype(np.float64)
    return np.moveaxis((codes * scale).reshape(v.shape), -1, axis)


WIDE = False


def mx_kscale(k):
    if not WIDE:
        return np.ones(k)
    levels = np.array([10, -10, 5, -5, 0])
    if k % 512:
        return np.exp2(np.random.permutation(np.resize(levels, k // 32))).repeat(32)
    a = np.empty((k // 512, 16))
    for p in range(k // 512):
        a[p, :8] = np.random.permutation(np.resize(levels, 8))
        for g in range(8):
            far = levels[np.abs(levels - a[p, g]) >= 10]
            a[p, g + 8] = far[np.random.randint(len(far))]
    return np.exp2(a.ravel()).repeat(32)


def f64(x):
    return np.asarray(x).astype(np.float64)


def striped(idx):
    return np.tile(idx.reshape(-1, 16).T, (8, 1)).astype(np.uint16)


def unstriped(offs):
    return offs[:16].T.reshape(-1).astype(np.int64)


E2M1 = np.array([0.0, 0.5, 1.0, 1.5, 2.0, 3.0, 4.0, 6.0, -0.0, -0.5, -1.0, -1.5, -2.0, -3.0, -4.0, -6.0])


def pack_weight(w, fmt):
    k, n = w.shape
    w = f64(np.asarray(w, np.float32).astype(ml_dtypes.bfloat16)).reshape(k // 32, 32, n)
    amax = np.abs(w).max(1)
    if fmt == "e4m3":
        byte = np.frexp(amax)[1] - 1 + 127 - 7
    else:
        mant, ex = np.frexp(amax / 6.0)
        byte = np.where(mant > 0.5, ex, ex - 1) + 127
    byte = np.clip(np.where(amax > 0, byte, 1), 1, 254)
    scaled = (w * np.exp2(127.0 - byte)[:, None, :]).reshape(k, n).astype(np.float32)
    by_word = np.ascontiguousarray(scaled.reshape(k // 512, 128, 4, n).transpose(0, 1, 3, 2))
    if fmt == "e4m3":
        words = by_word.astype(ml_dtypes.float8_e4m3fn).view(np.uint8)
    else:
        c = by_word.astype(ml_dtypes.float4_e2m1fn).view(np.uint8) & 0xF
        words = (c[..., 0::2] | (c[..., 1::2] << 4)).reshape(k // 512, 128, 2 * n)
    return np.ascontiguousarray(words), np.ascontiguousarray(byte.astype(np.uint8).reshape(k // 512, 16, n))


def unpack_weight(words, scales, fmt):
    g, _, n = scales.shape
    words = np.ascontiguousarray(words).reshape(g, 128, n, -1)
    if fmt == "e4m3":
        vals = words.view(ml_dtypes.float8_e4m3fn).astype(np.float64)
    else:
        nib = np.empty((g, 128, n, 4), np.uint8)
        nib[..., 0::2] = words & 0xF
        nib[..., 1::2] = words >> 4
        vals = E2M1[nib]
    vals = vals * np.repeat(np.exp2(scales.astype(np.float64) - 127.0), 8, axis=1)[..., None]
    return vals.transpose(0, 1, 3, 2).reshape(g * 512, n)


def gelu(v):
    return 0.5 * v * (1.0 + np.tanh(np.sqrt(2.0 / np.pi) * (v + 0.044715 * v**3)))


K, T, S, M, N, T2 = 1024, 2048, 1024, 512, 1024, 2048

def setup_inputs():
    n = np.random.standard_normal
    s = mx_kscale(K)[:, None]
    u = mx_kscale(M)[:, None]
    tab_words, tab_scales = pack_weight(2.0 * np.maximum(n((K, T)) - 0.5, 0.0) * s, "e4m3")
    A = n((K, M)) / np.sqrt(K)
    w1 = (A / s * u.T).astype(np.float32)
    wt_words, wt_scales = pack_weight(0.6 * A.T / u, "e2m1")
    keep_words, keep_scales = pack_weight((np.eye(K, N) + 0.5 * n((K, N)) / np.sqrt(K)) / s, "e4m3")
    return {"tab_words": tab_words, "tab_scales": tab_scales,
            "offs": striped(np.random.permutation(T)[:S]),
            "w1": w1,
            "meas": (n((M, S)) * u).astype(np.float32),
            "wt_words": wt_words, "wt_scales": wt_scales,
            "keep_words": keep_words, "keep_scales": keep_scales,
            "thr": (0.1 + 0.3 * np.abs(n(N))).astype(np.float32),
            "wgo": np.exp(0.3 * n((128, S))).astype(np.float32),
            "offs2": striped(np.random.permutation(T2)[:S])}

def reference(tab_words, tab_scales, offs, w1, meas, wt_words, wt_scales, keep_words, keep_scales, thr, wgo, offs2):
    v = unpack_weight(tab_words, tab_scales, "e4m3")[:, unstriped(offs)]
    wt = unpack_weight(wt_words, wt_scales, "e2m1")
    keep = unpack_weight(keep_words, keep_scales, "e4m3")
    h = f64(meas) - (mxq(f64(w1), 0, "e4m3").T @ v)
    z = keep.T @ v + wt.T @ mxq(h, 0, "e4m3")
    y = np.maximum(z - f64(thr)[:, None], 0.0)
    out = np.zeros((N, T2))
    out[:, unstriped(offs2)] = np.tile(f64(wgo), (N // 128, 1)) * y
    return out

@@ -1,0 +1,186 @@
+from contextlib import ExitStack
+
+import concourse.mybir as mybir
+from concourse.masks import make_identity
+
+K, T, S, M, N, T2 = 1024, 2048, 1024, 512, 1024, 2048
+FLOPS = 2 * S * (K * M + K * N + M * N)
+
+F32 = mybir.dt.float32
+BF16 = mybir.dt.bfloat16
+I32 = mybir.dt.int32
+U32 = mybir.dt.uint32
+U16 = mybir.dt.uint16
+U8 = mybir.dt.uint8
+FP8X4 = mybir.dt.float8_e4m3fn_x4
+FP4X4 = mybir.dt.float4_e2m1fn_x4
+ALU = mybir.AluOpType
+ACT = mybir.ActivationFunctionType
+
+P = 128
+PACK = 4
+PASSES = K // (P * PACK)
+HALF = 512
+HALVES = S // HALF
+SUB = 128
+BLOCKS = N // P
+EARLY = 256
+WINDOWS = 3
+
+
+def tile_list_sparse_code_step_kernel(
+    tc, tab_words, tab_scales, offs, w1, meas, wt_words, wt_scales, keep_words, keep_scales, thr, wgo, offs2, out
+):
+    nc = tc.nc
+    with ExitStack() as ctx:
+        held = ctx.enter_context(tc.tile_pool(name="held", bufs=1))
+        ring = ctx.enter_context(tc.tile_pool(name="ring", bufs=3))
+        psum_h = ctx.enter_context(tc.psum_pool(name="psum_h", bufs=3))
+        psum_z = ctx.enter_context(tc.psum_pool(name="psum_z", bufs=4))
+        psum_t = ctx.enter_context(tc.psum_pool(name="psum_t", bufs=1))
+
+        pick = held.tile([P, S // 16], U16, name="pick")
+        place = held.tile([P, S // 16], U16, name="place")
+        tab_w = [held.tile([P, T], I32, name=f"tab_w{a}", align_bytes=64) for a in range(PASSES)]
+        tab_s = held.tile([P, T], U8, name="tab_s", align_bytes=64)
+        w1_raw = [held.tile([P, PACK, M], F32, name=f"w1_raw{a}") for a in range(PASSES)]
+        meas_sb = [held.tile([P, PACK, HALF], F32, name=f"meas{u}") for u in range(HALVES)]
+        keep_early = held.tile([P, PASSES, EARLY], I32, name="keep_early", align_bytes=64)
+        keep_late = held.tile([P, PASSES, N - EARLY], I32, name="keep_late", align_bytes=64)
+        wt_w = held.tile([P, 2 * N], U8, name="wt_w", align_bytes=64)
+        weight_s = held.tile([P, N], U8, name="weight_s", align_bytes=64)
+        wgo_sb = held.tile([P, S], F32, name="wgo_sb")
+        thr_rows = held.tile([P, P], F32, name="thr_rows")
+        ident = held.tile([P, P], F32, name="ident")
+        neg_thr = held.tile([P, BLOCKS], F32, name="neg_thr")
+        windows = [held.tile([P, T2], F32, name=f"window{i}") for i in range(WINDOWS)]
+
+        make_identity(nc, ident[:])
+        nc.vector.memset(tab_s[:].bitcast(I32), 0)
+        nc.vector.memset(weight_s[:].bitcast(I32), 0)
+        nc.vector.memset(thr_rows[:], 0.0)
+        for q in range(4):
+            nc.gpsimd.dma_start(
+                out=tab_s[32 * q : 32 * q + 8, :].bitcast(I32), in_=tab_scales[:, 4 * q : 4 * q + 4, :].bitcast(I32)
+            )
+
+        keep_view = keep_words.rearrange("a p c i -> p a (c i)")
+        meas_view = meas.rearrange("(p t) j -> p t j", t=PACK)
+        nc.sync.dma_start(pick[:], offs)
+        for a in range(PASSES):
+            nc.sync.dma_start(
+                out=w1_raw[a][:], in_=w1[512 * a : 512 * (a + 1), :].rearrange("(p i) c -> p i c", i=PACK)
+            )
+            nc.sync.dma_start(out=tab_w[a][:], in_=tab_words[a].rearrange("p t i -> p (t i)").bitcast(I32))
+        for u in range(HALVES):
+            nc.sync.dma_start(out=meas_sb[u][:], in_=meas_view[:, :, u * HALF : (u + 1) * HALF])
+        nc.sync.dma_start(out=keep_early[:], in_=keep_view[:, :, 0 : 4 * EARLY].bitcast(I32))
+        nc.sync.dma_start(out=thr_rows[0:BLOCKS, :], in_=thr.rearrange("(b p) -> b p", p=P))
+        nc.sync.dma_start(place[:], offs2)
+        nc.sync.dma_start(out=wt_w[:].bitcast(I32), in_=wt_words[0].bitcast(I32))
+        nc.sync.dma_start(out=wgo_sb[:], in_=wgo)
+        nc.sync.dma_start(out=keep_late[:], in_=keep_view[:, :, 4 * EARLY : 4 * N].bitcast(I32))
+
+        for q in range(4):
+            nc.gpsimd.dma_start(
+                out=weight_s[32 * q + 4 : 32 * q + 12, :].bitcast(I32),
+                in_=keep_scales[:, 4 * q : 4 * q + 4, :].bitcast(I32),
+            )
+            nc.gpsimd.dma_start(
+                out=weight_s[32 * q : 32 * q + 4, :].bitcast(I32), in_=wt_scales[0, 4 * q : 4 * q + 4, :].bitcast(I32)
+            )
+
+        for window in windows:
+            nc.vector.memset(window[:], 0.0)
+
+        w1_w = [held.tile([P, M], U32, name=f"w1_w{a}", align_bytes=64) for a in range(PASSES)]
+        w1_s = [held.tile([P, M], U8, name=f"w1_s{a}", align_bytes=64) for a in range(PASSES)]
+        v_w = [[held.tile([P, HALF], U32, name=f"v_w{a}_{u}", align_bytes=64) for u in range(HALVES)] for a in range(PASSES)]
+        v_s = held.tile([P, S], U8, name="v_s", align_bytes=64)
+
+        def quantize_w1(a):
+            grouped = held.tile([P, PACK * M], BF16, name=f"w1_grouped{a}", align_bytes=64)
+            nc.scalar.copy(
+                out=grouped[:].rearrange("p (t m i) -> p m t i", t=PACK, i=PACK),
+                in_=w1_raw[a][:].rearrange("p i (m t) -> p m t i", t=PACK),
+            )
+            nc.vector.quantize_mx(out=w1_w[a][:].bitcast(FP8X4), scales=w1_s[a][:], in_=grouped[:])
+
+        def gather_words(a, u):
+            cols = slice(u * HALF // 16, (u + 1) * HALF // 16)
+            nc.vector.tensor_copy(v_w[a][u][:], tab_w[a][:].bitcast(U32).indirect(pick[:, cols]))
+
+        nc.vector.tensor_copy(v_s[:], tab_s[:].indirect(pick[:]))
+        for a in range(PASSES):
+            quantize_w1(a)
+            for u in range(HALVES):
+                gather_words(a, u)
+
+        thr_ps = psum_t.tile([P, P], F32, name="thr_ps")
+        nc.tensor.transpose(thr_ps[:], thr_rows[:], ident[:])
+        nc.scalar.mul(neg_thr[:], thr_ps[:, 0:BLOCKS], -1.0)
+
+        h_w = [held.tile([P, HALF], U32, name=f"h_w{u}", align_bytes=64) for u in range(HALVES)]
+        h_s = [held.tile([P, HALF], U8, name=f"h_s{u}", align_bytes=64) for u in range(HALVES)]
+        for u in range(HALVES):
+            h_grouped = held.tile([P, HALF, PACK], BF16, name=f"h_grouped{u}", align_bytes=64)
+            for s in range(HALF // SUB):
+                js = slice(s * SUB, (s + 1) * SUB)
+                js_all = slice(u * HALF + s * SUB, u * HALF + (s + 1) * SUB)
+                pred = psum_h.tile([P, PACK, SUB], F32, name="pred")
+                for t in range(PACK):
+                    ms = slice(t * P, (t + 1) * P)
+                    for a in range(PASSES):
+                        nc.tensor.matmul_mx(
+                            out=pred[:, t, :],
+                            lhsT=w1_w[a][:, ms].bitcast(FP8X4),
+                            lhsT_scale=w1_s[a][:, ms],
+                            rhs=v_w[a][u][:, js].bitcast(FP8X4),
+                            rhs_scale=v_s[4 * a :, js_all],
+                            start=(a == 0),
+                            stop=(a == PASSES - 1),
+                        )
+                nc.vector.tensor_tensor(
+                    h_grouped[:, js, :].rearrange("p (c i) t -> p c t i", i=4),
+                    meas_sb[u][:, :, js].rearrange("p t (c i) -> p c t i", i=4),
+                    pred[:].rearrange("p t (c i) -> p c t i", i=4),
+                    ALU.subtract,
+                )
+            nc.vector.quantize_mx(
+                out=h_w[u][:].bitcast(FP8X4), scales=h_s[u][:], in_=h_grouped[:].rearrange("p j t -> p (j t)")
+            )
+
+        for b in range(BLOCKS):
+            ns = slice(b * P, (b + 1) * P)
+            y = ring.tile([P, S], F32, name="y")
+            weighted = ring.tile([P, S], F32, name="weighted")
+            for u in range(HALVES):
+                js_all = slice(u * HALF, (u + 1) * HALF)
+                z = psum_z.tile([P, HALF], F32, name="z")
+                for a in range(PASSES):
+                    keep_cols = (
+                        keep_early[:, a, ns] if b * P < EARLY else keep_late[:, a, b * P - EARLY : (b + 1) * P - EARLY]
+                    )
+                    nc.tensor.matmul_mx(
+                        out=z[:],
+                        lhsT=keep_cols.bitcast(FP8X4),
+                        lhsT_scale=weight_s[4 + 4 * a :, ns],
+                        rhs=v_w[a][u][:].bitcast(FP8X4),
+                        rhs_scale=v_s[4 * a :, js_all],
+                        start=(a == 0),
+                        stop=False,
+                    )
+                nc.tensor.matmul_mx(
+                    out=z[:],
+                    lhsT=wt_w[:, 2 * b * P : 2 * (b + 1) * P].bitcast(FP4X4),
+                    lhsT_scale=weight_s[:, ns],
+                    rhs=h_w[u][:].bitcast(FP8X4),
+                    rhs_scale=h_s[u][:],
+                    start=False,
+                    stop=True,
+                )
+                nc.scalar.activation(y[:, js_all], z[:], ACT.Relu, bias=neg_thr[:, b : b + 1])
+                nc.gpsimd.tensor_tensor(weighted[:, js_all], y[:, js_all], wgo_sb[:, js_all], ALU.mult)
+            window = windows[b % WINDOWS]
+            nc.vector.tensor_copy(window[:].indirect(place[:]), weighted[:])
+            nc.sync.dma_start(out=out[ns, :], in_=window[:])

@@ -20,8 +20,8 @@ ACT = mybir.ActivationFunctionType
 P = 128
 PACK = 4
 PASSES = K // (P * PACK)
-HALF = 512
-HALVES = S // HALF
+BANK = 512
+QUARTER = 256
 SUB = 128
 BLOCKS = N // P
 EARLY = 256
@@ -34,7 +34,7 @@ def tile_list_sparse_code_step_kernel(
     nc = tc.nc
     with ExitStack() as ctx:
         held = ctx.enter_context(tc.tile_pool(name="held", bufs=1))
-        ring = ctx.enter_context(tc.tile_pool(name="ring", bufs=3))
+        ring = ctx.enter_context(tc.tile_pool(name="ring", bufs=4))
         psum_h = ctx.enter_context(tc.psum_pool(name="psum_h", bufs=3))
         psum_z = ctx.enter_context(tc.psum_pool(name="psum_z", bufs=4))
         psum_t = ctx.enter_context(tc.psum_pool(name="psum_t", bufs=1))
@@ -43,10 +43,9 @@ def tile_list_sparse_code_step_kernel(
         place = held.tile([P, S // 16], U16, name="place")
         tab_w = [held.tile([P, T], I32, name=f"tab_w{a}", align_bytes=64) for a in range(PASSES)]
         tab_s = held.tile([P, T], U8, name="tab_s", align_bytes=64)
-        w1_raw = [held.tile([P, PACK, M], F32, name=f"w1_raw{a}") for a in range(PASSES)]
-        meas_sb = [held.tile([P, PACK, HALF], F32, name=f"meas{u}") for u in range(HALVES)]
-        keep_early = held.tile([P, PASSES, EARLY], I32, name="keep_early", align_bytes=64)
-        keep_late = held.tile([P, PASSES, N - EARLY], I32, name="keep_late", align_bytes=64)
+        w1_raw = [[held.tile([P, PACK, M // 2], F32, name=f"w1_raw{a}_{c}") for c in range(2)] for a in range(PASSES)]
+        meas_sb = held.tile([P, PACK, S], F32, name="meas_sb")
+        keep_w = held.tile([P, PASSES, N], I32, name="keep_w", align_bytes=64)
         wt_w = held.tile([P, 2 * N], U8, name="wt_w", align_bytes=64)
         weight_s = held.tile([P, N], U8, name="weight_s", align_bytes=64)
         wgo_sb = held.tile([P, S], F32, name="wgo_sb")
@@ -59,74 +58,95 @@ def tile_list_sparse_code_step_kernel(
         nc.vector.memset(tab_s[:].bitcast(I32), 0)
         nc.vector.memset(weight_s[:].bitcast(I32), 0)
         nc.vector.memset(thr_rows[:], 0.0)
+        for window in windows:
+            nc.vector.memset(window[:], 0.0)
         for q in range(4):
             nc.gpsimd.dma_start(
                 out=tab_s[32 * q : 32 * q + 8, :].bitcast(I32), in_=tab_scales[:, 4 * q : 4 * q + 4, :].bitcast(I32)
             )
-
-        keep_view = keep_words.rearrange("a p c i -> p a (c i)")
-        meas_view = meas.rearrange("(p t) j -> p t j", t=PACK)
-        nc.sync.dma_start(pick[:], offs)
-        for a in range(PASSES):
-            nc.sync.dma_start(
-                out=w1_raw[a][:], in_=w1[512 * a : 512 * (a + 1), :].rearrange("(p i) c -> p i c", i=PACK)
-            )
-            nc.sync.dma_start(out=tab_w[a][:], in_=tab_words[a].rearrange("p t i -> p (t i)").bitcast(I32))
-        for u in range(HALVES):
-            nc.sync.dma_start(out=meas_sb[u][:], in_=meas_view[:, :, u * HALF : (u + 1) * HALF])
-        nc.sync.dma_start(out=keep_early[:], in_=keep_view[:, :, 0 : 4 * EARLY].bitcast(I32))
-        nc.sync.dma_start(out=thr_rows[0:BLOCKS, :], in_=thr.rearrange("(b p) -> b p", p=P))
-        nc.sync.dma_start(place[:], offs2)
-        nc.sync.dma_start(out=wt_w[:].bitcast(I32), in_=wt_words[0].bitcast(I32))
-        nc.sync.dma_start(out=wgo_sb[:], in_=wgo)
-        nc.sync.dma_start(out=keep_late[:], in_=keep_view[:, :, 4 * EARLY : 4 * N].bitcast(I32))
-
+        nc.gpsimd.dma_start(out=thr_rows[0:BLOCKS, :], in_=thr.rearrange("(b p) -> b p", p=P))
         for q in range(4):
-            nc.gpsimd.dma_start(
-                out=weight_s[32 * q + 4 : 32 * q + 12, :].bitcast(I32),
-                in_=keep_scales[:, 4 * q : 4 * q + 4, :].bitcast(I32),
-            )
             nc.gpsimd.dma_start(
                 out=weight_s[32 * q : 32 * q + 4, :].bitcast(I32), in_=wt_scales[0, 4 * q : 4 * q + 4, :].bitcast(I32)
             )
 
-        for window in windows:
-            nc.vector.memset(window[:], 0.0)
+        keep_view = keep_words.rearrange("a p c i -> p a (c i)")
+        meas_view = meas.rearrange("(p t) j -> p t j", t=PACK)
 
+        def load_table(a):
+            nc.sync.dma_start(out=tab_w[a][:], in_=tab_words[a].rearrange("p t i -> p (t i)").bitcast(I32))
+
+        def load_meas(j0, j1):
+            nc.sync.dma_start(out=meas_sb[:, :, j0:j1], in_=meas_view[:, :, j0:j1])
+
+        def load_keep(n0, n1):
+            nc.sync.dma_start(out=keep_w[:, :, n0:n1], in_=keep_view[:, :, 4 * n0 : 4 * n1].bitcast(I32))
+
+        nc.sync.dma_start(pick[:], offs)
+        load_table(0)
+        for a in range(PASSES):
+            rows = w1[512 * a : 512 * (a + 1), :].rearrange("(p i) c -> p i c", i=PACK)
+            for c in range(2):
+                nc.sync.dma_start(out=w1_raw[a][c][:], in_=rows[:, :, c * M // 2 : (c + 1) * M // 2])
+        load_table(1)
+        load_meas(0, QUARTER)
+        for q in range(4):
+            nc.sync.dma_start(
+                out=weight_s[32 * q + 4 : 32 * q + 12, :].bitcast(I32),
+                in_=keep_scales[:, 4 * q : 4 * q + 4, :].bitcast(I32),
+            )
+        load_keep(0, EARLY)
+        nc.sync.dma_start(out=wt_w[:].bitcast(I32), in_=wt_words[0].bitcast(I32))
+        load_meas(QUARTER, BANK)
+        nc.sync.dma_start(out=wgo_sb[:, 0:BANK], in_=wgo[:, 0:BANK])
+        nc.sync.dma_start(place[:], offs2)
+        load_meas(BANK, S)
+        nc.sync.dma_start(out=wgo_sb[:, BANK:S], in_=wgo[:, BANK:S])
+        load_keep(EARLY, N)
+
+        w1_grouped = [held.tile([P, PACK, P, PACK], BF16, name=f"w1_grouped{a}", align_bytes=64) for a in range(PASSES)]
         w1_w = [held.tile([P, M], U32, name=f"w1_w{a}", align_bytes=64) for a in range(PASSES)]
         w1_s = [held.tile([P, M], U8, name=f"w1_s{a}", align_bytes=64) for a in range(PASSES)]
-        v_w = [[held.tile([P, HALF], U32, name=f"v_w{a}_{u}", align_bytes=64) for u in range(HALVES)] for a in range(PASSES)]
+        v_w = [held.tile([P, S], U32, name=f"v_w{a}", align_bytes=64) for a in range(PASSES)]
         v_s = held.tile([P, S], U8, name="v_s", align_bytes=64)
+        h_grouped = held.tile([P, S, PACK], BF16, name="h_grouped", align_bytes=64)
+        h_w = held.tile([P, S], U32, name="h_w", align_bytes=64)
+        h_s = held.tile([P, S], U8, name="h_s", align_bytes=64)
+
+        def group_w1(a, c, copy):
+            copy(
+                out=w1_grouped[a][:, :, c * P // 2 : (c + 1) * P // 2, :].rearrange("p t m i -> p m t i"),
+                in_=w1_raw[a][c][:].rearrange("p i (m t) -> p m t i", t=PACK),
+            )
 
         def quantize_w1(a):
-            grouped = held.tile([P, PACK * M], BF16, name=f"w1_grouped{a}", align_bytes=64)
-            nc.scalar.copy(
-                out=grouped[:].rearrange("p (t m i) -> p m t i", t=PACK, i=PACK),
-                in_=w1_raw[a][:].rearrange("p i (m t) -> p m t i", t=PACK),
+            nc.vector.quantize_mx(
+                out=w1_w[a][:].bitcast(FP8X4),
+                scales=w1_s[a][:],
+                in_=w1_grouped[a][:].rearrange("p t m i -> p (t m i)"),
             )
-            nc.vector.quantize_mx(out=w1_w[a][:].bitcast(FP8X4), scales=w1_s[a][:], in_=grouped[:])
 
-        def gather_words(a, u):
-            cols = slice(u * HALF // 16, (u + 1) * HALF // 16)
-            nc.vector.tensor_copy(v_w[a][u][:], tab_w[a][:].bitcast(U32).indirect(pick[:, cols]))
+        def gather_words(a, j0, j1):
+            nc.vector.tensor_copy(v_w[a][:, j0:j1], tab_w[a][:].bitcast(U32).indirect(pick[:, j0 // 16 : j1 // 16]))
 
+        gather_words(0, 0, S)
         nc.vector.tensor_copy(v_s[:], tab_s[:].indirect(pick[:]))
-        for a in range(PASSES):
-            quantize_w1(a)
-            for u in range(HALVES):
-                gather_words(a, u)
+        group_w1(0, 0, nc.scalar.copy)
+        group_w1(0, 1, nc.scalar.copy)
+        group_w1(1, 0, nc.scalar.copy)
+        group_w1(1, 1, nc.vector.tensor_copy)
+        quantize_w1(0)
+        quantize_w1(1)
+        gather_words(1, 0, QUARTER)
+        gather_words(1, QUARTER, BANK)
 
         thr_ps = psum_t.tile([P, P], F32, name="thr_ps")
         nc.tensor.transpose(thr_ps[:], thr_rows[:], ident[:])
         nc.scalar.mul(neg_thr[:], thr_ps[:, 0:BLOCKS], -1.0)
 
-        h_w = [held.tile([P, HALF], U32, name=f"h_w{u}", align_bytes=64) for u in range(HALVES)]
-        h_s = [held.tile([P, HALF], U8, name=f"h_s{u}", align_bytes=64) for u in range(HALVES)]
-        for u in range(HALVES):
-            h_grouped = held.tile([P, HALF, PACK], BF16, name=f"h_grouped{u}", align_bytes=64)
-            for s in range(HALF // SUB):
-                js = slice(s * SUB, (s + 1) * SUB)
-                js_all = slice(u * HALF + s * SUB, u * HALF + (s + 1) * SUB)
+        def residual(quarter, on_vector):
+            for j0 in range(quarter * QUARTER, (quarter + 1) * QUARTER, SUB):
+                js = slice(j0, j0 + SUB)
                 pred = psum_h.tile([P, PACK, SUB], F32, name="pred")
                 for t in range(PACK):
                     ms = slice(t * P, (t + 1) * P)
@@ -135,52 +155,85 @@ def tile_list_sparse_code_step_kernel(
                             out=pred[:, t, :],
                             lhsT=w1_w[a][:, ms].bitcast(FP8X4),
                             lhsT_scale=w1_s[a][:, ms],
-                            rhs=v_w[a][u][:, js].bitcast(FP8X4),
-                            rhs_scale=v_s[4 * a :, js_all],
+                            rhs=v_w[a][:, js].bitcast(FP8X4),
+                            rhs_scale=v_s[4 * a :, js],
                             start=(a == 0),
                             stop=(a == PASSES - 1),
                         )
-                nc.vector.tensor_tensor(
-                    h_grouped[:, js, :].rearrange("p (c i) t -> p c t i", i=4),
-                    meas_sb[u][:, :, js].rearrange("p t (c i) -> p c t i", i=4),
-                    pred[:].rearrange("p t (c i) -> p c t i", i=4),
-                    ALU.subtract,
-                )
+                if on_vector:
+                    nc.vector.tensor_tensor(
+                        h_grouped[:, js, :].rearrange("p (c i) t -> p c t i", i=4),
+                        meas_sb[:, :, js].rearrange("p t (c i) -> p c t i", i=4),
+                        pred[:].rearrange("p t (c i) -> p c t i", i=4),
+                        ALU.subtract,
+                    )
+                else:
+                    pred_sb = ring.tile([P, SUB, PACK], F32, name="pred_sb")
+                    nc.scalar.copy(out=pred_sb[:], in_=pred[:].rearrange("p t j -> p j t"))
+                    nc.gpsimd.tensor_tensor(
+                        h_grouped[:, js, :], meas_sb[:, :, js].rearrange("p t j -> p j t"), pred_sb[:], ALU.subtract
+                    )
+            qs = slice(quarter * QUARTER, (quarter + 1) * QUARTER)
             nc.vector.quantize_mx(
-                out=h_w[u][:].bitcast(FP8X4), scales=h_s[u][:], in_=h_grouped[:].rearrange("p j t -> p (j t)")
+                out=h_w[:, qs].bitcast(FP8X4), scales=h_s[:, qs], in_=h_grouped[:, qs, :].rearrange("p j t -> p (j t)")
             )
 
-        for b in range(BLOCKS):
+        def shrink(b, j0, j1, weigh):
             ns = slice(b * P, (b + 1) * P)
-            y = ring.tile([P, S], F32, name="y")
-            weighted = ring.tile([P, S], F32, name="weighted")
-            for u in range(HALVES):
-                js_all = slice(u * HALF, (u + 1) * HALF)
-                z = psum_z.tile([P, HALF], F32, name="z")
-                for a in range(PASSES):
-                    keep_cols = (
-                        keep_early[:, a, ns] if b * P < EARLY else keep_late[:, a, b * P - EARLY : (b + 1) * P - EARLY]
-                    )
+            y = ring.tile([P, j1 - j0], F32, name="y")
+            weighted = ring.tile([P, j1 - j0], F32, name="weighted") if weigh else y
+            for c0 in range(j0, j1, BANK):
+                c1 = min(c0 + BANK, j1)
+                width = BANK if c1 - c0 == BANK else SUB
+                z = psum_z.tile([P, c1 - c0], F32, name="z")
+                for g0 in range(c0, c1, width):
+                    js = slice(g0, g0 + width)
+                    acc = z[:, g0 - c0 : g0 - c0 + width]
+                    for a in range(PASSES):
+                        nc.tensor.matmul_mx(
+                            out=acc,
+                            lhsT=keep_w[:, a, ns].bitcast(FP8X4),
+                            lhsT_scale=weight_s[4 + 4 * a :, ns],
+                            rhs=v_w[a][:, js].bitcast(FP8X4),
+                            rhs_scale=v_s[4 * a :, js],
+                            start=(a == 0),
+                            stop=False,
+                        )
                     nc.tensor.matmul_mx(
-                        out=z[:],
-                        lhsT=keep_cols.bitcast(FP8X4),
-                        lhsT_scale=weight_s[4 + 4 * a :, ns],
-                        rhs=v_w[a][u][:].bitcast(FP8X4),
-                        rhs_scale=v_s[4 * a :, js_all],
-                        start=(a == 0),
-                        stop=False,
+                        out=acc,
+                        lhsT=wt_w[:, 2 * b * P : 2 * (b + 1) * P].bitcast(FP4X4),
+                        lhsT_scale=weight_s[:, ns],
+                        rhs=h_w[:, js].bitcast(FP8X4),
+                        rhs_scale=h_s[:, js],
+                        start=False,
+                        stop=True,
                     )
-                nc.tensor.matmul_mx(
-                    out=z[:],
-                    lhsT=wt_w[:, 2 * b * P : 2 * (b + 1) * P].bitcast(FP4X4),
-                    lhsT_scale=weight_s[:, ns],
-                    rhs=h_w[u][:].bitcast(FP8X4),
-                    rhs_scale=h_s[u][:],
-                    start=False,
-                    stop=True,
-                )
-                nc.scalar.activation(y[:, js_all], z[:], ACT.Relu, bias=neg_thr[:, b : b + 1])
-                nc.gpsimd.tensor_tensor(weighted[:, js_all], y[:, js_all], wgo_sb[:, js_all], ALU.mult)
+                local = slice(c0 - j0, c1 - j0)
+                nc.scalar.activation(y[:, local], z[:], ACT.Relu, bias=neg_thr[:, b : b + 1])
+                if weigh:
+                    nc.gpsimd.tensor_tensor(weighted[:, local], y[:, local], wgo_sb[:, c0:c1], ALU.mult)
+            return weighted
+
+        def scatter(b, j0, j1, values):
             window = windows[b % WINDOWS]
-            nc.vector.tensor_copy(window[:].indirect(place[:]), weighted[:])
-            nc.sync.dma_start(out=out[ns, :], in_=window[:])
+            nc.vector.tensor_copy(window[:].indirect(place[:, j0 // 16 : j1 // 16]), values[:])
+            if j1 == S:
+                nc.sync.dma_start(out=out[b * P : (b + 1) * P, :], in_=window[:])
+
+        residual(0, True)
+        first = shrink(0, 0, QUARTER, False)
+        residual(1, True)
+        gather_words(1, BANK, S)
+        nc.vector.tensor_tensor(
+            windows[0][:].indirect(place[:, 0 : QUARTER // 16]), first[:], wgo_sb[:, 0:QUARTER], ALU.mult
+        )
+        scatter(0, QUARTER, BANK, shrink(0, QUARTER, BANK, True))
+        for b in (1, 2):
+            values = shrink(b, 0, BANK, True)
+            residual(b + 1, False)
+            scatter(b, 0, BANK, values)
+        for b, quarter in ((0, 2), (1, 2), (0, 3), (2, 2), (1, 3), (2, 3)):
+            j0, j1 = quarter * QUARTER, (quarter + 1) * QUARTER
+            scatter(b, j0, j1, shrink(b, j0, j1, True))
+        for b in range(WINDOWS, BLOCKS):
+            scatter(b, 0, S, shrink(b, 0, S, True))

@@ -43,7 +43,7 @@ def tile_list_sparse_code_step_kernel(
         place = held.tile([P, S // 16], U16, name="place")
         tab_w = [held.tile([P, T], I32, name=f"tab_w{a}", align_bytes=64) for a in range(PASSES)]
         tab_s = held.tile([P, T], U8, name="tab_s", align_bytes=64)
-        w1_raw = [[held.tile([P, PACK, M // 2], F32, name=f"w1_raw{a}_{c}") for c in range(2)] for a in range(PASSES)]
+        w1_raw = [held.tile([P, PACK, M], F32, name=f"w1_raw{a}") for a in range(PASSES)]
         meas_sb = held.tile([P, PACK, S], F32, name="meas_sb")
         keep_w = held.tile([P, PASSES, N], I32, name="keep_w", align_bytes=64)
         wt_w = held.tile([P, 2 * N], U8, name="wt_w", align_bytes=64)
@@ -54,16 +54,12 @@ def tile_list_sparse_code_step_kernel(
         neg_thr = held.tile([P, BLOCKS], F32, name="neg_thr")
         windows = [held.tile([P, T2], F32, name=f"window{i}") for i in range(WINDOWS)]
 
+        nc.gpsimd.memset(tab_s[:].bitcast(I32), 0)
+        nc.gpsimd.memset(weight_s[:].bitcast(I32), 0)
+        nc.gpsimd.memset(thr_rows[:], 0.0)
         make_identity(nc, ident[:])
-        nc.vector.memset(tab_s[:].bitcast(I32), 0)
-        nc.vector.memset(weight_s[:].bitcast(I32), 0)
-        nc.vector.memset(thr_rows[:], 0.0)
         for window in windows:
-            nc.vector.memset(window[:], 0.0)
-        for q in range(4):
-            nc.gpsimd.dma_start(
-                out=tab_s[32 * q : 32 * q + 8, :].bitcast(I32), in_=tab_scales[:, 4 * q : 4 * q + 4, :].bitcast(I32)
-            )
+            nc.gpsimd.memset(window[:], 0.0)
         nc.gpsimd.dma_start(out=thr_rows[0:BLOCKS, :], in_=thr.rearrange("(b p) -> b p", p=P))
         for q in range(4):
             nc.gpsimd.dma_start(
@@ -82,14 +78,22 @@ def tile_list_sparse_code_step_kernel(
         def load_keep(n0, n1):
             nc.sync.dma_start(out=keep_w[:, :, n0:n1], in_=keep_view[:, :, 4 * n0 : 4 * n1].bitcast(I32))
 
+        def load_w1(a):
+            nc.sync.dma_start(
+                out=w1_raw[a][:], in_=w1[512 * a : 512 * (a + 1), :].rearrange("(p i) c -> p i c", i=PACK)
+            )
+
         nc.sync.dma_start(pick[:], offs)
+        load_w1(0)
+        for q in range(4):
+            nc.sync.dma_start(
+                out=tab_s[32 * q : 32 * q + 8, :].bitcast(I32), in_=tab_scales[:, 4 * q : 4 * q + 4, :].bitcast(I32)
+            )
         load_table(0)
-        for a in range(PASSES):
-            rows = w1[512 * a : 512 * (a + 1), :].rearrange("(p i) c -> p i c", i=PACK)
-            for c in range(2):
-                nc.sync.dma_start(out=w1_raw[a][c][:], in_=rows[:, :, c * M // 2 : (c + 1) * M // 2])
+        load_w1(1)
         load_table(1)
-        load_meas(0, QUARTER)
+        load_meas(0, BANK)
+        load_meas(BANK, S)
         for q in range(4):
             nc.sync.dma_start(
                 out=weight_s[32 * q + 4 : 32 * q + 12, :].bitcast(I32),
@@ -97,11 +101,8 @@ def tile_list_sparse_code_step_kernel(
             )
         load_keep(0, EARLY)
         nc.sync.dma_start(out=wt_w[:].bitcast(I32), in_=wt_words[0].bitcast(I32))
-        load_meas(QUARTER, BANK)
-        nc.sync.dma_start(out=wgo_sb[:, 0:BANK], in_=wgo[:, 0:BANK])
+        nc.sync.dma_start(out=wgo_sb[:], in_=wgo)
         nc.sync.dma_start(place[:], offs2)
-        load_meas(BANK, S)
-        nc.sync.dma_start(out=wgo_sb[:, BANK:S], in_=wgo[:, BANK:S])
         load_keep(EARLY, N)
 
         w1_grouped = [held.tile([P, PACK, P, PACK], BF16, name=f"w1_grouped{a}", align_bytes=64) for a in range(PASSES)]
@@ -113,10 +114,10 @@ def tile_list_sparse_code_step_kernel(
         h_w = held.tile([P, S], U32, name="h_w", align_bytes=64)
         h_s = held.tile([P, S], U8, name="h_s", align_bytes=64)
 
-        def group_w1(a, c, copy):
+        def group_w1(a, m0, m1, copy):
             copy(
-                out=w1_grouped[a][:, :, c * P // 2 : (c + 1) * P // 2, :].rearrange("p t m i -> p m t i"),
-                in_=w1_raw[a][c][:].rearrange("p i (m t) -> p m t i", t=PACK),
+                out=w1_grouped[a][:, :, m0:m1, :].rearrange("p t m i -> p m t i"),
+                in_=w1_raw[a][:, :, PACK * m0 : PACK * m1].rearrange("p i (m t) -> p m t i", t=PACK),
             )
 
         def quantize_w1(a):
@@ -129,23 +130,23 @@ def tile_list_sparse_code_step_kernel(
         def gather_words(a, j0, j1):
             nc.vector.tensor_copy(v_w[a][:, j0:j1], tab_w[a][:].bitcast(U32).indirect(pick[:, j0 // 16 : j1 // 16]))
 
-        gather_words(0, 0, S)
         nc.vector.tensor_copy(v_s[:], tab_s[:].indirect(pick[:]))
-        group_w1(0, 0, nc.scalar.copy)
-        group_w1(0, 1, nc.scalar.copy)
-        group_w1(1, 0, nc.scalar.copy)
-        group_w1(1, 1, nc.vector.tensor_copy)
+        group_w1(0, 0, P, nc.scalar.copy)
         quantize_w1(0)
+        gather_words(0, 0, S)
+        group_w1(1, 0, P // 2, nc.scalar.copy)
+        group_w1(1, P // 2, P, nc.vector.tensor_copy)
         quantize_w1(1)
         gather_words(1, 0, QUARTER)
         gather_words(1, QUARTER, BANK)
+        gather_words(1, BANK, S)
 
         thr_ps = psum_t.tile([P, P], F32, name="thr_ps")
         nc.tensor.transpose(thr_ps[:], thr_rows[:], ident[:])
         nc.scalar.mul(neg_thr[:], thr_ps[:, 0:BLOCKS], -1.0)
 
-        def residual(quarter, on_vector):
-            for j0 in range(quarter * QUARTER, (quarter + 1) * QUARTER, SUB):
+        def residual(half):
+            for j0 in range(half * BANK, (half + 1) * BANK, SUB):
                 js = slice(j0, j0 + SUB)
                 pred = psum_h.tile([P, PACK, SUB], F32, name="pred")
                 for t in range(PACK):
@@ -160,80 +161,57 @@ def tile_list_sparse_code_step_kernel(
                             start=(a == 0),
                             stop=(a == PASSES - 1),
                         )
-                if on_vector:
-                    nc.vector.tensor_tensor(
-                        h_grouped[:, js, :].rearrange("p (c i) t -> p c t i", i=4),
-                        meas_sb[:, :, js].rearrange("p t (c i) -> p c t i", i=4),
-                        pred[:].rearrange("p t (c i) -> p c t i", i=4),
-                        ALU.subtract,
-                    )
-                else:
-                    pred_sb = ring.tile([P, SUB, PACK], F32, name="pred_sb")
-                    nc.scalar.copy(out=pred_sb[:], in_=pred[:].rearrange("p t j -> p j t"))
-                    nc.gpsimd.tensor_tensor(
-                        h_grouped[:, js, :], meas_sb[:, :, js].rearrange("p t j -> p j t"), pred_sb[:], ALU.subtract
-                    )
-            qs = slice(quarter * QUARTER, (quarter + 1) * QUARTER)
+                nc.vector.tensor_tensor(
+                    h_grouped[:, js, :].rearrange("p (c i) t -> p c t i", i=4),
+                    meas_sb[:, :, js].rearrange("p t (c i) -> p c t i", i=4),
+                    pred[:].rearrange("p t (c i) -> p c t i", i=4),
+                    ALU.subtract,
+                )
+            qs = slice(half * BANK, (half + 1) * BANK)
             nc.vector.quantize_mx(
                 out=h_w[:, qs].bitcast(FP8X4), scales=h_s[:, qs], in_=h_grouped[:, qs, :].rearrange("p j t -> p (j t)")
             )
 
-        def shrink(b, j0, j1, weigh):
+        def shrink(b, j0, j1):
             ns = slice(b * P, (b + 1) * P)
             y = ring.tile([P, j1 - j0], F32, name="y")
-            weighted = ring.tile([P, j1 - j0], F32, name="weighted") if weigh else y
             for c0 in range(j0, j1, BANK):
-                c1 = min(c0 + BANK, j1)
-                width = BANK if c1 - c0 == BANK else SUB
-                z = psum_z.tile([P, c1 - c0], F32, name="z")
-                for g0 in range(c0, c1, width):
-                    js = slice(g0, g0 + width)
-                    acc = z[:, g0 - c0 : g0 - c0 + width]
-                    for a in range(PASSES):
-                        nc.tensor.matmul_mx(
-                            out=acc,
-                            lhsT=keep_w[:, a, ns].bitcast(FP8X4),
-                            lhsT_scale=weight_s[4 + 4 * a :, ns],
-                            rhs=v_w[a][:, js].bitcast(FP8X4),
-                            rhs_scale=v_s[4 * a :, js],
-                            start=(a == 0),
-                            stop=False,
-                        )
+                js = slice(c0, c0 + BANK)
+                z = psum_z.tile([P, BANK], F32, name="z")
+                for a in range(PASSES):
                     nc.tensor.matmul_mx(
-                        out=acc,
-                        lhsT=wt_w[:, 2 * b * P : 2 * (b + 1) * P].bitcast(FP4X4),
-                        lhsT_scale=weight_s[:, ns],
-                        rhs=h_w[:, js].bitcast(FP8X4),
-                        rhs_scale=h_s[:, js],
-                        start=False,
-                        stop=True,
+                        out=z[:],
+                        lhsT=keep_w[:, a, ns].bitcast(FP8X4),
+                        lhsT_scale=weight_s[4 + 4 * a :, ns],
+                        rhs=v_w[a][:, js].bitcast(FP8X4),
+                        rhs_scale=v_s[4 * a :, js],
+                        start=(a == 0),
+                        stop=False,
                     )
-                local = slice(c0 - j0, c1 - j0)
-                nc.scalar.activation(y[:, local], z[:], ACT.Relu, bias=neg_thr[:, b : b + 1])
-                if weigh:
-                    nc.gpsimd.tensor_tensor(weighted[:, local], y[:, local], wgo_sb[:, c0:c1], ALU.mult)
-            return weighted
+                nc.tensor.matmul_mx(
+                    out=z[:],
+                    lhsT=wt_w[:, 2 * b * P : 2 * (b + 1) * P].bitcast(FP4X4),
+                    lhsT_scale=weight_s[:, ns],
+                    rhs=h_w[:, js].bitcast(FP8X4),
+                    rhs_scale=h_s[:, js],
+                    start=False,
+                    stop=True,
+                )
+                nc.scalar.activation(y[:, c0 - j0 : c0 - j0 + BANK], z[:], ACT.Relu, bias=neg_thr[:, b : b + 1])
+            return y
 
-        def scatter(b, j0, j1, values):
+        def scatter(b, j0, j1, y):
             window = windows[b % WINDOWS]
-            nc.vector.tensor_copy(window[:].indirect(place[:, j0 // 16 : j1 // 16]), values[:])
+            nc.vector.tensor_tensor(
+                window[:].indirect(place[:, j0 // 16 : j1 // 16]), y[:], wgo_sb[:, j0:j1], ALU.mult
+            )
             if j1 == S:
                 nc.sync.dma_start(out=out[b * P : (b + 1) * P, :], in_=window[:])
 
-        residual(0, True)
-        first = shrink(0, 0, QUARTER, False)
-        residual(1, True)
-        gather_words(1, BANK, S)
-        nc.vector.tensor_tensor(
-            windows[0][:].indirect(place[:, 0 : QUARTER // 16]), first[:], wgo_sb[:, 0:QUARTER], ALU.mult
-        )
-        scatter(0, QUARTER, BANK, shrink(0, QUARTER, BANK, True))
-        for b in (1, 2):
-            values = shrink(b, 0, BANK, True)
-            residual(b + 1, False)
-            scatter(b, 0, BANK, values)
-        for b, quarter in ((0, 2), (1, 2), (0, 3), (2, 2), (1, 3), (2, 3)):
-            j0, j1 = quarter * QUARTER, (quarter + 1) * QUARTER
-            scatter(b, j0, j1, shrink(b, j0, j1, True))
-        for b in range(WINDOWS, BLOCKS):
-            scatter(b, 0, S, shrink(b, 0, S, True))
+        residual(0)
+        first = shrink(0, 0, BANK)
+        residual(1)
+        scatter(0, 0, BANK, first)
+        scatter(0, BANK, S, shrink(0, BANK, S))
+        for b in range(1, BLOCKS):
+            scatter(b, 0, S, shrink(b, 0, S))

@@ -35,8 +35,8 @@ def tile_list_sparse_code_step_kernel(
     with ExitStack() as ctx:
         held = ctx.enter_context(tc.tile_pool(name="held", bufs=1))
         ring = ctx.enter_context(tc.tile_pool(name="ring", bufs=4))
-        psum_h = ctx.enter_context(tc.psum_pool(name="psum_h", bufs=3))
-        psum_z = ctx.enter_context(tc.psum_pool(name="psum_z", bufs=4))
+        psum_h = ctx.enter_context(tc.psum_pool(name="psum_h", bufs=4))
+        psum_z = ctx.enter_context(tc.psum_pool(name="psum_z", bufs=3))
         psum_t = ctx.enter_context(tc.psum_pool(name="psum_t", bufs=1))
 
         pick = held.tile([P, S // 16], U16, name="pick")
@@ -44,8 +44,9 @@ def tile_list_sparse_code_step_kernel(
         tab_w = [held.tile([P, T], I32, name=f"tab_w{a}", align_bytes=64) for a in range(PASSES)]
         tab_s = held.tile([P, T], U8, name="tab_s", align_bytes=64)
         w1_raw = [held.tile([P, PACK, M], F32, name=f"w1_raw{a}") for a in range(PASSES)]
-        meas_sb = held.tile([P, PACK, S], F32, name="meas_sb")
-        keep_w = held.tile([P, PASSES, N], I32, name="keep_w", align_bytes=64)
+        meas_sb = [held.tile([P, PACK, BANK], F32, name=f"meas{u}") for u in range(S // BANK)]
+        keep_early = held.tile([P, PASSES, EARLY], I32, name="keep_early", align_bytes=64)
+        keep_late = held.tile([P, PASSES, N - EARLY], I32, name="keep_late", align_bytes=64)
         wt_w = held.tile([P, 2 * N], U8, name="wt_w", align_bytes=64)
         weight_s = held.tile([P, N], U8, name="weight_s", align_bytes=64)
         wgo_sb = held.tile([P, S], F32, name="wgo_sb")
@@ -73,10 +74,10 @@ def tile_list_sparse_code_step_kernel(
             nc.sync.dma_start(out=tab_w[a][:], in_=tab_words[a].rearrange("p t i -> p (t i)").bitcast(I32))
 
         def load_meas(j0, j1):
-            nc.sync.dma_start(out=meas_sb[:, :, j0:j1], in_=meas_view[:, :, j0:j1])
+            nc.sync.dma_start(out=meas_sb[j0 // BANK][:], in_=meas_view[:, :, j0:j1])
 
-        def load_keep(n0, n1):
-            nc.sync.dma_start(out=keep_w[:, :, n0:n1], in_=keep_view[:, :, 4 * n0 : 4 * n1].bitcast(I32))
+        def load_keep(tile, n0, n1):
+            nc.sync.dma_start(out=tile[:], in_=keep_view[:, :, 4 * n0 : 4 * n1].bitcast(I32))
 
         def load_w1(a):
             nc.sync.dma_start(
@@ -99,11 +100,12 @@ def tile_list_sparse_code_step_kernel(
                 out=weight_s[32 * q + 4 : 32 * q + 12, :].bitcast(I32),
                 in_=keep_scales[:, 4 * q : 4 * q + 4, :].bitcast(I32),
             )
-        load_keep(0, EARLY)
+        load_keep(keep_early, 0, EARLY)
         nc.sync.dma_start(out=wt_w[:].bitcast(I32), in_=wt_words[0].bitcast(I32))
-        nc.sync.dma_start(out=wgo_sb[:], in_=wgo)
         nc.sync.dma_start(place[:], offs2)
-        load_keep(EARLY, N)
+        nc.sync.dma_start(out=wgo_sb[:, 0:BANK], in_=wgo[:, 0:BANK])
+        nc.sync.dma_start(out=wgo_sb[:, BANK:S], in_=wgo[:, BANK:S])
+        load_keep(keep_late, EARLY, N)
 
         w1_grouped = [held.tile([P, PACK, P, PACK], BF16, name=f"w1_grouped{a}", align_bytes=64) for a in range(PASSES)]
         w1_w = [held.tile([P, M], U32, name=f"w1_w{a}", align_bytes=64) for a in range(PASSES)]
@@ -114,10 +116,10 @@ def tile_list_sparse_code_step_kernel(
         h_w = held.tile([P, S], U32, name="h_w", align_bytes=64)
         h_s = held.tile([P, S], U8, name="h_s", align_bytes=64)
 
-        def group_w1(a, m0, m1, copy):
+        def group_w1(a, t0, t1, copy):
             copy(
-                out=w1_grouped[a][:, :, m0:m1, :].rearrange("p t m i -> p m t i"),
-                in_=w1_raw[a][:, :, PACK * m0 : PACK * m1].rearrange("p i (m t) -> p m t i", t=PACK),
+                out=w1_grouped[a][:, t0:t1, :, :].rearrange("p t m i -> p m t i"),
+                in_=w1_raw[a][:].rearrange("p i (m t) -> p m t i", t=PACK)[:, :, t0:t1, :],
             )
 
         def quantize_w1(a):
@@ -131,11 +133,11 @@ def tile_list_sparse_code_step_kernel(
             nc.vector.tensor_copy(v_w[a][:, j0:j1], tab_w[a][:].bitcast(U32).indirect(pick[:, j0 // 16 : j1 // 16]))
 
         nc.vector.tensor_copy(v_s[:], tab_s[:].indirect(pick[:]))
-        group_w1(0, 0, P, nc.scalar.copy)
+        group_w1(0, 0, PACK, nc.scalar.copy)
         quantize_w1(0)
         gather_words(0, 0, S)
-        group_w1(1, 0, P // 2, nc.scalar.copy)
-        group_w1(1, P // 2, P, nc.vector.tensor_copy)
+        group_w1(1, 0, PACK // 2, nc.scalar.copy)
+        group_w1(1, PACK // 2, PACK, nc.vector.tensor_copy)
         quantize_w1(1)
         gather_words(1, 0, QUARTER)
         gather_words(1, QUARTER, BANK)
@@ -163,7 +165,7 @@ def tile_list_sparse_code_step_kernel(
                         )
                 nc.vector.tensor_tensor(
                     h_grouped[:, js, :].rearrange("p (c i) t -> p c t i", i=4),
-                    meas_sb[:, :, js].rearrange("p t (c i) -> p c t i", i=4),
+                    meas_sb[j0 // BANK][:, :, j0 % BANK : j0 % BANK + SUB].rearrange("p t (c i) -> p c t i", i=4),
                     pred[:].rearrange("p t (c i) -> p c t i", i=4),
                     ALU.subtract,
                 )
@@ -171,6 +173,11 @@ def tile_list_sparse_code_step_kernel(
             nc.vector.quantize_mx(
                 out=h_w[:, qs].bitcast(FP8X4), scales=h_s[:, qs], in_=h_grouped[:, qs, :].rearrange("p j t -> p (j t)")
             )
+
+        def keep_cols(a, b):
+            if b * P < EARLY:
+                return keep_early[:, a, b * P : (b + 1) * P]
+            return keep_late[:, a, b * P - EARLY : (b + 1) * P - EARLY]
 
         def shrink(b, j0, j1):
             ns = slice(b * P, (b + 1) * P)
@@ -181,7 +188,7 @@ def tile_list_sparse_code_step_kernel(
                 for a in range(PASSES):
                     nc.tensor.matmul_mx(
                         out=z[:],
-                        lhsT=keep_w[:, a, ns].bitcast(FP8X4),
+                        lhsT=keep_cols(a, b).bitcast(FP8X4),
                         lhsT_scale=weight_s[4 + 4 * a :, ns],
                         rhs=v_w[a][:, js].bitcast(FP8X4),
                         rhs_scale=v_s[4 * a :, js],

@@ -24,8 +24,7 @@ BANK = 512
 QUARTER = 256
 SUB = 128
 BLOCKS = N // P
-EARLY = 256
-WINDOWS = 3
+WINDOWS = 4
 
 
 def tile_list_sparse_code_step_kernel(
@@ -34,21 +33,27 @@ def tile_list_sparse_code_step_kernel(
     nc = tc.nc
     with ExitStack() as ctx:
         held = ctx.enter_context(tc.tile_pool(name="held", bufs=1))
-        ring = ctx.enter_context(tc.tile_pool(name="ring", bufs=4))
-        psum_h = ctx.enter_context(tc.psum_pool(name="psum_h", bufs=4))
-        psum_z = ctx.enter_context(tc.psum_pool(name="psum_z", bufs=3))
-        psum_t = ctx.enter_context(tc.psum_pool(name="psum_t", bufs=1))
+        psum = ctx.enter_context(tc.psum_pool(name="psum", bufs=1))
+        banks = [psum.tile([P, BANK], F32, name=f"bank{i}") for i in range(8)]
 
         pick = held.tile([P, S // 16], U16, name="pick")
         place = held.tile([P, S // 16], U16, name="place")
         tab_w = [held.tile([P, T], I32, name=f"tab_w{a}", align_bytes=64) for a in range(PASSES)]
         tab_s = held.tile([P, T], U8, name="tab_s", align_bytes=64)
         w1_raw = [held.tile([P, PACK, M], F32, name=f"w1_raw{a}") for a in range(PASSES)]
-        meas_sb = [held.tile([P, PACK, BANK], F32, name=f"meas{u}") for u in range(S // BANK)]
-        keep_early = held.tile([P, PASSES, EARLY], I32, name="keep_early", align_bytes=64)
-        keep_late = held.tile([P, PASSES, N - EARLY], I32, name="keep_late", align_bytes=64)
+        meas_cuts = [0, QUARTER, BANK, S]
+        meas_sb = [
+            held.tile([P, PACK, j1 - j0], F32, name=f"meas{j0}", align_bytes=64)
+            for j0, j1 in zip(meas_cuts, meas_cuts[1:])
+        ]
+        keep_cuts = [0, 2 * P, 4 * P, N]
+        keep_sb = [
+            held.tile([P, PASSES, n1 - n0], I32, name=f"keep{n0}", align_bytes=64)
+            for n0, n1 in zip(keep_cuts, keep_cuts[1:])
+        ]
         wt_w = held.tile([P, 2 * N], U8, name="wt_w", align_bytes=64)
-        weight_s = held.tile([P, N], U8, name="weight_s", align_bytes=64)
+        keep_s = held.tile([P, N], U8, name="keep_s", align_bytes=64)
+        wt_s = held.tile([P, N], U8, name="wt_s", align_bytes=64)
         wgo_sb = held.tile([P, S], F32, name="wgo_sb")
         thr_rows = held.tile([P, P], F32, name="thr_rows")
         ident = held.tile([P, P], F32, name="ident")
@@ -56,15 +61,16 @@ def tile_list_sparse_code_step_kernel(
         windows = [held.tile([P, T2], F32, name=f"window{i}") for i in range(WINDOWS)]
 
         nc.gpsimd.memset(tab_s[:].bitcast(I32), 0)
-        nc.gpsimd.memset(weight_s[:].bitcast(I32), 0)
         nc.gpsimd.memset(thr_rows[:], 0.0)
-        make_identity(nc, ident[:])
-        for window in windows:
-            nc.gpsimd.memset(window[:], 0.0)
         nc.gpsimd.dma_start(out=thr_rows[0:BLOCKS, :], in_=thr.rearrange("(b p) -> b p", p=P))
+        nc.gpsimd.memset(keep_s[:].bitcast(I32), 0)
+        nc.gpsimd.memset(wt_s[:].bitcast(I32), 0)
+        make_identity(nc, ident[:])
+        for window in windows[0:2]:
+            nc.vector.memset(window[:], 0.0)
         for q in range(4):
             nc.gpsimd.dma_start(
-                out=weight_s[32 * q : 32 * q + 4, :].bitcast(I32), in_=wt_scales[0, 4 * q : 4 * q + 4, :].bitcast(I32)
+                out=wt_s[32 * q : 32 * q + 4, :].bitcast(I32), in_=wt_scales[0, 4 * q : 4 * q + 4, :].bitcast(I32)
             )
 
         keep_view = keep_words.rearrange("a p c i -> p a (c i)")
@@ -73,11 +79,13 @@ def tile_list_sparse_code_step_kernel(
         def load_table(a):
             nc.sync.dma_start(out=tab_w[a][:], in_=tab_words[a].rearrange("p t i -> p (t i)").bitcast(I32))
 
-        def load_meas(j0, j1):
-            nc.sync.dma_start(out=meas_sb[j0 // BANK][:], in_=meas_view[:, :, j0:j1])
+        def load_meas(u):
+            nc.sync.dma_start(out=meas_sb[u][:], in_=meas_view[:, :, meas_cuts[u] : meas_cuts[u + 1]])
 
-        def load_keep(tile, n0, n1):
-            nc.sync.dma_start(out=tile[:], in_=keep_view[:, :, 4 * n0 : 4 * n1].bitcast(I32))
+        def load_keep(u):
+            nc.sync.dma_start(
+                out=keep_sb[u][:], in_=keep_view[:, :, 4 * keep_cuts[u] : 4 * keep_cuts[u + 1]].bitcast(I32)
+            )
 
         def load_w1(a):
             nc.sync.dma_start(
@@ -85,36 +93,48 @@ def tile_list_sparse_code_step_kernel(
             )
 
         nc.sync.dma_start(pick[:], offs)
-        load_w1(0)
         for q in range(4):
             nc.sync.dma_start(
                 out=tab_s[32 * q : 32 * q + 8, :].bitcast(I32), in_=tab_scales[:, 4 * q : 4 * q + 4, :].bitcast(I32)
             )
         load_table(0)
+        load_w1(0)
         load_w1(1)
         load_table(1)
-        load_meas(0, BANK)
-        load_meas(BANK, S)
+        load_meas(0)
         for q in range(4):
             nc.sync.dma_start(
-                out=weight_s[32 * q + 4 : 32 * q + 12, :].bitcast(I32),
+                out=keep_s[32 * q : 32 * q + 8, :].bitcast(I32),
                 in_=keep_scales[:, 4 * q : 4 * q + 4, :].bitcast(I32),
             )
-        load_keep(keep_early, 0, EARLY)
+        load_keep(0)
         nc.sync.dma_start(out=wt_w[:].bitcast(I32), in_=wt_words[0].bitcast(I32))
+        load_meas(1)
         nc.sync.dma_start(place[:], offs2)
-        nc.sync.dma_start(out=wgo_sb[:, 0:BANK], in_=wgo[:, 0:BANK])
-        nc.sync.dma_start(out=wgo_sb[:, BANK:S], in_=wgo[:, BANK:S])
-        load_keep(keep_late, EARLY, N)
+        nc.sync.dma_start(out=wgo_sb[:, 0:QUARTER], in_=wgo[:, 0:QUARTER])
+        load_keep(1)
+        load_meas(2)
+        nc.sync.dma_start(out=wgo_sb[:, QUARTER:S], in_=wgo[:, QUARTER:S])
+        load_keep(2)
 
         w1_grouped = [held.tile([P, PACK, P, PACK], BF16, name=f"w1_grouped{a}", align_bytes=64) for a in range(PASSES)]
         w1_w = [held.tile([P, M], U32, name=f"w1_w{a}", align_bytes=64) for a in range(PASSES)]
         w1_s = [held.tile([P, M], U8, name=f"w1_s{a}", align_bytes=64) for a in range(PASSES)]
-        v_w = [held.tile([P, S], U32, name=f"v_w{a}", align_bytes=64) for a in range(PASSES)]
+        v_w = {
+            (0, 0): held.tile([P, BANK], U32, name="v_w00", align_bytes=64),
+            (0, 1): held.tile([P, BANK], U32, name="v_w01", align_bytes=64),
+            (1, 0): held.tile([P, BANK], U32, name="v_w10", align_bytes=64),
+        }
         v_s = held.tile([P, S], U8, name="v_s", align_bytes=64)
-        h_grouped = held.tile([P, S, PACK], BF16, name="h_grouped", align_bytes=64)
+        h_grouped = [
+            held.tile([P, QUARTER * PACK], BF16, name=f"h_grouped{u}", tag=f"h_grouped{u}", align_bytes=64) for u in range(S // QUARTER)
+        ]
         h_w = held.tile([P, S], U32, name="h_w", align_bytes=64)
         h_s = held.tile([P, S], U8, name="h_s", align_bytes=64)
+        ys = [held.tile([P, S], F32, name=f"y{b}") for b in range(BLOCKS)]
+
+        meas_turneds = [held.tile([P, M], F32, name=f"meas_turned{u}") for u in range(2)]
+        neg_preds = [held.tile([P, M], F32, name=f"neg_pred{u}") for u in range(2)]
 
         def group_w1(a, t0, t1, copy):
             copy(
@@ -129,96 +149,167 @@ def tile_list_sparse_code_step_kernel(
                 in_=w1_grouped[a][:].rearrange("p t m i -> p (t m i)"),
             )
 
+        def v_cols(a, j0, j1):
+            return v_w[a, j0 // BANK][:, j0 % BANK : j0 % BANK + j1 - j0]
+
         def gather_words(a, j0, j1):
-            nc.vector.tensor_copy(v_w[a][:, j0:j1], tab_w[a][:].bitcast(U32).indirect(pick[:, j0 // 16 : j1 // 16]))
+            nc.vector.tensor_copy(v_cols(a, j0, j1), tab_w[a][:].bitcast(U32).indirect(pick[:, j0 // 16 : j1 // 16]))
+
+        def meas_cols(j0, j1):
+            u = max(i for i, cut in enumerate(meas_cuts) if cut <= j0)
+            return meas_sb[u][:, :, j0 - meas_cuts[u] : j1 - meas_cuts[u]]
+
+        def h_cols(j0, j1):
+            tile = h_grouped[j0 // QUARTER]
+            return tile[:, PACK * (j0 % QUARTER) : PACK * (j0 % QUARTER + j1 - j0)]
+
+        def quantize_h(j0, j1):
+            nc.vector.quantize_mx(out=h_w[:, j0:j1].bitcast(FP8X4), scales=h_s[:, j0:j1], in_=h_cols(j0, j1))
 
         nc.vector.tensor_copy(v_s[:], tab_s[:].indirect(pick[:]))
+        gather_words(0, 0, BANK)
+        gather_words(0, BANK, S)
         group_w1(0, 0, PACK, nc.scalar.copy)
         quantize_w1(0)
-        gather_words(0, 0, S)
         group_w1(1, 0, PACK // 2, nc.scalar.copy)
         group_w1(1, PACK // 2, PACK, nc.vector.tensor_copy)
         quantize_w1(1)
         gather_words(1, 0, QUARTER)
         gather_words(1, QUARTER, BANK)
-        gather_words(1, BANK, S)
+        for window in windows[2:]:
+            nc.vector.memset(window[:], 0.0)
 
-        thr_ps = psum_t.tile([P, P], F32, name="thr_ps")
-        nc.tensor.transpose(thr_ps[:], thr_rows[:], ident[:])
-        nc.scalar.mul(neg_thr[:], thr_ps[:, 0:BLOCKS], -1.0)
+        nc.tensor.transpose(banks[7][:, 0:P], thr_rows[:], ident[:])
+        nc.scalar.mul(neg_thr[:], banks[7][:, 0:BLOCKS], -1.0)
 
-        def residual(half):
-            for j0 in range(half * BANK, (half + 1) * BANK, SUB):
-                js = slice(j0, j0 + SUB)
-                pred = psum_h.tile([P, PACK, SUB], F32, name="pred")
+        def residual_on_vector(j0):
+            pred = banks[j0 // SUB]
+            for a in range(PASSES):
                 for t in range(PACK):
                     ms = slice(t * P, (t + 1) * P)
-                    for a in range(PASSES):
-                        nc.tensor.matmul_mx(
-                            out=pred[:, t, :],
-                            lhsT=w1_w[a][:, ms].bitcast(FP8X4),
-                            lhsT_scale=w1_s[a][:, ms],
-                            rhs=v_w[a][:, js].bitcast(FP8X4),
-                            rhs_scale=v_s[4 * a :, js],
-                            start=(a == 0),
-                            stop=(a == PASSES - 1),
-                        )
-                nc.vector.tensor_tensor(
-                    h_grouped[:, js, :].rearrange("p (c i) t -> p c t i", i=4),
-                    meas_sb[j0 // BANK][:, :, j0 % BANK : j0 % BANK + SUB].rearrange("p t (c i) -> p c t i", i=4),
-                    pred[:].rearrange("p t (c i) -> p c t i", i=4),
-                    ALU.subtract,
+                    nc.tensor.matmul_mx(
+                        out=pred[:, ms],
+                        lhsT=w1_w[a][:, ms].bitcast(FP8X4),
+                        lhsT_scale=w1_s[a][:, ms],
+                        rhs=v_cols(a, j0, j0 + SUB).bitcast(FP8X4),
+                        rhs_scale=v_s[4 * a :, j0 : j0 + SUB],
+                        start=(a == 0 and t == 0),
+                        stop=(a == PASSES - 1 and t == PACK - 1),
+                    )
+            nc.vector.tensor_tensor(
+                h_cols(j0, j0 + SUB).rearrange("p (c i t) -> p c t i", i=2, t=PACK),
+                meas_cols(j0, j0 + SUB).rearrange("p t (c i) -> p c t i", i=2),
+                pred[:].rearrange("p (t c i) -> p c t i", t=PACK, i=2),
+                ALU.subtract,
+            )
+
+        def predict_turned(j0, pred):
+            for a in reversed(range(PASSES)):
+                nc.tensor.matmul_mx(
+                    out=pred[:],
+                    lhsT=v_cols(a, j0, j0 + SUB).bitcast(FP8X4),
+                    lhsT_scale=v_s[4 * a :, j0 : j0 + SUB],
+                    rhs=w1_w[a][:].bitcast(FP8X4),
+                    rhs_scale=w1_s[a][:],
+                    start=(a == PASSES - 1),
+                    stop=(a == 0),
                 )
-            qs = slice(half * BANK, (half + 1) * BANK)
-            nc.vector.quantize_mx(
-                out=h_w[:, qs].bitcast(FP8X4), scales=h_s[:, qs], in_=h_grouped[:, qs, :].rearrange("p j t -> p (j t)")
+            nc.scalar.mul(neg_preds[j0 // SUB % 2][:], pred[:], -1.0)
+
+        def residual_on_tensor(j0, meas_bank, turn_bank):
+            turn = j0 // SUB % 2
+            meas_turned, neg_pred = meas_turneds[turn], neg_preds[turn]
+            for t in range(PACK):
+                nc.tensor.transpose(meas_bank[:, t * P : (t + 1) * P], meas_cols(j0, j0 + SUB)[:, t, :], ident[:])
+            nc.scalar.copy(meas_turned[:], meas_bank[:])
+            for term, tile in enumerate((meas_turned, neg_pred)):
+                for t in range(PACK):
+                    ms = slice(t * P, (t + 1) * P)
+                    nc.tensor.matmul(
+                        turn_bank[:, ms],
+                        tile[:, ms],
+                        ident[:],
+                        is_transpose=True,
+                        start=(term == 0 and t == 0),
+                        stop=(term == 1 and t == PACK - 1),
+                    )
+            nc.scalar.copy(
+                h_cols(j0, j0 + SUB).rearrange("p (j t) -> p j t", t=PACK),
+                turn_bank[:].rearrange("p (t j) -> p j t", t=PACK),
             )
 
         def keep_cols(a, b):
-            if b * P < EARLY:
-                return keep_early[:, a, b * P : (b + 1) * P]
-            return keep_late[:, a, b * P - EARLY : (b + 1) * P - EARLY]
+            u = max(i for i, cut in enumerate(keep_cuts) if cut <= b * P)
+            return keep_sb[u][:, a, b * P - keep_cuts[u] : (b + 1) * P - keep_cuts[u]]
 
-        def shrink(b, j0, j1):
+        def shrink(b, j0, j1, bank, keep_first):
             ns = slice(b * P, (b + 1) * P)
-            y = ring.tile([P, j1 - j0], F32, name="y")
-            for c0 in range(j0, j1, BANK):
-                js = slice(c0, c0 + BANK)
-                z = psum_z.tile([P, BANK], F32, name="z")
-                for a in range(PASSES):
-                    nc.tensor.matmul_mx(
-                        out=z[:],
-                        lhsT=keep_cols(a, b).bitcast(FP8X4),
-                        lhsT_scale=weight_s[4 + 4 * a :, ns],
-                        rhs=v_w[a][:, js].bitcast(FP8X4),
-                        rhs_scale=v_s[4 * a :, js],
-                        start=(a == 0),
-                        stop=False,
-                    )
-                nc.tensor.matmul_mx(
-                    out=z[:],
-                    lhsT=wt_w[:, 2 * b * P : 2 * (b + 1) * P].bitcast(FP4X4),
-                    lhsT_scale=weight_s[:, ns],
-                    rhs=h_w[:, js].bitcast(FP8X4),
-                    rhs_scale=h_s[:, js],
-                    start=False,
-                    stop=True,
+            width = j1 - j0
+            step = BANK if width == BANK else SUB
+            keep_passes = [
+                (0, width, keep_cols(a, b).bitcast(FP8X4), keep_s[4 * a :, ns], v_cols(a, j0, j1), v_s[4 * a :, j0:j1])
+                for a in range(PASSES)
+            ]
+            wt_passes = [
+                (
+                    c0,
+                    c0 + step,
+                    wt_w[:, 2 * b * P : 2 * (b + 1) * P].bitcast(FP4X4),
+                    wt_s[:, ns],
+                    h_w[:, j0 + c0 : j0 + c0 + step],
+                    h_s[:, j0 + c0 : j0 + c0 + step],
                 )
-                nc.scalar.activation(y[:, c0 - j0 : c0 - j0 + BANK], z[:], ACT.Relu, bias=neg_thr[:, b : b + 1])
-            return y
+                for c0 in range(0, width, step)
+            ]
+            passes = keep_passes + wt_passes if keep_first else wt_passes + keep_passes
+            for u, (c0, c1, lhs, lhs_scale, rhs, rhs_scale) in enumerate(passes):
+                nc.tensor.matmul_mx(
+                    out=bank[:, c0:c1],
+                    lhsT=lhs,
+                    lhsT_scale=lhs_scale,
+                    rhs=rhs.bitcast(FP8X4),
+                    rhs_scale=rhs_scale,
+                    start=(u == 0),
+                    stop=(u == len(passes) - 1),
+                )
+            nc.scalar.activation(ys[b][:, j0:j1], bank[:, 0:width], ACT.Relu, bias=neg_thr[:, b : b + 1])
 
-        def scatter(b, j0, j1, y):
+        def scatter(b, j0, j1):
             window = windows[b % WINDOWS]
             nc.vector.tensor_tensor(
-                window[:].indirect(place[:, j0 // 16 : j1 // 16]), y[:], wgo_sb[:, j0:j1], ALU.mult
+                window[:].indirect(place[:, j0 // 16 : j1 // 16]), ys[b][:, j0:j1], wgo_sb[:, j0:j1], ALU.mult
             )
             if j1 == S:
                 nc.sync.dma_start(out=out[b * P : (b + 1) * P, :], in_=window[:])
 
-        residual(0)
-        first = shrink(0, 0, BANK)
-        residual(1)
-        scatter(0, 0, BANK, first)
-        scatter(0, BANK, S, shrink(0, BANK, S))
-        for b in range(1, BLOCKS):
-            scatter(b, 0, S, shrink(b, 0, S))
+        for j0 in range(0, QUARTER, SUB):
+            residual_on_vector(j0)
+        for j0 in range(0, QUARTER, SUB):
+            quantize_h(j0, j0 + SUB)
+        v_w[1, 1] = held.tile([P, BANK], U32, name="v_w11", tag="h_grouped0", align_bytes=64)
+        gather_words(1, BANK, S)
+
+        def put(b, j0, j1, bank, keep_first=False):
+            shrink(b, j0, j1, banks[bank], keep_first)
+            scatter(b, j0, j1)
+
+        put(0, 0, QUARTER, 4, keep_first=True)
+        for u in range(2):
+            predict_turned(QUARTER + u * SUB, banks[2 + u])
+        put(1, 0, QUARTER, 6)
+        put(2, 0, QUARTER, 7)
+        for j0 in range(QUARTER, S, QUARTER):
+            for u in range(2):
+                if j0 > QUARTER:
+                    predict_turned(j0 + u * SUB, banks[7])
+                residual_on_tensor(j0 + u * SUB, banks[4 + 2 * u], banks[u])
+            quantize_h(j0, j0 + QUARTER)
+            put(3, j0 - QUARTER, j0, 1)
+            put(0, j0, j0 + QUARTER, 5, keep_first=True)
+            put(1, j0, j0 + QUARTER, 2)
+            put(2, j0, j0 + QUARTER, 3)
+        put(3, S - QUARTER, S, 1)
+        for b, pair in zip(range(WINDOWS, BLOCKS), ((4, 6), (7, 0), (5, 2), (3, 1))):
+            for half in range(2):
+                shrink(b, half * BANK, (half + 1) * BANK, banks[pair[half]], True)
+            scatter(b, 0, S)

@@ -25,6 +25,7 @@ QUARTER = 256
 SUB = 128
 BLOCKS = N // P
 WINDOWS = 4
+ODD = T2 // 2 - 1
 
 
 def tile_list_sparse_code_step_kernel(
@@ -66,12 +67,16 @@ def tile_list_sparse_code_step_kernel(
         nc.gpsimd.memset(keep_s[:].bitcast(I32), 0)
         nc.gpsimd.memset(wt_s[:].bitcast(I32), 0)
         make_identity(nc, ident[:])
+        nc.gpsimd.memset(windows[2][:], 0.0)
         for window in windows[0:2]:
-            nc.vector.memset(window[:], 0.0)
+            nc.vector.memset(window[:, 0:ODD], 0.0)
+            nc.vector.memset(window[:, ODD:T2], 0.0)
         for q in range(4):
             nc.gpsimd.dma_start(
                 out=wt_s[32 * q : 32 * q + 4, :].bitcast(I32), in_=wt_scales[0, 4 * q : 4 * q + 4, :].bitcast(I32)
             )
+        for c0 in range(0, T2, BANK):
+            nc.gpsimd.memset(windows[3][:, c0 : c0 + BANK], 0.0)
 
         keep_view = keep_words.rearrange("a p c i -> p a (c i)")
         meas_view = meas.rearrange("(p t) j -> p t j", t=PACK)
@@ -97,9 +102,9 @@ def tile_list_sparse_code_step_kernel(
             nc.sync.dma_start(
                 out=tab_s[32 * q : 32 * q + 8, :].bitcast(I32), in_=tab_scales[:, 4 * q : 4 * q + 4, :].bitcast(I32)
             )
-        load_table(0)
         load_w1(0)
         load_w1(1)
+        load_table(0)
         load_table(1)
         load_meas(0)
         for q in range(4):
@@ -167,17 +172,15 @@ def tile_list_sparse_code_step_kernel(
             nc.vector.quantize_mx(out=h_w[:, j0:j1].bitcast(FP8X4), scales=h_s[:, j0:j1], in_=h_cols(j0, j1))
 
         nc.vector.tensor_copy(v_s[:], tab_s[:].indirect(pick[:]))
-        gather_words(0, 0, BANK)
-        gather_words(0, BANK, S)
         group_w1(0, 0, PACK, nc.scalar.copy)
         quantize_w1(0)
         group_w1(1, 0, PACK // 2, nc.scalar.copy)
         group_w1(1, PACK // 2, PACK, nc.vector.tensor_copy)
         quantize_w1(1)
+        gather_words(0, 0, BANK)
+        gather_words(0, BANK, S)
         gather_words(1, 0, QUARTER)
         gather_words(1, QUARTER, BANK)
-        for window in windows[2:]:
-            nc.vector.memset(window[:], 0.0)
 
         nc.tensor.transpose(banks[7][:, 0:P], thr_rows[:], ident[:])
         nc.scalar.mul(neg_thr[:], banks[7][:, 0:BLOCKS], -1.0)

@@ -24,7 +24,7 @@ BANK = 512
 QUARTER = 256
 SUB = 128
 BLOCKS = N // P
-WINDOWS = 4
+EARLY_WINDOWS = 2
 ODD = T2 // 2 - 1
 
 
@@ -39,7 +39,7 @@ def tile_list_sparse_code_step_kernel(
 
         pick = held.tile([P, S // 16], U16, name="pick")
         place = held.tile([P, S // 16], U16, name="place")
-        tab_w = [held.tile([P, T], I32, name=f"tab_w{a}", align_bytes=64) for a in range(PASSES)]
+        tab_w = [held.tile([P, T], I32, name=f"tab_w{a}", tag=f"tab_w{a}", align_bytes=64) for a in range(PASSES)]
         tab_s = held.tile([P, T], U8, name="tab_s", align_bytes=64)
         w1_raw = [held.tile([P, PACK, M], F32, name=f"w1_raw{a}") for a in range(PASSES)]
         meas_cuts = [0, QUARTER, BANK, S]
@@ -47,7 +47,7 @@ def tile_list_sparse_code_step_kernel(
             held.tile([P, PACK, j1 - j0], F32, name=f"meas{j0}", align_bytes=64)
             for j0, j1 in zip(meas_cuts, meas_cuts[1:])
         ]
-        keep_cuts = [0, 2 * P, 4 * P, N]
+        keep_cuts = [0, 2 * P, N]
         keep_sb = [
             held.tile([P, PASSES, n1 - n0], I32, name=f"keep{n0}", align_bytes=64)
             for n0, n1 in zip(keep_cuts, keep_cuts[1:])
@@ -59,7 +59,7 @@ def tile_list_sparse_code_step_kernel(
         thr_rows = held.tile([P, P], F32, name="thr_rows")
         ident = held.tile([P, P], F32, name="ident")
         neg_thr = held.tile([P, BLOCKS], F32, name="neg_thr")
-        windows = [held.tile([P, T2], F32, name=f"window{i}") for i in range(WINDOWS)]
+        windows = [held.tile([P, T2], F32, name=f"window{i}") for i in range(EARLY_WINDOWS)]
 
         nc.gpsimd.memset(tab_s[:].bitcast(I32), 0)
         nc.gpsimd.memset(thr_rows[:], 0.0)
@@ -67,16 +67,13 @@ def tile_list_sparse_code_step_kernel(
         nc.gpsimd.memset(keep_s[:].bitcast(I32), 0)
         nc.gpsimd.memset(wt_s[:].bitcast(I32), 0)
         make_identity(nc, ident[:])
-        nc.gpsimd.memset(windows[2][:], 0.0)
-        for window in windows[0:2]:
+        for window in windows:
             nc.vector.memset(window[:, 0:ODD], 0.0)
             nc.vector.memset(window[:, ODD:T2], 0.0)
         for q in range(4):
             nc.gpsimd.dma_start(
                 out=wt_s[32 * q : 32 * q + 4, :].bitcast(I32), in_=wt_scales[0, 4 * q : 4 * q + 4, :].bitcast(I32)
             )
-        for c0 in range(0, T2, BANK):
-            nc.gpsimd.memset(windows[3][:, c0 : c0 + BANK], 0.0)
 
         keep_view = keep_words.rearrange("a p c i -> p a (c i)")
         meas_view = meas.rearrange("(p t) j -> p t j", t=PACK)
@@ -98,15 +95,16 @@ def tile_list_sparse_code_step_kernel(
             )
 
         nc.sync.dma_start(pick[:], offs)
+        load_table(0)
         for q in range(4):
             nc.sync.dma_start(
                 out=tab_s[32 * q : 32 * q + 8, :].bitcast(I32), in_=tab_scales[:, 4 * q : 4 * q + 4, :].bitcast(I32)
             )
         load_w1(0)
         load_w1(1)
-        load_table(0)
         load_table(1)
         load_meas(0)
+        load_meas(1)
         for q in range(4):
             nc.sync.dma_start(
                 out=keep_s[32 * q : 32 * q + 8, :].bitcast(I32),
@@ -114,13 +112,11 @@ def tile_list_sparse_code_step_kernel(
             )
         load_keep(0)
         nc.sync.dma_start(out=wt_w[:].bitcast(I32), in_=wt_words[0].bitcast(I32))
-        load_meas(1)
         nc.sync.dma_start(place[:], offs2)
-        nc.sync.dma_start(out=wgo_sb[:, 0:QUARTER], in_=wgo[:, 0:QUARTER])
-        load_keep(1)
+        nc.sync.dma_start(out=wgo_sb[:, 0:BANK], in_=wgo[:, 0:BANK])
         load_meas(2)
-        nc.sync.dma_start(out=wgo_sb[:, QUARTER:S], in_=wgo[:, QUARTER:S])
-        load_keep(2)
+        nc.sync.dma_start(out=wgo_sb[:, BANK:S], in_=wgo[:, BANK:S])
+        load_keep(1)
 
         w1_grouped = [held.tile([P, PACK, P, PACK], BF16, name=f"w1_grouped{a}", align_bytes=64) for a in range(PASSES)]
         w1_w = [held.tile([P, M], U32, name=f"w1_w{a}", align_bytes=64) for a in range(PASSES)]
@@ -136,10 +132,13 @@ def tile_list_sparse_code_step_kernel(
         ]
         h_w = held.tile([P, S], U32, name="h_w", align_bytes=64)
         h_s = held.tile([P, S], U8, name="h_s", align_bytes=64)
-        ys = [held.tile([P, S], F32, name=f"y{b}") for b in range(BLOCKS)]
-
+        ys = [
+            [held.tile([P, BANK], F32, name=f"y{b}_{u}", tag=f"y{b}_{u}", align_bytes=64) for u in range(2)]
+            for b in range(BLOCKS)
+        ]
         meas_turneds = [held.tile([P, M], F32, name=f"meas_turned{u}") for u in range(2)]
         neg_preds = [held.tile([P, M], F32, name=f"neg_pred{u}") for u in range(2)]
+
 
         def group_w1(a, t0, t1, copy):
             copy(
@@ -171,21 +170,21 @@ def tile_list_sparse_code_step_kernel(
         def quantize_h(j0, j1):
             nc.vector.quantize_mx(out=h_w[:, j0:j1].bitcast(FP8X4), scales=h_s[:, j0:j1], in_=h_cols(j0, j1))
 
+        gather_words(0, 0, BANK)
+        gather_words(0, BANK, S)
         nc.vector.tensor_copy(v_s[:], tab_s[:].indirect(pick[:]))
         group_w1(0, 0, PACK, nc.scalar.copy)
         quantize_w1(0)
         group_w1(1, 0, PACK // 2, nc.scalar.copy)
         group_w1(1, PACK // 2, PACK, nc.vector.tensor_copy)
         quantize_w1(1)
-        gather_words(0, 0, BANK)
-        gather_words(0, BANK, S)
         gather_words(1, 0, QUARTER)
         gather_words(1, QUARTER, BANK)
 
         nc.tensor.transpose(banks[7][:, 0:P], thr_rows[:], ident[:])
         nc.scalar.mul(neg_thr[:], banks[7][:, 0:BLOCKS], -1.0)
 
-        def residual_on_vector(j0):
+        def residual(j0):
             pred = banks[j0 // SUB]
             for a in range(PASSES):
                 for t in range(PACK):
@@ -245,12 +244,11 @@ def tile_list_sparse_code_step_kernel(
             u = max(i for i, cut in enumerate(keep_cuts) if cut <= b * P)
             return keep_sb[u][:, a, b * P - keep_cuts[u] : (b + 1) * P - keep_cuts[u]]
 
-        def shrink(b, j0, j1, bank, keep_first):
+        def put(b, half, bank, keep_first=False, step=BANK):
             ns = slice(b * P, (b + 1) * P)
-            width = j1 - j0
-            step = BANK if width == BANK else SUB
+            j0, j1 = half * BANK, (half + 1) * BANK
             keep_passes = [
-                (0, width, keep_cols(a, b).bitcast(FP8X4), keep_s[4 * a :, ns], v_cols(a, j0, j1), v_s[4 * a :, j0:j1])
+                (0, BANK, keep_cols(a, b).bitcast(FP8X4), keep_s[4 * a :, ns], v_cols(a, j0, j1), v_s[4 * a :, j0:j1])
                 for a in range(PASSES)
             ]
             wt_passes = [
@@ -262,12 +260,12 @@ def tile_list_sparse_code_step_kernel(
                     h_w[:, j0 + c0 : j0 + c0 + step],
                     h_s[:, j0 + c0 : j0 + c0 + step],
                 )
-                for c0 in range(0, width, step)
+                for c0 in range(0, BANK, step)
             ]
             passes = keep_passes + wt_passes if keep_first else wt_passes + keep_passes
             for u, (c0, c1, lhs, lhs_scale, rhs, rhs_scale) in enumerate(passes):
                 nc.tensor.matmul_mx(
-                    out=bank[:, c0:c1],
+                    out=banks[bank][:, c0:c1],
                     lhsT=lhs,
                     lhsT_scale=lhs_scale,
                     rhs=rhs.bitcast(FP8X4),
@@ -275,44 +273,39 @@ def tile_list_sparse_code_step_kernel(
                     start=(u == 0),
                     stop=(u == len(passes) - 1),
                 )
-            nc.scalar.activation(ys[b][:, j0:j1], bank[:, 0:width], ACT.Relu, bias=neg_thr[:, b : b + 1])
-
-        def scatter(b, j0, j1):
-            window = windows[b % WINDOWS]
+            y = ys[b][half]
+            nc.scalar.activation(y[:], banks[bank][:], ACT.Relu, bias=neg_thr[:, b : b + 1])
             nc.vector.tensor_tensor(
-                window[:].indirect(place[:, j0 // 16 : j1 // 16]), ys[b][:, j0:j1], wgo_sb[:, j0:j1], ALU.mult
+                windows[b][:].indirect(place[:, j0 // 16 : j1 // 16]), y[:], wgo_sb[:, j0:j1], ALU.mult
             )
-            if j1 == S:
-                nc.sync.dma_start(out=out[b * P : (b + 1) * P, :], in_=window[:])
+            if half == 1:
+                nc.sync.dma_start(out=out[b * P : (b + 1) * P, :], in_=windows[b][:])
 
-        for j0 in range(0, QUARTER, SUB):
-            residual_on_vector(j0)
-        for j0 in range(0, QUARTER, SUB):
-            quantize_h(j0, j0 + SUB)
-        v_w[1, 1] = held.tile([P, BANK], U32, name="v_w11", tag="h_grouped0", align_bytes=64)
-        gather_words(1, BANK, S)
+        def zero_window(tag):
+            window = held.tile([P, T2], F32, name=f"window{len(windows)}", tag=tag, align_bytes=64)
+            nc.gpsimd.memset(window[:], 0.0)
+            windows.append(window)
 
-        def put(b, j0, j1, bank, keep_first=False):
-            shrink(b, j0, j1, banks[bank], keep_first)
-            scatter(b, j0, j1)
-
-        put(0, 0, QUARTER, 4, keep_first=True)
-        for u in range(2):
-            predict_turned(QUARTER + u * SUB, banks[2 + u])
-        put(1, 0, QUARTER, 6)
-        put(2, 0, QUARTER, 7)
-        for j0 in range(QUARTER, S, QUARTER):
-            for u in range(2):
-                if j0 > QUARTER:
-                    predict_turned(j0 + u * SUB, banks[7])
-                residual_on_tensor(j0 + u * SUB, banks[4 + 2 * u], banks[u])
+        for j0 in range(0, BANK, SUB):
+            residual(j0)
+        for j0 in range(0, BANK, QUARTER):
             quantize_h(j0, j0 + QUARTER)
-            put(3, j0 - QUARTER, j0, 1)
-            put(0, j0, j0 + QUARTER, 5, keep_first=True)
-            put(1, j0, j0 + QUARTER, 2)
-            put(2, j0, j0 + QUARTER, 3)
-        put(3, S - QUARTER, S, 1)
-        for b, pair in zip(range(WINDOWS, BLOCKS), ((4, 6), (7, 0), (5, 2), (3, 1))):
-            for half in range(2):
-                shrink(b, half * BANK, (half + 1) * BANK, banks[pair[half]], True)
-            scatter(b, 0, S)
+        v_w[1, 1] = held.tile([P, BANK], U32, name="v_w11", tag="h_grouped1", align_bytes=64)
+        gather_words(1, BANK, S)
+        zero_window("tab_w1")
+
+        put(0, 0, 4, keep_first=True, step=SUB)
+        for b in range(1, 4):
+            zero_window(f"y{b - 1}_0")
+            put(b, 0, 4 + b)
+        for c0 in range(BANK, S, QUARTER):
+            for u in range(2):
+                predict_turned(c0 + u * SUB, banks[4])
+                residual_on_tensor(c0 + u * SUB, banks[5 + u], banks[u])
+            quantize_h(c0, c0 + QUARTER)
+        for b, bank in zip(range(4, BLOCKS), (2, 3, 7, 1)):
+            if len(windows) < BLOCKS:
+                zero_window(f"y{b - 1}_0")
+            put(b, 0, bank)
+        for b, bank in enumerate((4, 5, 6, 0, 2, 3, 7, 1)):
+            put(b, 1, bank, keep_first=True)

@@ -24,7 +24,7 @@ BANK = 512
 QUARTER = 256
 SUB = 128
 BLOCKS = N // P
-EARLY_WINDOWS = 2
+EARLY_WINDOWS = 1
 ODD = T2 // 2 - 1
 
 
@@ -95,11 +95,12 @@ def tile_list_sparse_code_step_kernel(
             )
 
         nc.sync.dma_start(pick[:], offs)
-        load_table(0)
+        nc.sync.dma_start(place[:], offs2)
         for q in range(4):
             nc.sync.dma_start(
                 out=tab_s[32 * q : 32 * q + 8, :].bitcast(I32), in_=tab_scales[:, 4 * q : 4 * q + 4, :].bitcast(I32)
             )
+        load_table(0)
         load_w1(0)
         load_w1(1)
         load_table(1)
@@ -112,13 +113,11 @@ def tile_list_sparse_code_step_kernel(
             )
         load_keep(0)
         nc.sync.dma_start(out=wt_w[:].bitcast(I32), in_=wt_words[0].bitcast(I32))
-        nc.sync.dma_start(place[:], offs2)
         nc.sync.dma_start(out=wgo_sb[:, 0:BANK], in_=wgo[:, 0:BANK])
         load_meas(2)
         nc.sync.dma_start(out=wgo_sb[:, BANK:S], in_=wgo[:, BANK:S])
         load_keep(1)
 
-        w1_grouped = [held.tile([P, PACK, P, PACK], BF16, name=f"w1_grouped{a}", align_bytes=64) for a in range(PASSES)]
         w1_w = [held.tile([P, M], U32, name=f"w1_w{a}", align_bytes=64) for a in range(PASSES)]
         w1_s = [held.tile([P, M], U8, name=f"w1_s{a}", align_bytes=64) for a in range(PASSES)]
         v_w = {
@@ -140,17 +139,18 @@ def tile_list_sparse_code_step_kernel(
         neg_preds = [held.tile([P, M], F32, name=f"neg_pred{u}") for u in range(2)]
 
 
-        def group_w1(a, t0, t1, copy):
+        def group_w1(a, grouped, t0, t1, copy):
             copy(
-                out=w1_grouped[a][:, t0:t1, :, :].rearrange("p t m i -> p m t i"),
+                out=grouped[:, t0:t1, :, :].rearrange("p t m i -> p m t i"),
                 in_=w1_raw[a][:].rearrange("p i (m t) -> p m t i", t=PACK)[:, :, t0:t1, :],
             )
 
         def quantize_w1(a):
+            grouped = held.tile([P, PACK, P, PACK], BF16, name="w1_grouped", align_bytes=64)
+            group_w1(a, grouped, 0, PACK // 2, nc.scalar.copy)
+            group_w1(a, grouped, PACK // 2, PACK, nc.vector.tensor_copy)
             nc.vector.quantize_mx(
-                out=w1_w[a][:].bitcast(FP8X4),
-                scales=w1_s[a][:],
-                in_=w1_grouped[a][:].rearrange("p t m i -> p (t m i)"),
+                out=w1_w[a][:].bitcast(FP8X4), scales=w1_s[a][:], in_=grouped[:].rearrange("p t m i -> p (t m i)")
             )
 
         def v_cols(a, j0, j1):
@@ -170,19 +170,13 @@ def tile_list_sparse_code_step_kernel(
         def quantize_h(j0, j1):
             nc.vector.quantize_mx(out=h_w[:, j0:j1].bitcast(FP8X4), scales=h_s[:, j0:j1], in_=h_cols(j0, j1))
 
+        nc.vector.tensor_copy(v_s[:], tab_s[:].indirect(pick[:]))
         gather_words(0, 0, BANK)
         gather_words(0, BANK, S)
-        nc.vector.tensor_copy(v_s[:], tab_s[:].indirect(pick[:]))
-        group_w1(0, 0, PACK, nc.scalar.copy)
-        quantize_w1(0)
-        group_w1(1, 0, PACK // 2, nc.scalar.copy)
-        group_w1(1, PACK // 2, PACK, nc.vector.tensor_copy)
-        quantize_w1(1)
+        for a in range(PASSES):
+            quantize_w1(a)
         gather_words(1, 0, QUARTER)
         gather_words(1, QUARTER, BANK)
-
-        nc.tensor.transpose(banks[7][:, 0:P], thr_rows[:], ident[:])
-        nc.scalar.mul(neg_thr[:], banks[7][:, 0:BLOCKS], -1.0)
 
         def residual(j0):
             pred = banks[j0 // SUB]
@@ -290,6 +284,8 @@ def tile_list_sparse_code_step_kernel(
             residual(j0)
         for j0 in range(0, BANK, QUARTER):
             quantize_h(j0, j0 + QUARTER)
+        nc.tensor.transpose(banks[0][:, 0:P], thr_rows[:], ident[:])
+        nc.scalar.mul(neg_thr[:], banks[0][:, 0:BLOCKS], -1.0)
         v_w[1, 1] = held.tile([P, BANK], U32, name="v_w11", tag="h_grouped1", align_bytes=64)
         gather_words(1, BANK, S)
         zero_window("tab_w1")

@@ -25,7 +25,6 @@ QUARTER = 256
 SUB = 128
 BLOCKS = N // P
 EARLY_WINDOWS = 1
-ODD = T2 // 2 - 1
 
 
 def tile_list_sparse_code_step_kernel(
@@ -67,13 +66,12 @@ def tile_list_sparse_code_step_kernel(
         nc.gpsimd.memset(keep_s[:].bitcast(I32), 0)
         nc.gpsimd.memset(wt_s[:].bitcast(I32), 0)
         make_identity(nc, ident[:])
-        for window in windows:
-            nc.vector.memset(window[:, 0:ODD], 0.0)
-            nc.vector.memset(window[:, ODD:T2], 0.0)
         for q in range(4):
             nc.gpsimd.dma_start(
                 out=wt_s[32 * q : 32 * q + 4, :].bitcast(I32), in_=wt_scales[0, 4 * q : 4 * q + 4, :].bitcast(I32)
             )
+
+        nc.gpsimd.memset(windows[0][:], 0.0)
 
         keep_view = keep_words.rearrange("a p c i -> p a (c i)")
         meas_view = meas.rearrange("(p t) j -> p t j", t=PACK)
@@ -94,6 +92,7 @@ def tile_list_sparse_code_step_kernel(
                 out=w1_raw[a][:], in_=w1[512 * a : 512 * (a + 1), :].rearrange("(p i) c -> p i c", i=PACK)
             )
 
+        load_w1(0)
         nc.sync.dma_start(pick[:], offs)
         nc.sync.dma_start(place[:], offs2)
         for q in range(4):
@@ -101,7 +100,6 @@ def tile_list_sparse_code_step_kernel(
                 out=tab_s[32 * q : 32 * q + 8, :].bitcast(I32), in_=tab_scales[:, 4 * q : 4 * q + 4, :].bitcast(I32)
             )
         load_table(0)
-        load_w1(0)
         load_w1(1)
         load_table(1)
         load_meas(0)
@@ -126,8 +124,10 @@ def tile_list_sparse_code_step_kernel(
             (1, 0): held.tile([P, BANK], U32, name="v_w10", align_bytes=64),
         }
         v_s = held.tile([P, S], U8, name="v_s", align_bytes=64)
+        h_cuts = [0, QUARTER, BANK, S]
         h_grouped = [
-            held.tile([P, QUARTER * PACK], BF16, name=f"h_grouped{u}", tag=f"h_grouped{u}", align_bytes=64) for u in range(S // QUARTER)
+            held.tile([P, (j1 - j0) * PACK], BF16, name=f"h_grouped{u}", tag=f"h_grouped{u}", align_bytes=64)
+            for u, (j0, j1) in enumerate(zip(h_cuts, h_cuts[1:]))
         ]
         h_w = held.tile([P, S], U32, name="h_w", align_bytes=64)
         h_s = held.tile([P, S], U8, name="h_s", align_bytes=64)
@@ -146,9 +146,9 @@ def tile_list_sparse_code_step_kernel(
             )
 
         def quantize_w1(a):
-            grouped = held.tile([P, PACK, P, PACK], BF16, name="w1_grouped", align_bytes=64)
+            grouped = held.tile([P, PACK, P, PACK], BF16, name=f"w1_grouped{a}", align_bytes=64)
             group_w1(a, grouped, 0, PACK // 2, nc.scalar.copy)
-            group_w1(a, grouped, PACK // 2, PACK, nc.vector.tensor_copy)
+            group_w1(a, grouped, PACK // 2, PACK, nc.vector.tensor_copy if a else nc.scalar.copy)
             nc.vector.quantize_mx(
                 out=w1_w[a][:].bitcast(FP8X4), scales=w1_s[a][:], in_=grouped[:].rearrange("p t m i -> p (t m i)")
             )
@@ -164,8 +164,8 @@ def tile_list_sparse_code_step_kernel(
             return meas_sb[u][:, :, j0 - meas_cuts[u] : j1 - meas_cuts[u]]
 
         def h_cols(j0, j1):
-            tile = h_grouped[j0 // QUARTER]
-            return tile[:, PACK * (j0 % QUARTER) : PACK * (j0 % QUARTER + j1 - j0)]
+            u = max(i for i, cut in enumerate(h_cuts) if cut <= j0)
+            return h_grouped[u][:, PACK * (j0 - h_cuts[u]) : PACK * (j1 - h_cuts[u])]
 
         def quantize_h(j0, j1):
             nc.vector.quantize_mx(out=h_w[:, j0:j1].bitcast(FP8X4), scales=h_s[:, j0:j1], in_=h_cols(j0, j1))
@@ -294,14 +294,17 @@ def tile_list_sparse_code_step_kernel(
         for b in range(1, 4):
             zero_window(f"y{b - 1}_0")
             put(b, 0, 4 + b)
-        for c0 in range(BANK, S, QUARTER):
-            for u in range(2):
-                predict_turned(c0 + u * SUB, banks[4])
-                residual_on_tensor(c0 + u * SUB, banks[5 + u], banks[u])
-            quantize_h(c0, c0 + QUARTER)
-        for b, bank in zip(range(4, BLOCKS), (2, 3, 7, 1)):
-            if len(windows) < BLOCKS:
-                zero_window(f"y{b - 1}_0")
+        def turn(u):
+            predict_turned(BANK + u * SUB, banks[4])
+            residual_on_tensor(BANK + u * SUB, banks[5 + u % 2], banks[u % 2])
+
+        for u in range(3):
+            turn(u)
+        for b, bank in zip(range(4, BLOCKS - 1), (2, 3, 1)):
+            zero_window(f"y{b - 1}_0")
             put(b, 0, bank)
+        turn(3)
+        quantize_h(BANK, S)
+        put(BLOCKS - 1, 0, 1)
         for b, bank in enumerate((4, 5, 6, 0, 2, 3, 7, 1)):
             put(b, 1, bank, keep_first=True)

@@ -24,7 +24,8 @@ BANK = 512
 QUARTER = 256
 SUB = 128
 BLOCKS = N // P
-EARLY_WINDOWS = 1
+EARLY_WINDOWS = 3
+ODD = T2 // 2 - 1
 
 
 def tile_list_sparse_code_step_kernel(
@@ -71,7 +72,12 @@ def tile_list_sparse_code_step_kernel(
                 out=wt_s[32 * q : 32 * q + 4, :].bitcast(I32), in_=wt_scales[0, 4 * q : 4 * q + 4, :].bitcast(I32)
             )
 
-        nc.gpsimd.memset(windows[0][:], 0.0)
+        nc.vector.memset(windows[0][:, 0:ODD], 0.0)
+        nc.vector.memset(windows[0][:, ODD:T2], 0.0)
+        nc.vector.memset(windows[1][:, 0 : BANK - 1], 0.0)
+        nc.vector.memset(windows[1][:, BANK - 1 : T2 // 2], 0.0)
+        nc.gpsimd.memset(windows[1][:, T2 // 2 : T2], 0.0)
+        nc.gpsimd.memset(windows[2][:], 0.0)
 
         keep_view = keep_words.rearrange("a p c i -> p a (c i)")
         meas_view = meas.rearrange("(p t) j -> p t j", t=PACK)
@@ -87,12 +93,13 @@ def tile_list_sparse_code_step_kernel(
                 out=keep_sb[u][:], in_=keep_view[:, :, 4 * keep_cuts[u] : 4 * keep_cuts[u + 1]].bitcast(I32)
             )
 
-        def load_w1(a):
+        def load_w1(a, i0, i1):
             nc.sync.dma_start(
-                out=w1_raw[a][:], in_=w1[512 * a : 512 * (a + 1), :].rearrange("(p i) c -> p i c", i=PACK)
+                out=w1_raw[a][:, i0:i1, :],
+                in_=w1[512 * a : 512 * (a + 1), :].rearrange("(p i) c -> p i c", i=PACK)[:, i0:i1, :],
             )
 
-        load_w1(0)
+        load_w1(0, 0, PACK // 2)
         nc.sync.dma_start(pick[:], offs)
         nc.sync.dma_start(place[:], offs2)
         for q in range(4):
@@ -100,10 +107,10 @@ def tile_list_sparse_code_step_kernel(
                 out=tab_s[32 * q : 32 * q + 8, :].bitcast(I32), in_=tab_scales[:, 4 * q : 4 * q + 4, :].bitcast(I32)
             )
         load_table(0)
-        load_w1(1)
+        load_w1(0, PACK // 2, PACK)
+        load_w1(1, 0, PACK)
         load_table(1)
         load_meas(0)
-        load_meas(1)
         for q in range(4):
             nc.sync.dma_start(
                 out=keep_s[32 * q : 32 * q + 8, :].bitcast(I32),
@@ -111,10 +118,11 @@ def tile_list_sparse_code_step_kernel(
             )
         load_keep(0)
         nc.sync.dma_start(out=wt_w[:].bitcast(I32), in_=wt_words[0].bitcast(I32))
-        nc.sync.dma_start(out=wgo_sb[:, 0:BANK], in_=wgo[:, 0:BANK])
-        load_meas(2)
-        nc.sync.dma_start(out=wgo_sb[:, BANK:S], in_=wgo[:, BANK:S])
+        nc.sync.dma_start(out=wgo_sb[:, 0:QUARTER], in_=wgo[:, 0:QUARTER])
         load_keep(1)
+        load_meas(1)
+        load_meas(2)
+        nc.sync.dma_start(out=wgo_sb[:, QUARTER:S], in_=wgo[:, QUARTER:S])
 
         w1_w = [held.tile([P, M], U32, name=f"w1_w{a}", align_bytes=64) for a in range(PASSES)]
         w1_s = [held.tile([P, M], U8, name=f"w1_s{a}", align_bytes=64) for a in range(PASSES)]
@@ -124,19 +132,15 @@ def tile_list_sparse_code_step_kernel(
             (1, 0): held.tile([P, BANK], U32, name="v_w10", align_bytes=64),
         }
         v_s = held.tile([P, S], U8, name="v_s", align_bytes=64)
-        h_cuts = [0, QUARTER, BANK, S]
+        h_cuts = [0, SUB] + list(range(QUARTER, S + 1, QUARTER))
         h_grouped = [
             held.tile([P, (j1 - j0) * PACK], BF16, name=f"h_grouped{u}", tag=f"h_grouped{u}", align_bytes=64)
             for u, (j0, j1) in enumerate(zip(h_cuts, h_cuts[1:]))
         ]
         h_w = held.tile([P, S], U32, name="h_w", align_bytes=64)
         h_s = held.tile([P, S], U8, name="h_s", align_bytes=64)
-        ys = [
-            [held.tile([P, BANK], F32, name=f"y{b}_{u}", tag=f"y{b}_{u}", align_bytes=64) for u in range(2)]
-            for b in range(BLOCKS)
-        ]
-        meas_turneds = [held.tile([P, M], F32, name=f"meas_turned{u}") for u in range(2)]
-        neg_preds = [held.tile([P, M], F32, name=f"neg_pred{u}") for u in range(2)]
+        meas_turneds = {j0: held.tile([P, M], F32, name=f"meas_turned{j0}") for j0 in range(QUARTER, S, SUB)}
+        neg_preds = {j0: held.tile([P, M], F32, name=f"neg_pred{j0}") for j0 in range(QUARTER, S, SUB)}
 
 
         def group_w1(a, grouped, t0, t1, copy):
@@ -148,7 +152,7 @@ def tile_list_sparse_code_step_kernel(
         def quantize_w1(a):
             grouped = held.tile([P, PACK, P, PACK], BF16, name=f"w1_grouped{a}", align_bytes=64)
             group_w1(a, grouped, 0, PACK // 2, nc.scalar.copy)
-            group_w1(a, grouped, PACK // 2, PACK, nc.vector.tensor_copy if a else nc.scalar.copy)
+            group_w1(a, grouped, PACK // 2, PACK, nc.vector.tensor_copy)
             nc.vector.quantize_mx(
                 out=w1_w[a][:].bitcast(FP8X4), scales=w1_s[a][:], in_=grouped[:].rearrange("p t m i -> p (t m i)")
             )
@@ -199,30 +203,30 @@ def tile_list_sparse_code_step_kernel(
                 ALU.subtract,
             )
 
-        def predict_turned(j0, pred):
-            for a in reversed(range(PASSES)):
+        def predict_turned(j0, bank):
+            for a in range(PASSES):
                 nc.tensor.matmul_mx(
-                    out=pred[:],
+                    out=banks[bank][:],
                     lhsT=v_cols(a, j0, j0 + SUB).bitcast(FP8X4),
                     lhsT_scale=v_s[4 * a :, j0 : j0 + SUB],
                     rhs=w1_w[a][:].bitcast(FP8X4),
                     rhs_scale=w1_s[a][:],
-                    start=(a == PASSES - 1),
-                    stop=(a == 0),
+                    start=(a == 0),
+                    stop=(a == PASSES - 1),
                 )
-            nc.scalar.mul(neg_preds[j0 // SUB % 2][:], pred[:], -1.0)
+            nc.scalar.mul(neg_preds[j0][:], banks[bank][:], -1.0)
 
-        def residual_on_tensor(j0, meas_bank, turn_bank):
-            turn = j0 // SUB % 2
-            meas_turned, neg_pred = meas_turneds[turn], neg_preds[turn]
+        def turn_meas(j0, bank):
             for t in range(PACK):
-                nc.tensor.transpose(meas_bank[:, t * P : (t + 1) * P], meas_cols(j0, j0 + SUB)[:, t, :], ident[:])
-            nc.scalar.copy(meas_turned[:], meas_bank[:])
-            for term, tile in enumerate((meas_turned, neg_pred)):
+                nc.tensor.transpose(banks[bank][:, t * P : (t + 1) * P], meas_cols(j0, j0 + SUB)[:, t, :], ident[:])
+            nc.scalar.copy(meas_turneds[j0][:], banks[bank][:])
+
+        def sum_turned(j0, bank):
+            for term, tile in enumerate((meas_turneds[j0], neg_preds[j0])):
                 for t in range(PACK):
                     ms = slice(t * P, (t + 1) * P)
                     nc.tensor.matmul(
-                        turn_bank[:, ms],
+                        banks[bank][:, ms],
                         tile[:, ms],
                         ident[:],
                         is_transpose=True,
@@ -231,18 +235,19 @@ def tile_list_sparse_code_step_kernel(
                     )
             nc.scalar.copy(
                 h_cols(j0, j0 + SUB).rearrange("p (j t) -> p j t", t=PACK),
-                turn_bank[:].rearrange("p (t j) -> p j t", t=PACK),
+                banks[bank][:].rearrange("p (t j) -> p j t", t=PACK),
             )
 
         def keep_cols(a, b):
             u = max(i for i, cut in enumerate(keep_cuts) if cut <= b * P)
             return keep_sb[u][:, a, b * P - keep_cuts[u] : (b + 1) * P - keep_cuts[u]]
 
-        def put(b, half, bank, keep_first=False, step=BANK):
+        def put(b, j0, j1, bank, keep_first=False):
             ns = slice(b * P, (b + 1) * P)
-            j0, j1 = half * BANK, (half + 1) * BANK
+            width = j1 - j0
+            step = BANK if width == BANK else SUB
             keep_passes = [
-                (0, BANK, keep_cols(a, b).bitcast(FP8X4), keep_s[4 * a :, ns], v_cols(a, j0, j1), v_s[4 * a :, j0:j1])
+                (0, width, keep_cols(a, b).bitcast(FP8X4), keep_s[4 * a :, ns], v_cols(a, j0, j1), v_s[4 * a :, j0:j1])
                 for a in range(PASSES)
             ]
             wt_passes = [
@@ -254,7 +259,7 @@ def tile_list_sparse_code_step_kernel(
                     h_w[:, j0 + c0 : j0 + c0 + step],
                     h_s[:, j0 + c0 : j0 + c0 + step],
                 )
-                for c0 in range(0, BANK, step)
+                for c0 in range(0, width, step)
             ]
             passes = keep_passes + wt_passes if keep_first else wt_passes + keep_passes
             for u, (c0, c1, lhs, lhs_scale, rhs, rhs_scale) in enumerate(passes):
@@ -267,12 +272,12 @@ def tile_list_sparse_code_step_kernel(
                     start=(u == 0),
                     stop=(u == len(passes) - 1),
                 )
-            y = ys[b][half]
-            nc.scalar.activation(y[:], banks[bank][:], ACT.Relu, bias=neg_thr[:, b : b + 1])
+            y = held.tile([P, width], F32, name=f"y{b}_{j0}", tag=f"y{b}_{j0}", align_bytes=64)
+            nc.scalar.activation(y[:], banks[bank][:, 0:width], ACT.Relu, bias=neg_thr[:, b : b + 1])
             nc.vector.tensor_tensor(
                 windows[b][:].indirect(place[:, j0 // 16 : j1 // 16]), y[:], wgo_sb[:, j0:j1], ALU.mult
             )
-            if half == 1:
+            if j1 == S:
                 nc.sync.dma_start(out=out[b * P : (b + 1) * P, :], in_=windows[b][:])
 
         def zero_window(tag):
@@ -280,31 +285,64 @@ def tile_list_sparse_code_step_kernel(
             nc.gpsimd.memset(window[:], 0.0)
             windows.append(window)
 
-        for j0 in range(0, BANK, SUB):
+        for j0 in range(0, QUARTER, SUB):
             residual(j0)
-        for j0 in range(0, BANK, QUARTER):
-            quantize_h(j0, j0 + QUARTER)
+        for j0 in range(0, QUARTER, SUB):
+            quantize_h(j0, j0 + SUB)
         nc.tensor.transpose(banks[0][:, 0:P], thr_rows[:], ident[:])
         nc.scalar.mul(neg_thr[:], banks[0][:, 0:BLOCKS], -1.0)
-        v_w[1, 1] = held.tile([P, BANK], U32, name="v_w11", tag="h_grouped1", align_bytes=64)
+        v_w[1, 1] = held.tile([P, BANK], U32, name="v_w11", tag="h_grouped0", align_bytes=64)
         gather_words(1, BANK, S)
+        zero_window("h_grouped1")
         zero_window("tab_w1")
 
-        put(0, 0, 4, keep_first=True, step=SUB)
-        for b in range(1, 4):
-            zero_window(f"y{b - 1}_0")
-            put(b, 0, 4 + b)
-        def turn(u):
-            predict_turned(BANK + u * SUB, banks[4])
-            residual_on_tensor(BANK + u * SUB, banks[5 + u % 2], banks[u % 2])
+        q1, q2, q3, q4 = (0, 256), (256, 512), (512, 768), (768, 1024)
+        put(0, *q1, 2, keep_first=True)
+        zero_window("y0_0")
+        put(1, *q1, 3)
+        zero_window("y1_0")
+        predict_turned(256, 4)
+        put(2, *q1, 5)
+        zero_window("y2_0")
+        predict_turned(384, 2)
+        turn_meas(256, 6)
+        put(3, *q1, 7)
+        turn_meas(384, 0)
+        put(4, *q1, 1)
+        sum_turned(256, 3)
+        put(5, *q1, 4)
+        predict_turned(512, 2)
+        put(6, *q1, 5)
+        sum_turned(384, 5)
+        quantize_h(*q2)
+        put(7, *q1, 5)
+        predict_turned(640, 6)
 
-        for u in range(3):
-            turn(u)
-        for b, bank in zip(range(4, BLOCKS - 1), (2, 3, 1)):
-            zero_window(f"y{b - 1}_0")
-            put(b, 0, bank)
-        turn(3)
-        quantize_h(BANK, S)
-        put(BLOCKS - 1, 0, 1)
-        for b, bank in enumerate((4, 5, 6, 0, 2, 3, 7, 1)):
-            put(b, 1, bank, keep_first=True)
+        put(0, *q2, 7, keep_first=True)
+        turn_meas(512, 0)
+        put(1, *q2, 1)
+        turn_meas(640, 3)
+        put(2, *q2, 4)
+        sum_turned(512, 2)
+        put(3, *q2, 6)
+        predict_turned(768, 5)
+        put(4, *q2, 7)
+        predict_turned(896, 0)
+        put(5, *q2, 1)
+        turn_meas(768, 3)
+        put(6, *q2, 4)
+        sum_turned(640, 4)
+        quantize_h(*q3)
+        put(7, *q2, 4)
+        turn_meas(896, 2)
+
+        put(0, *q3, 6, keep_first=True)
+        put(1, *q3, 5)
+        sum_turned(768, 7)
+        put(2, *q3, 0)
+        sum_turned(896, 0)
+        quantize_h(*q4)
+        put(3, *q3, 0)
+        for b, banks_b in enumerate(((1, 3), (4, 2), (6, 5), (7, 0))):
+            put(b, *q4, banks_b[0], keep_first=True)
+            put(4 + b, BANK, S, banks_b[1])

@@ -47,7 +47,7 @@ def tile_list_sparse_code_step_kernel(
             held.tile([P, PACK, j1 - j0], F32, name=f"meas{j0}", align_bytes=64)
             for j0, j1 in zip(meas_cuts, meas_cuts[1:])
         ]
-        keep_cuts = [0, 2 * P, N]
+        keep_cuts = [0, 2 * P, 4 * P, N]
         keep_sb = [
             held.tile([P, PASSES, n1 - n0], I32, name=f"keep{n0}", align_bytes=64)
             for n0, n1 in zip(keep_cuts, keep_cuts[1:])
@@ -99,6 +99,16 @@ def tile_list_sparse_code_step_kernel(
                 in_=w1[512 * a : 512 * (a + 1), :].rearrange("(p i) c -> p i c", i=PACK)[:, i0:i1, :],
             )
 
+        def load_keep_scales(n0, n1):
+            for q in range(4):
+                nc.sync.dma_start(
+                    out=keep_s[32 * q : 32 * q + 8, n0:n1].bitcast(I32),
+                    in_=keep_scales[:, 4 * q : 4 * q + 4, n0:n1].bitcast(I32),
+                )
+
+        def load_wt(n0, n1):
+            nc.sync.dma_start(out=wt_w[:, 2 * n0 : 2 * n1].bitcast(I32), in_=wt_words[0, :, 2 * n0 : 2 * n1].bitcast(I32))
+
         load_w1(0, 0, PACK // 2)
         nc.sync.dma_start(pick[:], offs)
         nc.sync.dma_start(place[:], offs2)
@@ -111,16 +121,14 @@ def tile_list_sparse_code_step_kernel(
         load_w1(1, 0, PACK)
         load_table(1)
         load_meas(0)
-        for q in range(4):
-            nc.sync.dma_start(
-                out=keep_s[32 * q : 32 * q + 8, :].bitcast(I32),
-                in_=keep_scales[:, 4 * q : 4 * q + 4, :].bitcast(I32),
-            )
+        load_keep_scales(0, N)
         load_keep(0)
-        nc.sync.dma_start(out=wt_w[:].bitcast(I32), in_=wt_words[0].bitcast(I32))
+        load_wt(0, 2 * P)
         nc.sync.dma_start(out=wgo_sb[:, 0:QUARTER], in_=wgo[:, 0:QUARTER])
         load_keep(1)
+        load_wt(2 * P, N)
         load_meas(1)
+        load_keep(2)
         load_meas(2)
         nc.sync.dma_start(out=wgo_sb[:, QUARTER:S], in_=wgo[:, QUARTER:S])
 
@@ -150,7 +158,7 @@ def tile_list_sparse_code_step_kernel(
             )
 
         def quantize_w1(a):
-            grouped = held.tile([P, PACK, P, PACK], BF16, name=f"w1_grouped{a}", align_bytes=64)
+            grouped = held.tile([P, PACK, P, PACK], BF16, name=f"w1_grouped{a}", tag=f"w1_grouped{a}", align_bytes=64)
             group_w1(a, grouped, 0, PACK // 2, nc.scalar.copy)
             group_w1(a, grouped, PACK // 2, PACK, nc.vector.tensor_copy)
             nc.vector.quantize_mx(
@@ -248,7 +256,7 @@ def tile_list_sparse_code_step_kernel(
             step = BANK if width == BANK else SUB
             keep_passes = [
                 (0, width, keep_cols(a, b).bitcast(FP8X4), keep_s[4 * a :, ns], v_cols(a, j0, j1), v_s[4 * a :, j0:j1])
-                for a in range(PASSES)
+                for a in reversed(range(PASSES))
             ]
             wt_passes = [
                 (
@@ -291,58 +299,43 @@ def tile_list_sparse_code_step_kernel(
             quantize_h(j0, j0 + SUB)
         nc.tensor.transpose(banks[0][:, 0:P], thr_rows[:], ident[:])
         nc.scalar.mul(neg_thr[:], banks[0][:, 0:BLOCKS], -1.0)
-        v_w[1, 1] = held.tile([P, BANK], U32, name="v_w11", tag="h_grouped0", align_bytes=64)
+        v_w[1, 1] = held.tile([P, BANK], U32, name="v_w11", tag="h_grouped1", align_bytes=64)
         gather_words(1, BANK, S)
-        zero_window("h_grouped1")
+        zero_window("w1_grouped1")
         zero_window("tab_w1")
 
-        q1, q2, q3, q4 = (0, 256), (256, 512), (512, 768), (768, 1024)
-        put(0, *q1, 2, keep_first=True)
-        zero_window("y0_0")
-        put(1, *q1, 3)
-        zero_window("y1_0")
-        predict_turned(256, 4)
-        put(2, *q1, 5)
-        zero_window("y2_0")
-        predict_turned(384, 2)
-        turn_meas(256, 6)
-        put(3, *q1, 7)
-        turn_meas(384, 0)
-        put(4, *q1, 1)
-        sum_turned(256, 3)
-        put(5, *q1, 4)
-        predict_turned(512, 2)
-        put(6, *q1, 5)
-        sum_turned(384, 5)
-        quantize_h(*q2)
-        put(7, *q1, 5)
-        predict_turned(640, 6)
+        taken = [0, 1]
 
-        put(0, *q2, 7, keep_first=True)
-        turn_meas(512, 0)
-        put(1, *q2, 1)
-        turn_meas(640, 3)
-        put(2, *q2, 4)
-        sum_turned(512, 2)
-        put(3, *q2, 6)
-        predict_turned(768, 5)
-        put(4, *q2, 7)
-        predict_turned(896, 0)
-        put(5, *q2, 1)
-        turn_meas(768, 3)
-        put(6, *q2, 4)
-        sum_turned(640, 4)
-        quantize_h(*q3)
-        put(7, *q2, 4)
-        turn_meas(896, 2)
+        def next_bank():
+            taken.append((taken[-1] + 1) % len(banks))
+            return taken[-1]
 
-        put(0, *q3, 6, keep_first=True)
-        put(1, *q3, 5)
-        sum_turned(768, 7)
-        put(2, *q3, 0)
-        sum_turned(896, 0)
-        quantize_h(*q4)
-        put(3, *q3, 0)
-        for b, banks_b in enumerate(((1, 3), (4, 2), (6, 5), (7, 0))):
-            put(b, *q4, banks_b[0], keep_first=True)
-            put(4 + b, BANK, S, banks_b[1])
+        steps = [
+            (step, j0)
+            for q0 in range(QUARTER, S, QUARTER)
+            for step, j0 in (
+                (predict_turned, q0),
+                (predict_turned, q0 + SUB),
+                (turn_meas, q0),
+                (turn_meas, q0 + SUB),
+                (sum_turned, q0),
+            )
+        ]
+        predict_turned(QUARTER, next_bank())
+        steps = steps[1:]
+        for q0, blocks in ((0, BLOCKS), (QUARTER, BLOCKS), (BANK, BLOCKS // 2)):
+            q1 = q0 + QUARTER
+            for b in range(blocks):
+                put(b, q0, q1, taken[-1] if b == blocks - 1 else next_bank(), keep_first=(b == 0))
+                if len(windows) < BLOCKS:
+                    zero_window(f"y{b}_0")
+                if b == blocks - 2:
+                    sum_turned(q1 + SUB, taken[-1])
+                    quantize_h(q1, q1 + QUARTER)
+                    continue
+                for step, j0 in steps[:1]:
+                    step(j0, taken[-1] if (q0, b) == (0, 0) else next_bank())
+                steps = steps[1:]
+        for b in range(BLOCKS // 2):
+            put(b, S - QUARTER, S, next_bank(), keep_first=True)
+            put(BLOCKS // 2 + b, BANK, S, next_bank())

@@ -19,13 +19,16 @@ ACT = mybir.ActivationFunctionType
 
 P = 128
 PACK = 4
-PASSES = K // (P * PACK)
+PASS = P * PACK
+PASSES = K // PASS
+QUADRANTS = 4
 BANK = 512
-QUARTER = 256
+BANKS = 8
+HALF = S // 2
+QUARTER = S // 4
 SUB = 128
 BLOCKS = N // P
 EARLY_WINDOWS = 3
-ODD = T2 // 2 - 1
 
 
 def tile_list_sparse_code_step_kernel(
@@ -35,14 +38,14 @@ def tile_list_sparse_code_step_kernel(
     with ExitStack() as ctx:
         held = ctx.enter_context(tc.tile_pool(name="held", bufs=1))
         psum = ctx.enter_context(tc.psum_pool(name="psum", bufs=1))
-        banks = [psum.tile([P, BANK], F32, name=f"bank{i}") for i in range(8)]
+        banks = [psum.tile([P, BANK], F32, name=f"bank{i}") for i in range(BANKS)]
 
         pick = held.tile([P, S // 16], U16, name="pick")
         place = held.tile([P, S // 16], U16, name="place")
         tab_w = [held.tile([P, T], I32, name=f"tab_w{a}", tag=f"tab_w{a}", align_bytes=64) for a in range(PASSES)]
         tab_s = held.tile([P, T], U8, name="tab_s", align_bytes=64)
         w1_raw = [held.tile([P, PACK, M], F32, name=f"w1_raw{a}") for a in range(PASSES)]
-        meas_cuts = [0, QUARTER, BANK, S]
+        meas_cuts = [0, QUARTER, HALF, S]
         meas_sb = [
             held.tile([P, PACK, j1 - j0], F32, name=f"meas{j0}", align_bytes=64)
             for j0, j1 in zip(meas_cuts, meas_cuts[1:])
@@ -67,15 +70,15 @@ def tile_list_sparse_code_step_kernel(
         nc.gpsimd.memset(keep_s[:].bitcast(I32), 0)
         nc.gpsimd.memset(wt_s[:].bitcast(I32), 0)
         make_identity(nc, ident[:])
-        for q in range(4):
+        for q in range(QUADRANTS):
             nc.gpsimd.dma_start(
                 out=wt_s[32 * q : 32 * q + 4, :].bitcast(I32), in_=wt_scales[0, 4 * q : 4 * q + 4, :].bitcast(I32)
             )
 
-        nc.vector.memset(windows[0][:, 0:ODD], 0.0)
-        nc.vector.memset(windows[0][:, ODD:T2], 0.0)
-        nc.vector.memset(windows[1][:, 0 : BANK - 1], 0.0)
-        nc.vector.memset(windows[1][:, BANK - 1 : T2 // 2], 0.0)
+        for window, columns in ((windows[0], T2), (windows[1], T2 // 2)):
+            odd = columns // 2 - 1
+            nc.vector.memset(window[:, 0:odd], 0.0)
+            nc.vector.memset(window[:, odd:columns], 0.0)
         nc.gpsimd.memset(windows[1][:, T2 // 2 : T2], 0.0)
         nc.gpsimd.memset(windows[2][:], 0.0)
 
@@ -90,43 +93,35 @@ def tile_list_sparse_code_step_kernel(
 
         def load_keep(u):
             nc.sync.dma_start(
-                out=keep_sb[u][:], in_=keep_view[:, :, 4 * keep_cuts[u] : 4 * keep_cuts[u + 1]].bitcast(I32)
+                out=keep_sb[u][:], in_=keep_view[:, :, PACK * keep_cuts[u] : PACK * keep_cuts[u + 1]].bitcast(I32)
             )
 
         def load_w1(a, i0, i1):
             nc.sync.dma_start(
                 out=w1_raw[a][:, i0:i1, :],
-                in_=w1[512 * a : 512 * (a + 1), :].rearrange("(p i) c -> p i c", i=PACK)[:, i0:i1, :],
+                in_=w1[PASS * a : PASS * (a + 1), :].rearrange("(p i) c -> p i c", i=PACK)[:, i0:i1, :],
             )
 
-        def load_keep_scales(n0, n1):
-            for q in range(4):
+        def load_scale_rows(tile, scales):
+            for q in range(QUADRANTS):
                 nc.sync.dma_start(
-                    out=keep_s[32 * q : 32 * q + 8, n0:n1].bitcast(I32),
-                    in_=keep_scales[:, 4 * q : 4 * q + 4, n0:n1].bitcast(I32),
+                    out=tile[32 * q : 32 * q + 8, :].bitcast(I32), in_=scales[:, 4 * q : 4 * q + 4, :].bitcast(I32)
                 )
-
-        def load_wt(n0, n1):
-            nc.sync.dma_start(out=wt_w[:, 2 * n0 : 2 * n1].bitcast(I32), in_=wt_words[0, :, 2 * n0 : 2 * n1].bitcast(I32))
 
         load_w1(0, 0, PACK // 2)
         nc.sync.dma_start(pick[:], offs)
         nc.sync.dma_start(place[:], offs2)
-        for q in range(4):
-            nc.sync.dma_start(
-                out=tab_s[32 * q : 32 * q + 8, :].bitcast(I32), in_=tab_scales[:, 4 * q : 4 * q + 4, :].bitcast(I32)
-            )
+        load_scale_rows(tab_s, tab_scales)
         load_table(0)
         load_w1(0, PACK // 2, PACK)
         load_w1(1, 0, PACK)
         load_table(1)
         load_meas(0)
-        load_keep_scales(0, N)
+        load_scale_rows(keep_s, keep_scales)
         load_keep(0)
-        load_wt(0, 2 * P)
+        nc.sync.dma_start(out=wt_w[:].bitcast(I32), in_=wt_words[0].bitcast(I32))
         nc.sync.dma_start(out=wgo_sb[:, 0:QUARTER], in_=wgo[:, 0:QUARTER])
         load_keep(1)
-        load_wt(2 * P, N)
         load_meas(1)
         load_keep(2)
         load_meas(2)
@@ -135,9 +130,9 @@ def tile_list_sparse_code_step_kernel(
         w1_w = [held.tile([P, M], U32, name=f"w1_w{a}", align_bytes=64) for a in range(PASSES)]
         w1_s = [held.tile([P, M], U8, name=f"w1_s{a}", align_bytes=64) for a in range(PASSES)]
         v_w = {
-            (0, 0): held.tile([P, BANK], U32, name="v_w00", align_bytes=64),
-            (0, 1): held.tile([P, BANK], U32, name="v_w01", align_bytes=64),
-            (1, 0): held.tile([P, BANK], U32, name="v_w10", align_bytes=64),
+            (0, 0): held.tile([P, HALF], U32, name="v_w00", align_bytes=64),
+            (0, 1): held.tile([P, HALF], U32, name="v_w01", align_bytes=64),
+            (1, 0): held.tile([P, HALF], U32, name="v_w10", align_bytes=64),
         }
         v_s = held.tile([P, S], U8, name="v_s", align_bytes=64)
         h_cuts = [0, SUB] + list(range(QUARTER, S + 1, QUARTER))
@@ -150,48 +145,56 @@ def tile_list_sparse_code_step_kernel(
         meas_turneds = {j0: held.tile([P, M], F32, name=f"meas_turned{j0}") for j0 in range(QUARTER, S, SUB)}
         neg_preds = {j0: held.tile([P, M], F32, name=f"neg_pred{j0}") for j0 in range(QUARTER, S, SUB)}
 
-
-        def group_w1(a, grouped, t0, t1, copy):
+        def group_w1(a, grouped, t0, t1, r0, r1, copy):
             copy(
-                out=grouped[:, t0:t1, :, :].rearrange("p t m i -> p m t i"),
-                in_=w1_raw[a][:].rearrange("p i (m t) -> p m t i", t=PACK)[:, :, t0:t1, :],
+                out=grouped[:, t0:t1, r0:r1, :].rearrange("p t r i -> p r t i"),
+                in_=w1_raw[a][:].rearrange("p i (r t) -> p r t i", t=PACK)[:, r0:r1, t0:t1, :],
             )
 
-        def quantize_w1(a):
+        def quantize_w1(a, scalar_rows):
             grouped = held.tile([P, PACK, P, PACK], BF16, name=f"w1_grouped{a}", tag=f"w1_grouped{a}", align_bytes=64)
-            group_w1(a, grouped, 0, PACK // 2, nc.scalar.copy)
-            group_w1(a, grouped, PACK // 2, PACK, nc.vector.tensor_copy)
+            group_w1(a, grouped, 0, PACK // 2, 0, P, nc.scalar.copy)
+            if scalar_rows:
+                group_w1(a, grouped, PACK // 2, PACK, 0, scalar_rows, nc.scalar.copy)
+            group_w1(a, grouped, PACK // 2, PACK, scalar_rows, P, nc.vector.tensor_copy)
             nc.vector.quantize_mx(
-                out=w1_w[a][:].bitcast(FP8X4), scales=w1_s[a][:], in_=grouped[:].rearrange("p t m i -> p (t m i)")
+                out=w1_w[a][:].bitcast(FP8X4), scales=w1_s[a][:], in_=grouped[:].rearrange("p t r i -> p (t r i)")
             )
 
         def v_cols(a, j0, j1):
-            return v_w[a, j0 // BANK][:, j0 % BANK : j0 % BANK + j1 - j0]
+            return v_w[a, j0 // HALF][:, j0 % HALF : j0 % HALF + j1 - j0]
 
         def gather_words(a, j0, j1):
             nc.vector.tensor_copy(v_cols(a, j0, j1), tab_w[a][:].bitcast(U32).indirect(pick[:, j0 // 16 : j1 // 16]))
 
+        def part_of(cuts, first):
+            return max(u for u, cut in enumerate(cuts) if cut <= first)
+
         def meas_cols(j0, j1):
-            u = max(i for i, cut in enumerate(meas_cuts) if cut <= j0)
+            u = part_of(meas_cuts, j0)
             return meas_sb[u][:, :, j0 - meas_cuts[u] : j1 - meas_cuts[u]]
 
         def h_cols(j0, j1):
-            u = max(i for i, cut in enumerate(h_cuts) if cut <= j0)
+            u = part_of(h_cuts, j0)
             return h_grouped[u][:, PACK * (j0 - h_cuts[u]) : PACK * (j1 - h_cuts[u])]
+
+        def keep_cols(a, b):
+            u = part_of(keep_cuts, b * P)
+            return keep_sb[u][:, a, b * P - keep_cuts[u] : (b + 1) * P - keep_cuts[u]]
 
         def quantize_h(j0, j1):
             nc.vector.quantize_mx(out=h_w[:, j0:j1].bitcast(FP8X4), scales=h_s[:, j0:j1], in_=h_cols(j0, j1))
 
         nc.vector.tensor_copy(v_s[:], tab_s[:].indirect(pick[:]))
-        gather_words(0, 0, BANK)
-        gather_words(0, BANK, S)
-        for a in range(PASSES):
-            quantize_w1(a)
+        gather_words(0, 0, HALF)
+        gather_words(0, HALF, S)
+        quantize_w1(0, scalar_rows=P // 2)
+        quantize_w1(1, scalar_rows=0)
         gather_words(1, 0, QUARTER)
-        gather_words(1, QUARTER, BANK)
+        gather_words(1, QUARTER, HALF)
 
-        def residual(j0):
-            pred = banks[j0 // SUB]
+        def residual_on_vector(j0, bank):
+            pred = banks[bank]
             for a in range(PASSES):
                 for t in range(PACK):
                     ms = slice(t * P, (t + 1) * P)
@@ -205,9 +208,9 @@ def tile_list_sparse_code_step_kernel(
                         stop=(a == PASSES - 1 and t == PACK - 1),
                     )
             nc.vector.tensor_tensor(
-                h_cols(j0, j0 + SUB).rearrange("p (c i t) -> p c t i", i=2, t=PACK),
-                meas_cols(j0, j0 + SUB).rearrange("p t (c i) -> p c t i", i=2),
-                pred[:].rearrange("p (t c i) -> p c t i", t=PACK, i=2),
+                h_cols(j0, j0 + SUB).rearrange("p (c e t) -> p c t e", e=2, t=PACK),
+                meas_cols(j0, j0 + SUB).rearrange("p t (c e) -> p c t e", e=2),
+                pred[:].rearrange("p (t c e) -> p c t e", t=PACK, e=2),
                 ALU.subtract,
             )
 
@@ -246,14 +249,10 @@ def tile_list_sparse_code_step_kernel(
                 banks[bank][:].rearrange("p (t j) -> p j t", t=PACK),
             )
 
-        def keep_cols(a, b):
-            u = max(i for i, cut in enumerate(keep_cuts) if cut <= b * P)
-            return keep_sb[u][:, a, b * P - keep_cuts[u] : (b + 1) * P - keep_cuts[u]]
-
         def put(b, j0, j1, bank, keep_first=False):
             ns = slice(b * P, (b + 1) * P)
             width = j1 - j0
-            step = BANK if width == BANK else SUB
+            wt_width = BANK if width == BANK else SUB
             keep_passes = [
                 (0, width, keep_cols(a, b).bitcast(FP8X4), keep_s[4 * a :, ns], v_cols(a, j0, j1), v_s[4 * a :, j0:j1])
                 for a in reversed(range(PASSES))
@@ -261,13 +260,13 @@ def tile_list_sparse_code_step_kernel(
             wt_passes = [
                 (
                     c0,
-                    c0 + step,
+                    c0 + wt_width,
                     wt_w[:, 2 * b * P : 2 * (b + 1) * P].bitcast(FP4X4),
                     wt_s[:, ns],
-                    h_w[:, j0 + c0 : j0 + c0 + step],
-                    h_s[:, j0 + c0 : j0 + c0 + step],
+                    h_w[:, j0 + c0 : j0 + c0 + wt_width],
+                    h_s[:, j0 + c0 : j0 + c0 + wt_width],
                 )
-                for c0 in range(0, width, step)
+                for c0 in range(0, width, wt_width)
             ]
             passes = keep_passes + wt_passes if keep_first else wt_passes + keep_passes
             for u, (c0, c1, lhs, lhs_scale, rhs, rhs_scale) in enumerate(passes):
@@ -288,27 +287,28 @@ def tile_list_sparse_code_step_kernel(
             if j1 == S:
                 nc.sync.dma_start(out=out[b * P : (b + 1) * P, :], in_=windows[b][:])
 
-        def zero_window(tag):
-            window = held.tile([P, T2], F32, name=f"window{len(windows)}", tag=tag, align_bytes=64)
+        def zero_window(after):
+            window = held.tile([P, T2], F32, name=f"window{len(windows)}", tag=after, align_bytes=64)
             nc.gpsimd.memset(window[:], 0.0)
             windows.append(window)
 
-        for j0 in range(0, QUARTER, SUB):
-            residual(j0)
-        for j0 in range(0, QUARTER, SUB):
+        used = []
+
+        def next_bank():
+            used.append(len(used) % BANKS)
+            return used[-1]
+
+        first_entries = range(0, QUARTER, SUB)
+        for j0 in first_entries:
+            residual_on_vector(j0, next_bank())
+        for j0 in first_entries:
             quantize_h(j0, j0 + SUB)
         nc.tensor.transpose(banks[0][:, 0:P], thr_rows[:], ident[:])
         nc.scalar.mul(neg_thr[:], banks[0][:, 0:BLOCKS], -1.0)
-        v_w[1, 1] = held.tile([P, BANK], U32, name="v_w11", tag="h_grouped1", align_bytes=64)
-        gather_words(1, BANK, S)
+        v_w[1, 1] = held.tile([P, HALF], U32, name="v_w11", tag="h_grouped1", align_bytes=64)
+        gather_words(1, HALF, S)
         zero_window("w1_grouped1")
         zero_window("tab_w1")
-
-        taken = [0, 1]
-
-        def next_bank():
-            taken.append((taken[-1] + 1) % len(banks))
-            return taken[-1]
 
         steps = [
             (step, j0)
@@ -323,19 +323,21 @@ def tile_list_sparse_code_step_kernel(
         ]
         predict_turned(QUARTER, next_bank())
         steps = steps[1:]
-        for q0, blocks in ((0, BLOCKS), (QUARTER, BLOCKS), (BANK, BLOCKS // 2)):
+
+        for q0, blocks in ((0, BLOCKS), (QUARTER, BLOCKS), (HALF, BLOCKS // 2)):
             q1 = q0 + QUARTER
             for b in range(blocks):
-                put(b, q0, q1, taken[-1] if b == blocks - 1 else next_bank(), keep_first=(b == 0))
+                put(b, q0, q1, used[-1] if b == blocks - 1 else next_bank(), keep_first=(b == 0))
                 if len(windows) < BLOCKS:
                     zero_window(f"y{b}_0")
                 if b == blocks - 2:
-                    sum_turned(q1 + SUB, taken[-1])
+                    sum_turned(q1 + SUB, used[-1])
                     quantize_h(q1, q1 + QUARTER)
-                    continue
-                for step, j0 in steps[:1]:
-                    step(j0, taken[-1] if (q0, b) == (0, 0) else next_bank())
-                steps = steps[1:]
+                elif steps:
+                    step, j0 = steps[0]
+                    step(j0, used[-1] if (q0, b) == (0, 0) else next_bank())
+                    steps = steps[1:]
+
         for b in range(BLOCKS // 2):
             put(b, S - QUARTER, S, next_bank(), keep_first=True)
-            put(BLOCKS // 2 + b, BANK, S, next_bank())
+            put(BLOCKS // 2 + b, HALF, S, next_bank())

@@ -65,22 +65,18 @@ def tile_list_sparse_code_step_kernel(
         windows = [held.tile([P, T2], F32, name=f"window{i}") for i in range(EARLY_WINDOWS)]
 
         nc.gpsimd.memset(tab_s[:].bitcast(I32), 0)
-        nc.gpsimd.memset(thr_rows[:], 0.0)
-        nc.gpsimd.dma_start(out=thr_rows[0:BLOCKS, :], in_=thr.rearrange("(b p) -> b p", p=P))
-        nc.gpsimd.memset(keep_s[:].bitcast(I32), 0)
-        nc.gpsimd.memset(wt_s[:].bitcast(I32), 0)
-        make_identity(nc, ident[:])
+        nc.vector.memset(keep_s[:].bitcast(I32), 0)
+        for window in windows:
+            nc.vector.memset(window[:], 0.0)
+        nc.vector.memset(thr_rows[:], 0.0)
+        nc.vector.memset(wt_s[:].bitcast(I32), 0)
+        nc.vector.memset(ident[:], 0.0)
+        make_identity(nc, ident[:], nomemset=True)
         for q in range(QUADRANTS):
             nc.gpsimd.dma_start(
                 out=wt_s[32 * q : 32 * q + 4, :].bitcast(I32), in_=wt_scales[0, 4 * q : 4 * q + 4, :].bitcast(I32)
             )
-
-        for window, columns in ((windows[0], T2), (windows[1], T2 // 2)):
-            odd = columns // 2 - 1
-            nc.vector.memset(window[:, 0:odd], 0.0)
-            nc.vector.memset(window[:, odd:columns], 0.0)
-        nc.gpsimd.memset(windows[1][:, T2 // 2 : T2], 0.0)
-        nc.gpsimd.memset(windows[2][:], 0.0)
+        nc.gpsimd.dma_start(out=thr_rows[0:BLOCKS, :], in_=thr.rearrange("(b p) -> b p", p=P))
 
         keep_view = keep_words.rearrange("a p c i -> p a (c i)")
         meas_view = meas.rearrange("(p t) j -> p t j", t=PACK)

@@ -65,18 +65,13 @@ def tile_list_sparse_code_step_kernel(
         windows = [held.tile([P, T2], F32, name=f"window{i}") for i in range(EARLY_WINDOWS)]
 
         nc.gpsimd.memset(tab_s[:].bitcast(I32), 0)
-        nc.vector.memset(keep_s[:].bitcast(I32), 0)
-        for window in windows:
-            nc.vector.memset(window[:], 0.0)
         nc.vector.memset(thr_rows[:], 0.0)
         nc.vector.memset(wt_s[:].bitcast(I32), 0)
+        nc.vector.memset(keep_s[:].bitcast(I32), 0)
         nc.vector.memset(ident[:], 0.0)
+        for window in windows:
+            nc.vector.memset(window[:], 0.0)
         make_identity(nc, ident[:], nomemset=True)
-        for q in range(QUADRANTS):
-            nc.gpsimd.dma_start(
-                out=wt_s[32 * q : 32 * q + 4, :].bitcast(I32), in_=wt_scales[0, 4 * q : 4 * q + 4, :].bitcast(I32)
-            )
-        nc.gpsimd.dma_start(out=thr_rows[0:BLOCKS, :], in_=thr.rearrange("(b p) -> b p", p=P))
 
         keep_view = keep_words.rearrange("a p c i -> p a (c i)")
         meas_view = meas.rearrange("(p t) j -> p t j", t=PACK)
@@ -106,17 +101,22 @@ def tile_list_sparse_code_step_kernel(
 
         load_w1(0, 0, PACK // 2)
         nc.sync.dma_start(pick[:], offs)
-        nc.sync.dma_start(place[:], offs2)
+        nc.sync.dma_start(out=thr_rows[0:BLOCKS, :], in_=thr.rearrange("(b p) -> b p", p=P))
         load_scale_rows(tab_s, tab_scales)
         load_table(0)
         load_w1(0, PACK // 2, PACK)
         load_w1(1, 0, PACK)
+        for q in range(QUADRANTS):
+            nc.sync.dma_start(
+                out=wt_s[q : P : 32, :].bitcast(I32), in_=wt_scales[0, q::4, :].bitcast(I32)
+            )
         load_table(1)
         load_meas(0)
         load_scale_rows(keep_s, keep_scales)
         load_keep(0)
         nc.sync.dma_start(out=wt_w[:].bitcast(I32), in_=wt_words[0].bitcast(I32))
         nc.sync.dma_start(out=wgo_sb[:, 0:QUARTER], in_=wgo[:, 0:QUARTER])
+        nc.sync.dma_start(place[:], offs2)
         load_keep(1)
         load_meas(1)
         load_keep(2)
@@ -301,10 +301,9 @@ def tile_list_sparse_code_step_kernel(
             quantize_h(j0, j0 + SUB)
         nc.tensor.transpose(banks[0][:, 0:P], thr_rows[:], ident[:])
         nc.scalar.mul(neg_thr[:], banks[0][:, 0:BLOCKS], -1.0)
-        v_w[1, 1] = held.tile([P, HALF], U32, name="v_w11", tag="h_grouped1", align_bytes=64)
+        v_w[1, 1] = held.tile([P, HALF], U32, name="v_w11", tag="h_grouped0", align_bytes=64)
         gather_words(1, HALF, S)
-        zero_window("w1_grouped1")
-        zero_window("tab_w1")
+        zero_window("h_grouped1")
 
         steps = [
             (step, j0)

@@ -28,7 +28,9 @@ HALF = S // 2
 QUARTER = S // 4
 SUB = 128
 BLOCKS = N // P
-EARLY_WINDOWS = 3
+EARLY_WINDOWS = 2
+VECTOR_ZEROES = 1024
+FLAT = 96
 
 
 def tile_list_sparse_code_step_kernel(
@@ -40,38 +42,51 @@ def tile_list_sparse_code_step_kernel(
         psum = ctx.enter_context(tc.psum_pool(name="psum", bufs=1))
         banks = [psum.tile([P, BANK], F32, name=f"bank{i}") for i in range(BANKS)]
 
+        shared = ctx.enter_context(tc.tile_pool(name="shared", bufs=1))
+
+        def placed(name, shape, dtype, kib):
+            return shared.tile(shape, dtype, name=name, offset=kib * 1024, align_bytes=64)
+
         pick = held.tile([P, S // 16], U16, name="pick")
         place = held.tile([P, S // 16], U16, name="place")
-        tab_w = [held.tile([P, T], I32, name=f"tab_w{a}", tag=f"tab_w{a}", align_bytes=64) for a in range(PASSES)]
-        tab_s = held.tile([P, T], U8, name="tab_s", align_bytes=64)
-        w1_raw = [held.tile([P, PACK, M], F32, name=f"w1_raw{a}") for a in range(PASSES)]
+        tab_w = [placed("tab_w0", [P, T], I32, 0), placed("tab_w1", [P, T], I32, 9)]
+        tab_s = placed("tab_s", [P, T], U8, 8)
+        keep_s = placed("keep_s", [P, N], U8, 8)
+        w1_raw = [placed(f"w1_raw{a}", [P, PACK, M], F32, 17 + 8 * a) for a in range(PASSES)]
+        w1_grouped = [placed(f"w1_grouped{a}", [P, PACK, P, PACK], BF16, 33 + 4 * a) for a in range(PASSES)]
         meas_cuts = [0, QUARTER, HALF, S]
         meas_sb = [
-            held.tile([P, PACK, j1 - j0], F32, name=f"meas{j0}", align_bytes=64)
-            for j0, j1 in zip(meas_cuts, meas_cuts[1:])
+            placed(f"meas{j0}", [P, PACK, j1 - j0], F32, kib)
+            for j0, j1, kib in zip(meas_cuts, meas_cuts[1:], (0, 17, 25))
         ]
         keep_cuts = [0, 2 * P, 4 * P, N]
         keep_sb = [
-            held.tile([P, PASSES, n1 - n0], I32, name=f"keep{n0}", align_bytes=64)
-            for n0, n1 in zip(keep_cuts, keep_cuts[1:])
+            placed(f"keep{n0}", [P, PASSES, n1 - n0], I32, kib)
+            for n0, n1, kib in zip(keep_cuts, keep_cuts[1:], (4, 21, 33))
         ]
-        wt_w = held.tile([P, 2 * N], U8, name="wt_w", align_bytes=64)
-        keep_s = held.tile([P, N], U8, name="keep_s", align_bytes=64)
+        wt_cuts = [0, N // 2, N]
+        wt_sb = [placed(f"wt{n0}", [P, 2 * (n1 - n0)], U8, kib) for n0, n1, kib in zip(wt_cuts, wt_cuts[1:], (6, 23))]
+        wgo_cuts = [0, QUARTER, S]
+        wgo_sb = [placed(f"wgo{j0}", [P, j1 - j0], F32, kib) for j0, j1, kib in zip(wgo_cuts, wgo_cuts[1:], (7, 10))]
         wt_s = held.tile([P, N], U8, name="wt_s", align_bytes=64)
-        wgo_sb = held.tile([P, S], F32, name="wgo_sb")
+        v_flat = held.tile([P, S], U8, name="v_flat", align_bytes=64)
+        v_s = [held.tile([P, S], U8, name=f"v_s{a}", align_bytes=64) for a in range(PASSES)]
         thr_rows = held.tile([P, P], F32, name="thr_rows")
         ident = held.tile([P, P], F32, name="ident")
         neg_thr = held.tile([P, BLOCKS], F32, name="neg_thr")
         windows = [held.tile([P, T2], F32, name=f"window{i}") for i in range(EARLY_WINDOWS)]
 
-        nc.gpsimd.memset(tab_s[:].bitcast(I32), 0)
-        nc.vector.memset(thr_rows[:], 0.0)
         nc.vector.memset(wt_s[:].bitcast(I32), 0)
-        nc.vector.memset(keep_s[:].bitcast(I32), 0)
-        nc.vector.memset(ident[:], 0.0)
-        for window in windows:
-            nc.vector.memset(window[:], 0.0)
-        make_identity(nc, ident[:], nomemset=True)
+        for plane in v_s:
+            nc.vector.memset(plane[:].bitcast(I32), 0)
+        nc.vector.memset(windows[0][:, 0 : VECTOR_ZEROES - 1], 0.0)
+        nc.vector.memset(windows[0][:, VECTOR_ZEROES - 1 : VECTOR_ZEROES], 0.0)
+        nc.gpsimd.memset(tab_s[0:FLAT, :].bitcast(I32), 0)
+        nc.gpsimd.memset(thr_rows[:], 0.0)
+        nc.gpsimd.dma_start(out=thr_rows[0:BLOCKS, :], in_=thr.rearrange("(b p) -> b p", p=P))
+        make_identity(nc, ident[:])
+        nc.gpsimd.memset(windows[0][:, VECTOR_ZEROES:T2], 0.0)
+        nc.gpsimd.memset(windows[1][:], 0.0)
 
         keep_view = keep_words.rearrange("a p c i -> p a (c i)")
         meas_view = meas.rearrange("(p t) j -> p t j", t=PACK)
@@ -87,41 +102,40 @@ def tile_list_sparse_code_step_kernel(
                 out=keep_sb[u][:], in_=keep_view[:, :, PACK * keep_cuts[u] : PACK * keep_cuts[u + 1]].bitcast(I32)
             )
 
-        def load_w1(a, i0, i1):
+        def load_wt(u):
             nc.sync.dma_start(
-                out=w1_raw[a][:, i0:i1, :],
-                in_=w1[PASS * a : PASS * (a + 1), :].rearrange("(p i) c -> p i c", i=PACK)[:, i0:i1, :],
+                out=wt_sb[u][:].bitcast(I32), in_=wt_words[0][:, 2 * wt_cuts[u] : 2 * wt_cuts[u + 1]].bitcast(I32)
             )
 
-        def load_scale_rows(tile, scales):
-            for q in range(QUADRANTS):
-                nc.sync.dma_start(
-                    out=tile[32 * q : 32 * q + 8, :].bitcast(I32), in_=scales[:, 4 * q : 4 * q + 4, :].bitcast(I32)
-                )
+        def load_wgo(u):
+            nc.sync.dma_start(out=wgo_sb[u][:], in_=wgo[:, wgo_cuts[u] : wgo_cuts[u + 1]])
 
-        load_w1(0, 0, PACK // 2)
+        def load_w1(a):
+            nc.sync.dma_start(
+                out=w1_raw[a][:], in_=w1[PASS * a : PASS * (a + 1), :].rearrange("(p i) c -> p i c", i=PACK)
+            )
+
+        def carry_scale_rows(a, r):
+            nc.sync.dma_start(
+                out=v_s[a][4 * a + r : P : 32, :].bitcast(I32),
+                in_=v_flat[FLAT + 16 * a + r : FLAT + 16 * a + 16 : 4, :].bitcast(I32),
+            )
+
+        nc.sync.dma_start(out=tab_s[FLAT:P, :].bitcast(I32), in_=tab_scales.rearrange("a q t -> (a q) t").bitcast(I32))
         nc.sync.dma_start(pick[:], offs)
-        nc.sync.dma_start(out=thr_rows[0:BLOCKS, :], in_=thr.rearrange("(b p) -> b p", p=P))
-        load_scale_rows(tab_s, tab_scales)
         load_table(0)
-        load_w1(0, PACK // 2, PACK)
-        load_w1(1, 0, PACK)
-        for q in range(QUADRANTS):
-            nc.sync.dma_start(
-                out=wt_s[q : P : 32, :].bitcast(I32), in_=wt_scales[0, q::4, :].bitcast(I32)
-            )
-        load_table(1)
-        load_meas(0)
-        load_scale_rows(keep_s, keep_scales)
-        load_keep(0)
-        nc.sync.dma_start(out=wt_w[:].bitcast(I32), in_=wt_words[0].bitcast(I32))
-        nc.sync.dma_start(out=wgo_sb[:, 0:QUARTER], in_=wgo[:, 0:QUARTER])
         nc.sync.dma_start(place[:], offs2)
-        load_keep(1)
-        load_meas(1)
-        load_keep(2)
-        load_meas(2)
-        nc.sync.dma_start(out=wgo_sb[:, QUARTER:S], in_=wgo[:, QUARTER:S])
+        for q in range(QUADRANTS):
+            nc.sync.dma_start(out=wt_s[q:P:32, :].bitcast(I32), in_=wt_scales[0, q::4, :].bitcast(I32))
+        load_w1(0)
+        load_w1(1)
+        nc.vector.tensor_copy(v_flat[:], tab_s[:].indirect(pick[:]))
+        carries = [(0, 0), (1, 0), (0, 1), (1, 1), (0, 2), (0, 3), (1, 2), (1, 3)]
+        for a, r in carries[:6]:
+            carry_scale_rows(a, r)
+        load_table(1)
+        for a, r in carries[6:]:
+            carry_scale_rows(a, r)
 
         w1_w = [held.tile([P, M], U32, name=f"w1_w{a}", align_bytes=64) for a in range(PASSES)]
         w1_s = [held.tile([P, M], U8, name=f"w1_s{a}", align_bytes=64) for a in range(PASSES)]
@@ -130,7 +144,6 @@ def tile_list_sparse_code_step_kernel(
             (0, 1): held.tile([P, HALF], U32, name="v_w01", align_bytes=64),
             (1, 0): held.tile([P, HALF], U32, name="v_w10", align_bytes=64),
         }
-        v_s = held.tile([P, S], U8, name="v_s", align_bytes=64)
         h_cuts = [0, SUB] + list(range(QUARTER, S + 1, QUARTER))
         h_grouped = [
             held.tile([P, (j1 - j0) * PACK], BF16, name=f"h_grouped{u}", tag=f"h_grouped{u}", align_bytes=64)
@@ -148,7 +161,7 @@ def tile_list_sparse_code_step_kernel(
             )
 
         def quantize_w1(a, scalar_rows):
-            grouped = held.tile([P, PACK, P, PACK], BF16, name=f"w1_grouped{a}", tag=f"w1_grouped{a}", align_bytes=64)
+            grouped = w1_grouped[a]
             group_w1(a, grouped, 0, PACK // 2, 0, P, nc.scalar.copy)
             if scalar_rows:
                 group_w1(a, grouped, PACK // 2, PACK, 0, scalar_rows, nc.scalar.copy)
@@ -178,14 +191,37 @@ def tile_list_sparse_code_step_kernel(
             u = part_of(keep_cuts, b * P)
             return keep_sb[u][:, a, b * P - keep_cuts[u] : (b + 1) * P - keep_cuts[u]]
 
+        def wt_cols(b):
+            u = part_of(wt_cuts, b * P)
+            return wt_sb[u][:, 2 * (b * P - wt_cuts[u]) : 2 * ((b + 1) * P - wt_cuts[u])]
+
+        def wgo_cols(j0, j1):
+            u = part_of(wgo_cuts, j0)
+            return wgo_sb[u][:, j0 - wgo_cuts[u] : j1 - wgo_cuts[u]]
+
         def quantize_h(j0, j1):
             nc.vector.quantize_mx(out=h_w[:, j0:j1].bitcast(FP8X4), scales=h_s[:, j0:j1], in_=h_cols(j0, j1))
 
-        nc.vector.tensor_copy(v_s[:], tab_s[:].indirect(pick[:]))
         gather_words(0, 0, HALF)
         gather_words(0, HALF, S)
-        quantize_w1(0, scalar_rows=P // 2)
+        load_meas(0)
+        nc.gpsimd.memset(keep_s[:].bitcast(I32), 0)
+        for q in range(QUADRANTS):
+            nc.sync.dma_start(
+                out=keep_s[32 * q : 32 * q + 8, :].bitcast(I32), in_=keep_scales[:, 4 * q : 4 * q + 4, :].bitcast(I32)
+            )
+        load_keep(0)
+        load_wt(0)
+        load_wgo(0)
+        quantize_w1(0, scalar_rows=0)
         quantize_w1(1, scalar_rows=0)
+        load_keep(1)
+        load_meas(1)
+        load_wt(1)
+        load_keep(2)
+        load_meas(2)
+        windows.append(placed("window2", [P, T2], F32, 37))
+        nc.gpsimd.memset(windows[2][:], 0.0)
         gather_words(1, 0, QUARTER)
         gather_words(1, QUARTER, HALF)
 
@@ -199,7 +235,7 @@ def tile_list_sparse_code_step_kernel(
                         lhsT=w1_w[a][:, ms].bitcast(FP8X4),
                         lhsT_scale=w1_s[a][:, ms],
                         rhs=v_cols(a, j0, j0 + SUB).bitcast(FP8X4),
-                        rhs_scale=v_s[4 * a :, j0 : j0 + SUB],
+                        rhs_scale=v_s[a][4 * a :, j0 : j0 + SUB],
                         start=(a == 0 and t == 0),
                         stop=(a == PASSES - 1 and t == PACK - 1),
                     )
@@ -215,7 +251,7 @@ def tile_list_sparse_code_step_kernel(
                 nc.tensor.matmul_mx(
                     out=banks[bank][:],
                     lhsT=v_cols(a, j0, j0 + SUB).bitcast(FP8X4),
-                    lhsT_scale=v_s[4 * a :, j0 : j0 + SUB],
+                    lhsT_scale=v_s[a][4 * a :, j0 : j0 + SUB],
                     rhs=w1_w[a][:].bitcast(FP8X4),
                     rhs_scale=w1_s[a][:],
                     start=(a == 0),
@@ -250,14 +286,14 @@ def tile_list_sparse_code_step_kernel(
             width = j1 - j0
             wt_width = BANK if width == BANK else SUB
             keep_passes = [
-                (0, width, keep_cols(a, b).bitcast(FP8X4), keep_s[4 * a :, ns], v_cols(a, j0, j1), v_s[4 * a :, j0:j1])
+                (0, width, keep_cols(a, b).bitcast(FP8X4), keep_s[4 * a :, ns], v_cols(a, j0, j1), v_s[a][4 * a :, j0:j1])
                 for a in reversed(range(PASSES))
             ]
             wt_passes = [
                 (
                     c0,
                     c0 + wt_width,
-                    wt_w[:, 2 * b * P : 2 * (b + 1) * P].bitcast(FP4X4),
+                    wt_cols(b).bitcast(FP4X4),
                     wt_s[:, ns],
                     h_w[:, j0 + c0 : j0 + c0 + wt_width],
                     h_s[:, j0 + c0 : j0 + c0 + wt_width],
@@ -278,7 +314,7 @@ def tile_list_sparse_code_step_kernel(
             y = held.tile([P, width], F32, name=f"y{b}_{j0}", tag=f"y{b}_{j0}", align_bytes=64)
             nc.scalar.activation(y[:], banks[bank][:, 0:width], ACT.Relu, bias=neg_thr[:, b : b + 1])
             nc.vector.tensor_tensor(
-                windows[b][:].indirect(place[:, j0 // 16 : j1 // 16]), y[:], wgo_sb[:, j0:j1], ALU.mult
+                windows[b][:].indirect(place[:, j0 // 16 : j1 // 16]), y[:], wgo_cols(j0, j1), ALU.mult
             )
             if j1 == S:
                 nc.sync.dma_start(out=out[b * P : (b + 1) * P, :], in_=windows[b][:])
@@ -303,6 +339,7 @@ def tile_list_sparse_code_step_kernel(
         nc.scalar.mul(neg_thr[:], banks[0][:, 0:BLOCKS], -1.0)
         v_w[1, 1] = held.tile([P, HALF], U32, name="v_w11", tag="h_grouped0", align_bytes=64)
         gather_words(1, HALF, S)
+        load_wgo(1)
         zero_window("h_grouped1")
 
         steps = [

@@ -54,10 +54,10 @@ def tile_list_sparse_code_step_kernel(
         keep_s = placed("keep_s", [P, N], U8, 8)
         w1_raw = [placed(f"w1_raw{a}", [P, PACK, M], F32, 17 + 8 * a) for a in range(PASSES)]
         w1_grouped = [placed(f"w1_grouped{a}", [P, PACK, P, PACK], BF16, 33 + 4 * a) for a in range(PASSES)]
-        meas_cuts = [0, QUARTER, HALF, S]
+        meas_cuts = [0, SUB, QUARTER, HALF, S]
         meas_sb = [
             placed(f"meas{j0}", [P, PACK, j1 - j0], F32, kib)
-            for j0, j1, kib in zip(meas_cuts, meas_cuts[1:], (0, 17, 25))
+            for j0, j1, kib in zip(meas_cuts, meas_cuts[1:], (0, 2, 17, 25))
         ]
         keep_cuts = [0, 2 * P, 4 * P, N]
         keep_sb = [
@@ -115,27 +115,39 @@ def tile_list_sparse_code_step_kernel(
                 out=w1_raw[a][:], in_=w1[PASS * a : PASS * (a + 1), :].rearrange("(p i) c -> p i c", i=PACK)
             )
 
-        def carry_scale_rows(a, r):
+        def carry_scale_rows(a, r, cols):
             nc.sync.dma_start(
-                out=v_s[a][4 * a + r : P : 32, :].bitcast(I32),
-                in_=v_flat[FLAT + 16 * a + r : FLAT + 16 * a + 16 : 4, :].bitcast(I32),
+                out=v_s[a][4 * a + r : P : 32, cols].bitcast(I32),
+                in_=v_flat[FLAT + 16 * a + r : FLAT + 16 * a + 16 : 4, cols].bitcast(I32),
             )
+
+        def load_wt_scales(cols):
+            for q in range(QUADRANTS):
+                nc.sync.dma_start(out=wt_s[q:P:32, cols].bitcast(I32), in_=wt_scales[0, q::4, cols].bitcast(I32))
+
+        def load_keep_scales(cols):
+            for q in range(QUADRANTS):
+                nc.sync.dma_start(
+                    out=keep_s[32 * q : 32 * q + 8, cols].bitcast(I32),
+                    in_=keep_scales[:, 4 * q : 4 * q + 4, cols].bitcast(I32),
+                )
+
+        first_half, second_half = slice(0, HALF), slice(HALF, S)
 
         nc.sync.dma_start(out=tab_s[FLAT:P, :].bitcast(I32), in_=tab_scales.rearrange("a q t -> (a q) t").bitcast(I32))
         nc.sync.dma_start(pick[:], offs)
         load_table(0)
         nc.sync.dma_start(place[:], offs2)
-        for q in range(QUADRANTS):
-            nc.sync.dma_start(out=wt_s[q:P:32, :].bitcast(I32), in_=wt_scales[0, q::4, :].bitcast(I32))
+        load_wt_scales(first_half)
         load_w1(0)
         load_w1(1)
         nc.vector.tensor_copy(v_flat[:], tab_s[:].indirect(pick[:]))
         carries = [(0, 0), (1, 0), (0, 1), (1, 1), (0, 2), (0, 3), (1, 2), (1, 3)]
         for a, r in carries[:6]:
-            carry_scale_rows(a, r)
+            carry_scale_rows(a, r, first_half)
         load_table(1)
         for a, r in carries[6:]:
-            carry_scale_rows(a, r)
+            carry_scale_rows(a, r, first_half)
 
         w1_w = [held.tile([P, M], U32, name=f"w1_w{a}", align_bytes=64) for a in range(PASSES)]
         w1_s = [held.tile([P, M], U8, name=f"w1_s{a}", align_bytes=64) for a in range(PASSES)]
@@ -205,24 +217,27 @@ def tile_list_sparse_code_step_kernel(
         gather_words(0, 0, HALF)
         gather_words(0, HALF, S)
         load_meas(0)
+        load_meas(1)
         nc.gpsimd.memset(keep_s[:].bitcast(I32), 0)
-        for q in range(QUADRANTS):
-            nc.sync.dma_start(
-                out=keep_s[32 * q : 32 * q + 8, :].bitcast(I32), in_=keep_scales[:, 4 * q : 4 * q + 4, :].bitcast(I32)
-            )
+        load_keep_scales(first_half)
         load_keep(0)
         load_wt(0)
         load_wgo(0)
         quantize_w1(0, scalar_rows=0)
         quantize_w1(1, scalar_rows=0)
         load_keep(1)
-        load_meas(1)
+        load_meas(2)
+        load_wt_scales(second_half)
+        load_keep_scales(second_half)
         load_wt(1)
         load_keep(2)
-        load_meas(2)
+        for a, r in carries:
+            carry_scale_rows(a, r, second_half)
+        load_meas(3)
         windows.append(placed("window2", [P, T2], F32, 37))
         nc.gpsimd.memset(windows[2][:], 0.0)
-        gather_words(1, 0, QUARTER)
+        gather_words(1, 0, SUB)
+        gather_words(1, SUB, QUARTER)
         gather_words(1, QUARTER, HALF)
 
         def residual_on_vector(j0, bank):

@@ -76,11 +76,14 @@ def tile_list_sparse_code_step_kernel(
         neg_thr = held.tile([P, BLOCKS], F32, name="neg_thr")
         windows = [held.tile([P, T2], F32, name=f"window{i}") for i in range(EARLY_WINDOWS)]
 
-        nc.vector.memset(wt_s[:].bitcast(I32), 0)
-        for plane in v_s:
-            nc.vector.memset(plane[:].bitcast(I32), 0)
-        nc.vector.memset(windows[0][:, 0 : VECTOR_ZEROES - 1], 0.0)
-        nc.vector.memset(windows[0][:, VECTOR_ZEROES - 1 : VECTOR_ZEROES], 0.0)
+        def zero_on_vector(words):
+            count = words.shape[1]
+            nc.vector.memset(words[:, 0 : count - 1], 0)
+            nc.vector.memset(words[:, count - 1 : count], 0)
+
+        for plane in [wt_s] + v_s:
+            zero_on_vector(plane[:].bitcast(I32))
+        zero_on_vector(windows[0][:, 0:VECTOR_ZEROES])
         nc.gpsimd.memset(tab_s[0:FLAT, :].bitcast(I32), 0)
         nc.gpsimd.memset(thr_rows[:], 0.0)
         nc.gpsimd.dma_start(out=thr_rows[0:BLOCKS, :], in_=thr.rearrange("(b p) -> b p", p=P))

@@ -84,9 +84,8 @@ def tile_list_sparse_code_step_kernel(
         for plane in [wt_s] + v_s:
             zero_on_vector(plane[:].bitcast(I32))
         zero_on_vector(windows[0][:, 0:VECTOR_ZEROES])
-        nc.gpsimd.memset(tab_s[0:FLAT, :].bitcast(I32), 0)
         nc.gpsimd.memset(thr_rows[:], 0.0)
-        nc.gpsimd.dma_start(out=thr_rows[0:BLOCKS, :], in_=thr.rearrange("(b p) -> b p", p=P))
+        nc.gpsimd.memset(tab_s[0:FLAT, :].bitcast(I32), 0)
         make_identity(nc, ident[:])
         nc.gpsimd.memset(windows[0][:, VECTOR_ZEROES:T2], 0.0)
         nc.gpsimd.memset(windows[1][:], 0.0)
@@ -139,18 +138,20 @@ def tile_list_sparse_code_step_kernel(
 
         nc.sync.dma_start(out=tab_s[FLAT:P, :].bitcast(I32), in_=tab_scales.rearrange("a q t -> (a q) t").bitcast(I32))
         nc.sync.dma_start(pick[:], offs)
+        nc.sync.dma_start(out=thr_rows[0:BLOCKS, :], in_=thr.rearrange("(b p) -> b p", p=P))
         load_table(0)
-        nc.sync.dma_start(place[:], offs2)
         load_wt_scales(first_half)
         load_w1(0)
+        nc.sync.dma_start(place[:], offs2)
+        for j0 in (0, HALF):
+            nc.vector.tensor_copy(v_flat[:, j0 : j0 + HALF], tab_s[:].indirect(pick[:, j0 // 16 : (j0 + HALF) // 16]))
+        carries = [(a, r) for a in range(PASSES) for r in range(4)]
+        for a, r in carries[:4]:
+            carry_scale_rows(a, r, first_half)
         load_w1(1)
-        nc.vector.tensor_copy(v_flat[:], tab_s[:].indirect(pick[:]))
-        carries = [(0, 0), (1, 0), (0, 1), (1, 1), (0, 2), (0, 3), (1, 2), (1, 3)]
-        for a, r in carries[:6]:
+        for a, r in carries[4:]:
             carry_scale_rows(a, r, first_half)
         load_table(1)
-        for a, r in carries[6:]:
-            carry_scale_rows(a, r, first_half)
 
         w1_w = [held.tile([P, M], U32, name=f"w1_w{a}", align_bytes=64) for a in range(PASSES)]
         w1_s = [held.tile([P, M], U8, name=f"w1_s{a}", align_bytes=64) for a in range(PASSES)]

@@ -373,7 +373,8 @@ def tile_list_sparse_code_step_kernel(
             )
         ]
         predict_turned(QUARTER, next_bank())
-        steps = steps[1:]
+        predict_turned(QUARTER + SUB, next_bank())
+        steps = steps[2:]
 
         for q0, blocks in ((0, BLOCKS), (QUARTER, BLOCKS), (HALF, BLOCKS // 2)):
             q1 = q0 + QUARTER
@@ -384,9 +385,9 @@ def tile_list_sparse_code_step_kernel(
                 if b == blocks - 2:
                     sum_turned(q1 + SUB, used[-1])
                     quantize_h(q1, q1 + QUARTER)
-                elif steps:
+                elif steps and (q0, b) != (0, 0):
                     step, j0 = steps[0]
-                    step(j0, used[-1] if (q0, b) == (0, 0) else next_bank())
+                    step(j0, next_bank())
                     steps = steps[1:]
 
         for b in range(BLOCKS // 2):

@@ -28,9 +28,9 @@ HALF = S // 2
 QUARTER = S // 4
 SUB = 128
 BLOCKS = N // P
-EARLY_WINDOWS = 2
 VECTOR_ZEROES = 1024
 FLAT = 96
+BRIDGES = 3
 
 
 def tile_list_sparse_code_step_kernel(
@@ -41,7 +41,6 @@ def tile_list_sparse_code_step_kernel(
         held = ctx.enter_context(tc.tile_pool(name="held", bufs=1))
         psum = ctx.enter_context(tc.psum_pool(name="psum", bufs=1))
         banks = [psum.tile([P, BANK], F32, name=f"bank{i}") for i in range(BANKS)]
-
         shared = ctx.enter_context(tc.tile_pool(name="shared", bufs=1))
 
         def placed(name, shape, dtype, kib):
@@ -54,10 +53,10 @@ def tile_list_sparse_code_step_kernel(
         keep_s = placed("keep_s", [P, N], U8, 8)
         w1_raw = [placed(f"w1_raw{a}", [P, PACK, M], F32, 17 + 8 * a) for a in range(PASSES)]
         w1_grouped = [placed(f"w1_grouped{a}", [P, PACK, P, PACK], BF16, 33 + 4 * a) for a in range(PASSES)]
-        meas_cuts = [0, SUB, QUARTER, HALF, S]
+        meas_cuts = [0, SUB, QUARTER, HALF, HALF + QUARTER, S]
         meas_sb = [
             placed(f"meas{j0}", [P, PACK, j1 - j0], F32, kib)
-            for j0, j1, kib in zip(meas_cuts, meas_cuts[1:], (0, 2, 17, 25))
+            for j0, j1, kib in zip(meas_cuts, meas_cuts[1:], (0, 2, 17, 25, 29))
         ]
         keep_cuts = [0, 2 * P, 4 * P, N]
         keep_sb = [
@@ -74,7 +73,7 @@ def tile_list_sparse_code_step_kernel(
         thr_rows = held.tile([P, P], F32, name="thr_rows")
         ident = held.tile([P, P], F32, name="ident")
         neg_thr = held.tile([P, BLOCKS], F32, name="neg_thr")
-        windows = [held.tile([P, T2], F32, name=f"window{i}") for i in range(EARLY_WINDOWS)]
+        windows = [held.tile([P, T2], F32, name=f"window{i}") for i in range(3)]
 
         def zero_on_vector(words):
             count = words.shape[1]
@@ -89,6 +88,7 @@ def tile_list_sparse_code_step_kernel(
         make_identity(nc, ident[:])
         nc.gpsimd.memset(windows[0][:, VECTOR_ZEROES:T2], 0.0)
         nc.gpsimd.memset(windows[1][:], 0.0)
+        nc.gpsimd.memset(windows[2][:], 0.0)
 
         keep_view = keep_words.rearrange("a p c i -> p a (c i)")
         meas_view = meas.rearrange("(p t) j -> p t j", t=PACK)
@@ -140,7 +140,7 @@ def tile_list_sparse_code_step_kernel(
         nc.sync.dma_start(pick[:], offs)
         nc.sync.dma_start(out=thr_rows[0:BLOCKS, :], in_=thr.rearrange("(b p) -> b p", p=P))
         load_table(0)
-        load_wt_scales(first_half)
+        load_wt_scales(slice(0, N))
         load_w1(0)
         nc.sync.dma_start(place[:], offs2)
         for j0 in (0, HALF):
@@ -150,7 +150,7 @@ def tile_list_sparse_code_step_kernel(
             carry_scale_rows(a, r, first_half)
         load_w1(1)
         for a, r in carries[4:]:
-            carry_scale_rows(a, r, first_half)
+            carry_scale_rows(a, r, slice(0, S))
         load_table(1)
 
         w1_w = [held.tile([P, M], U32, name=f"w1_w{a}", align_bytes=64) for a in range(PASSES)]
@@ -160,30 +160,33 @@ def tile_list_sparse_code_step_kernel(
             (0, 1): held.tile([P, HALF], U32, name="v_w01", align_bytes=64),
             (1, 0): held.tile([P, HALF], U32, name="v_w10", align_bytes=64),
         }
-        h_cuts = [0, SUB] + list(range(QUARTER, S + 1, QUARTER))
+        h_cuts = [0, SUB, QUARTER, HALF, S]
         h_grouped = [
             held.tile([P, (j1 - j0) * PACK], BF16, name=f"h_grouped{u}", tag=f"h_grouped{u}", align_bytes=64)
             for u, (j0, j1) in enumerate(zip(h_cuts, h_cuts[1:]))
         ]
         h_w = held.tile([P, S], U32, name="h_w", align_bytes=64)
         h_s = held.tile([P, S], U8, name="h_s", align_bytes=64)
-        meas_turneds = {j0: held.tile([P, M], F32, name=f"meas_turned{j0}") for j0 in range(QUARTER, S, SUB)}
-        neg_preds = {j0: held.tile([P, M], F32, name=f"neg_pred{j0}") for j0 in range(QUARTER, S, SUB)}
+        neg_preds = {
+            (q0, u): held.tile([P, BANK], F32, name=f"neg_pred{q0}_{u}")
+            for q0 in range(QUARTER, S, QUARTER)
+            for u in range(2)
+        }
+        h_turneds = {j0: held.tile([P, M], BF16, name=f"h_turned{j0}") for j0 in range(QUARTER, S, SUB)}
 
-        def group_w1(a, grouped, t0, t1, r0, r1, copy):
+        def group_w1(a, t0, t1, copy):
             copy(
-                out=grouped[:, t0:t1, r0:r1, :].rearrange("p t r i -> p r t i"),
-                in_=w1_raw[a][:].rearrange("p i (r t) -> p r t i", t=PACK)[:, r0:r1, t0:t1, :],
+                out=w1_grouped[a][:, t0:t1, :, :].rearrange("p t r i -> p r t i"),
+                in_=w1_raw[a][:].rearrange("p i (r t) -> p r t i", t=PACK)[:, :, t0:t1, :],
             )
 
-        def quantize_w1(a, scalar_rows):
-            grouped = w1_grouped[a]
-            group_w1(a, grouped, 0, PACK // 2, 0, P, nc.scalar.copy)
-            if scalar_rows:
-                group_w1(a, grouped, PACK // 2, PACK, 0, scalar_rows, nc.scalar.copy)
-            group_w1(a, grouped, PACK // 2, PACK, scalar_rows, P, nc.vector.tensor_copy)
+        def quantize_w1(a):
+            group_w1(a, 0, PACK // 2, nc.scalar.copy)
+            group_w1(a, PACK // 2, PACK, nc.vector.tensor_copy)
             nc.vector.quantize_mx(
-                out=w1_w[a][:].bitcast(FP8X4), scales=w1_s[a][:], in_=grouped[:].rearrange("p t r i -> p (t r i)")
+                out=w1_w[a][:].bitcast(FP8X4),
+                scales=w1_s[a][:],
+                in_=w1_grouped[a][:].rearrange("p t r i -> p (t r i)"),
             )
 
         def v_cols(a, j0, j1):
@@ -227,83 +230,106 @@ def tile_list_sparse_code_step_kernel(
         load_keep(0)
         load_wt(0)
         load_wgo(0)
-        quantize_w1(0, scalar_rows=0)
-        quantize_w1(1, scalar_rows=0)
+        quantize_w1(0)
+        quantize_w1(1)
         load_keep(1)
         load_meas(2)
-        load_wt_scales(second_half)
         load_keep_scales(second_half)
         load_wt(1)
         load_keep(2)
-        for a, r in carries:
+        for a, r in carries[:4]:
             carry_scale_rows(a, r, second_half)
         load_meas(3)
-        windows.append(placed("window2", [P, T2], F32, 37))
-        nc.gpsimd.memset(windows[2][:], 0.0)
+        load_meas(4)
+        windows.append(placed("window3", [P, T2], F32, 37))
+        nc.gpsimd.memset(windows[3][:], 0.0)
         gather_words(1, 0, SUB)
         gather_words(1, SUB, QUARTER)
         gather_words(1, QUARTER, HALF)
 
-        def residual_on_vector(j0, bank):
-            pred = banks[bank]
+        used = []
+
+        def next_bank():
+            used.append(len(used) % BANKS)
+            return banks[used[-1]]
+
+        def predict(bank, j0, j1, t0, t1):
+            width = j1 - j0
             for a in range(PASSES):
-                for t in range(PACK):
+                for t in range(t0, t1):
                     ms = slice(t * P, (t + 1) * P)
                     nc.tensor.matmul_mx(
-                        out=pred[:, ms],
+                        out=bank[:, (t - t0) * width : (t - t0 + 1) * width],
                         lhsT=w1_w[a][:, ms].bitcast(FP8X4),
                         lhsT_scale=w1_s[a][:, ms],
-                        rhs=v_cols(a, j0, j0 + SUB).bitcast(FP8X4),
-                        rhs_scale=v_s[a][4 * a :, j0 : j0 + SUB],
-                        start=(a == 0 and t == 0),
-                        stop=(a == PASSES - 1 and t == PACK - 1),
+                        rhs=v_cols(a, j0, j1).bitcast(FP8X4),
+                        rhs_scale=v_s[a][4 * a :, j0:j1],
+                        start=(a == 0 and t == t0),
+                        stop=(a == PASSES - 1 and t == t1 - 1),
                     )
+
+        def residual_on_vector(j0):
+            bank = next_bank()
+            predict(bank, j0, j0 + SUB, 0, PACK)
             nc.vector.tensor_tensor(
                 h_cols(j0, j0 + SUB).rearrange("p (c e t) -> p c t e", e=2, t=PACK),
                 meas_cols(j0, j0 + SUB).rearrange("p t (c e) -> p c t e", e=2),
-                pred[:].rearrange("p (t c e) -> p c t e", t=PACK, e=2),
+                bank[:].rearrange("p (t c e) -> p c t e", t=PACK, e=2),
                 ALU.subtract,
             )
 
-        def predict_turned(j0, bank):
-            for a in range(PASSES):
-                nc.tensor.matmul_mx(
-                    out=banks[bank][:],
-                    lhsT=v_cols(a, j0, j0 + SUB).bitcast(FP8X4),
-                    lhsT_scale=v_s[a][4 * a :, j0 : j0 + SUB],
-                    rhs=w1_w[a][:].bitcast(FP8X4),
-                    rhs_scale=w1_s[a][:],
-                    start=(a == 0),
-                    stop=(a == PASSES - 1),
+        def predict_out(q0):
+            for u in range(2):
+                bank = next_bank()
+                predict(bank, q0, q0 + QUARTER, 2 * u, 2 * u + 2)
+                nc.scalar.mul(neg_preds[q0, u][:], bank[:], -1.0)
+            return bank
+
+        def sum_turned(j0):
+            bank = next_bank()
+            q0 = j0 - j0 % QUARTER
+            terms = [meas_cols(j0, j0 + SUB)[:, t, :] for t in range(PACK)] + [
+                neg_preds[q0, t // 2][:, (t % 2) * QUARTER + j0 - q0 : (t % 2) * QUARTER + j0 - q0 + SUB]
+                for t in range(PACK)
+            ]
+            for u, term in enumerate(terms):
+                t = u % PACK
+                nc.tensor.matmul(
+                    bank[:, t * P : (t + 1) * P],
+                    term,
+                    ident[:],
+                    is_transpose=True,
+                    start=(u == 0),
+                    stop=(u == len(terms) - 1),
                 )
-            nc.scalar.mul(neg_preds[j0][:], banks[bank][:], -1.0)
-
-        def turn_meas(j0, bank):
-            for t in range(PACK):
-                nc.tensor.transpose(banks[bank][:, t * P : (t + 1) * P], meas_cols(j0, j0 + SUB)[:, t, :], ident[:])
-            nc.scalar.copy(meas_turneds[j0][:], banks[bank][:])
-
-        def sum_turned(j0, bank):
-            for term, tile in enumerate((meas_turneds[j0], neg_preds[j0])):
-                for t in range(PACK):
-                    ms = slice(t * P, (t + 1) * P)
-                    nc.tensor.matmul(
-                        banks[bank][:, ms],
-                        tile[:, ms],
-                        ident[:],
-                        is_transpose=True,
-                        start=(term == 0 and t == 0),
-                        stop=(term == 1 and t == PACK - 1),
-                    )
             nc.scalar.copy(
-                h_cols(j0, j0 + SUB).rearrange("p (j t) -> p j t", t=PACK),
-                banks[bank][:].rearrange("p (t j) -> p j t", t=PACK),
+                h_turneds[j0][:].rearrange("j (u p e) -> j u p e", u=2, e=2),
+                bank[:].rearrange("j (u e p) -> j u p e", u=2, e=2),
             )
+            return bank
 
-        def put(b, j0, j1, bank, keep_first=False):
+        def turn_back(q0, bank=None):
+            bank = bank or next_bank()
+            for s in range(2):
+                pairs = h_turneds[q0 + s * SUB][:].bitcast(F32)
+                for u in range(2):
+                    nc.tensor.transpose(bank[:, (2 * s + u) * P : (2 * s + u + 1) * P], pairs[:, u * P : (u + 1) * P], ident[:])
+            nc.scalar.copy(
+                h_cols(q0, q0 + QUARTER).bitcast(F32).rearrange("p (s j u) -> p s j u", s=2, u=2),
+                bank[:].rearrange("p (s u j) -> p s j u", s=2, u=2),
+            )
+            return bank
+
+        ys = {}
+
+        def y_tile(b, j0, j1):
+            ys[b, j0] = held.tile([P, j1 - j0], F32, name=f"y{b}_{j0}", tag=f"y{b}_{j0}", align_bytes=64)
+            return ys[b, j0]
+
+        def shrink(b, j0, j1, y, bank, keep_first=False, wt_width=None):
             ns = slice(b * P, (b + 1) * P)
             width = j1 - j0
-            wt_width = BANK if width == BANK else SUB
+            wt_width = wt_width or width
             keep_passes = [
                 (0, width, keep_cols(a, b).bitcast(FP8X4), keep_s[4 * a :, ns], v_cols(a, j0, j1), v_s[a][4 * a :, j0:j1])
                 for a in reversed(range(PASSES))
@@ -322,7 +348,7 @@ def tile_list_sparse_code_step_kernel(
             passes = keep_passes + wt_passes if keep_first else wt_passes + keep_passes
             for u, (c0, c1, lhs, lhs_scale, rhs, rhs_scale) in enumerate(passes):
                 nc.tensor.matmul_mx(
-                    out=banks[bank][:, c0:c1],
+                    out=bank[:, c0:c1],
                     lhsT=lhs,
                     lhsT_scale=lhs_scale,
                     rhs=rhs.bitcast(FP8X4),
@@ -330,10 +356,11 @@ def tile_list_sparse_code_step_kernel(
                     start=(u == 0),
                     stop=(u == len(passes) - 1),
                 )
-            y = held.tile([P, width], F32, name=f"y{b}_{j0}", tag=f"y{b}_{j0}", align_bytes=64)
-            nc.scalar.activation(y[:], banks[bank][:, 0:width], ACT.Relu, bias=neg_thr[:, b : b + 1])
+            nc.scalar.activation(y, bank[:, 0:width], ACT.Relu, bias=neg_thr[:, b : b + 1])
+
+        def scatter(b, j0, j1):
             nc.vector.tensor_tensor(
-                windows[b][:].indirect(place[:, j0 // 16 : j1 // 16]), y[:], wgo_cols(j0, j1), ALU.mult
+                windows[b][:].indirect(place[:, j0 // 16 : j1 // 16]), ys[b, j0][:], wgo_cols(j0, j1), ALU.mult
             )
             if j1 == S:
                 nc.sync.dma_start(out=out[b * P : (b + 1) * P, :], in_=windows[b][:])
@@ -343,17 +370,17 @@ def tile_list_sparse_code_step_kernel(
             nc.gpsimd.memset(window[:], 0.0)
             windows.append(window)
 
-        used = []
+        def put(b, j0, j1, bank=None, keep_first=False, wt_width=None):
+            shrink(b, j0, j1, y_tile(b, j0, j1)[:], bank or next_bank(), keep_first, wt_width)
+            scatter(b, j0, j1)
+            if len(windows) < BLOCKS:
+                zero_window(f"y{b}_0")
 
-        def next_bank():
-            used.append(len(used) % BANKS)
-            return used[-1]
-
-        first_entries = range(0, QUARTER, SUB)
-        for j0 in first_entries:
-            residual_on_vector(j0, next_bank())
-        for j0 in first_entries:
-            quantize_h(j0, j0 + SUB)
+        q1, q2, q3 = QUARTER, HALF, HALF + QUARTER
+        residual_on_vector(0)
+        residual_on_vector(SUB)
+        quantize_h(0, SUB)
+        quantize_h(SUB, q1)
         nc.tensor.transpose(banks[0][:, 0:P], thr_rows[:], ident[:])
         nc.scalar.mul(neg_thr[:], banks[0][:, 0:BLOCKS], -1.0)
         v_w[1, 1] = held.tile([P, HALF], U32, name="v_w11", tag="h_grouped0", align_bytes=64)
@@ -361,35 +388,38 @@ def tile_list_sparse_code_step_kernel(
         load_wgo(1)
         zero_window("h_grouped1")
 
-        steps = [
-            (step, j0)
-            for q0 in range(QUARTER, S, QUARTER)
-            for step, j0 in (
-                (predict_turned, q0),
-                (predict_turned, q0 + SUB),
-                (turn_meas, q0),
-                (turn_meas, q0 + SUB),
-                (sum_turned, q0),
-            )
-        ]
-        predict_turned(QUARTER, next_bank())
-        predict_turned(QUARTER + SUB, next_bank())
-        steps = steps[2:]
+        predict_out(q1)
+        put(0, 0, q1, keep_first=True, wt_width=SUB)
+        for b in range(1, 4):
+            put(b, 0, q1)
+        sum_turned(q1)
+        sum_turned(q1 + SUB)
+        put(4, 0, q1)
+        seventh = next_bank()
+        put(5, 0, q1, bank=seventh)
+        turn_back(q1, seventh)
+        quantize_h(q1, q2)
+        put(6, 0, q1, bank=seventh)
+        put(7, 0, q1, bank=seventh)
+        predict_out(q2)
+        sum_turned(q2)
+        sum_turned(q2 + SUB)
+        predicted = predict_out(q3)
+        put(0, q1, q2, bank=predicted)
+        turned = turn_back(q2)
+        sum_turned(q3)
+        put(1, q1, q2, bank=turned)
+        summed = sum_turned(q3 + SUB)
+        last = turn_back(q3)
+        quantize_h(q2, S)
+        put(2, q1, q2, bank=last)
 
-        for q0, blocks in ((0, BLOCKS), (QUARTER, BLOCKS), (HALF, BLOCKS // 2)):
-            q1 = q0 + QUARTER
-            for b in range(blocks):
-                put(b, q0, q1, used[-1] if b == blocks - 1 else next_bank(), keep_first=(b == 0))
-                if len(windows) < BLOCKS:
-                    zero_window(f"y{b}_0")
-                if b == blocks - 2:
-                    sum_turned(q1 + SUB, used[-1])
-                    quantize_h(q1, q1 + QUARTER)
-                elif steps and (q0, b) != (0, 0):
-                    step, j0 = steps[0]
-                    step(j0, next_bank())
-                    steps = steps[1:]
-
-        for b in range(BLOCKS // 2):
-            put(b, S - QUARTER, S, next_bank(), keep_first=True)
-            put(BLOCKS // 2 + b, HALF, S, next_bank())
+        put(0, q2, S, bank=seventh, keep_first=True)
+        others = [bank for bank in banks if bank is not summed and bank is not last and bank is not seventh]
+        for b in range(BRIDGES, BLOCKS):
+            y = y_tile(b, q1, S)
+            shrink(b, q2, S, y[:, QUARTER:], others[b % len(others)])
+            shrink(b, q1, q2, y[:, 0:QUARTER], summed)
+            scatter(b, q1, S)
+            if b - BRIDGES + 1 < BRIDGES:
+                put(b - BRIDGES + 1, q2, S, bank=last)

@@ -30,7 +30,7 @@ SUB = 128
 BLOCKS = N // P
 VECTOR_ZEROES = 1024
 FLAT = 96
-BRIDGES = 3
+BRIDGES = 4
 
 
 def tile_list_sparse_code_step_kernel(
@@ -160,7 +160,7 @@ def tile_list_sparse_code_step_kernel(
             (0, 1): held.tile([P, HALF], U32, name="v_w01", align_bytes=64),
             (1, 0): held.tile([P, HALF], U32, name="v_w10", align_bytes=64),
         }
-        h_cuts = [0, SUB, QUARTER, HALF, S]
+        h_cuts = [0, SUB, QUARTER, HALF, HALF + QUARTER, S]
         h_grouped = [
             held.tile([P, (j1 - j0) * PACK], BF16, name=f"h_grouped{u}", tag=f"h_grouped{u}", align_bytes=64)
             for u, (j0, j1) in enumerate(zip(h_cuts, h_cuts[1:]))
@@ -233,12 +233,12 @@ def tile_list_sparse_code_step_kernel(
         quantize_w1(0)
         quantize_w1(1)
         load_keep(1)
+        for a, r in carries[:4]:
+            carry_scale_rows(a, r, second_half)
         load_meas(2)
         load_keep_scales(second_half)
         load_wt(1)
         load_keep(2)
-        for a, r in carries[:4]:
-            carry_scale_rows(a, r, second_half)
         load_meas(3)
         load_meas(4)
         windows.append(placed("window3", [P, T2], F32, 37))
@@ -246,12 +246,6 @@ def tile_list_sparse_code_step_kernel(
         gather_words(1, 0, SUB)
         gather_words(1, SUB, QUARTER)
         gather_words(1, QUARTER, HALF)
-
-        used = []
-
-        def next_bank():
-            used.append(len(used) % BANKS)
-            return banks[used[-1]]
 
         def predict(bank, j0, j1, t0, t1):
             width = j1 - j0
@@ -268,8 +262,7 @@ def tile_list_sparse_code_step_kernel(
                         stop=(a == PASSES - 1 and t == t1 - 1),
                     )
 
-        def residual_on_vector(j0):
-            bank = next_bank()
+        def residual_on_vector(j0, bank):
             predict(bank, j0, j0 + SUB, 0, PACK)
             nc.vector.tensor_tensor(
                 h_cols(j0, j0 + SUB).rearrange("p (c e t) -> p c t e", e=2, t=PACK),
@@ -278,15 +271,12 @@ def tile_list_sparse_code_step_kernel(
                 ALU.subtract,
             )
 
-        def predict_out(q0):
-            for u in range(2):
-                bank = next_bank()
+        def predict_out(q0, pair):
+            for u, bank in enumerate(pair):
                 predict(bank, q0, q0 + QUARTER, 2 * u, 2 * u + 2)
                 nc.scalar.mul(neg_preds[q0, u][:], bank[:], -1.0)
-            return bank
 
-        def sum_turned(j0):
-            bank = next_bank()
+        def sum_turned(j0, bank):
             q0 = j0 - j0 % QUARTER
             terms = [meas_cols(j0, j0 + SUB)[:, t, :] for t in range(PACK)] + [
                 neg_preds[q0, t // 2][:, (t % 2) * QUARTER + j0 - q0 : (t % 2) * QUARTER + j0 - q0 + SUB]
@@ -306,10 +296,8 @@ def tile_list_sparse_code_step_kernel(
                 h_turneds[j0][:].rearrange("j (u p e) -> j u p e", u=2, e=2),
                 bank[:].rearrange("j (u e p) -> j u p e", u=2, e=2),
             )
-            return bank
 
-        def turn_back(q0, bank=None):
-            bank = bank or next_bank()
+        def turn_back(q0, bank):
             for s in range(2):
                 pairs = h_turneds[q0 + s * SUB][:].bitcast(F32)
                 for u in range(2):
@@ -318,7 +306,6 @@ def tile_list_sparse_code_step_kernel(
                 h_cols(q0, q0 + QUARTER).bitcast(F32).rearrange("p (s j u) -> p s j u", s=2, u=2),
                 bank[:].rearrange("p (s u j) -> p s j u", s=2, u=2),
             )
-            return bank
 
         ys = {}
 
@@ -326,29 +313,18 @@ def tile_list_sparse_code_step_kernel(
             ys[b, j0] = held.tile([P, j1 - j0], F32, name=f"y{b}_{j0}", tag=f"y{b}_{j0}", align_bytes=64)
             return ys[b, j0]
 
-        def shrink(b, j0, j1, y, bank, keep_first=False, wt_width=None):
+        def shrink(b, j0, j1, y, bank, keep_first=False):
             ns = slice(b * P, (b + 1) * P)
             width = j1 - j0
-            wt_width = wt_width or width
             keep_passes = [
-                (0, width, keep_cols(a, b).bitcast(FP8X4), keep_s[4 * a :, ns], v_cols(a, j0, j1), v_s[a][4 * a :, j0:j1])
+                (keep_cols(a, b).bitcast(FP8X4), keep_s[4 * a :, ns], v_cols(a, j0, j1), v_s[a][4 * a :, j0:j1])
                 for a in reversed(range(PASSES))
             ]
-            wt_passes = [
-                (
-                    c0,
-                    c0 + wt_width,
-                    wt_cols(b).bitcast(FP4X4),
-                    wt_s[:, ns],
-                    h_w[:, j0 + c0 : j0 + c0 + wt_width],
-                    h_s[:, j0 + c0 : j0 + c0 + wt_width],
-                )
-                for c0 in range(0, width, wt_width)
-            ]
+            wt_passes = [(wt_cols(b).bitcast(FP4X4), wt_s[:, ns], h_w[:, j0:j1], h_s[:, j0:j1])]
             passes = keep_passes + wt_passes if keep_first else wt_passes + keep_passes
-            for u, (c0, c1, lhs, lhs_scale, rhs, rhs_scale) in enumerate(passes):
+            for u, (lhs, lhs_scale, rhs, rhs_scale) in enumerate(passes):
                 nc.tensor.matmul_mx(
-                    out=bank[:, c0:c1],
+                    out=bank[:, 0:width],
                     lhsT=lhs,
                     lhsT_scale=lhs_scale,
                     rhs=rhs.bitcast(FP8X4),
@@ -370,15 +346,15 @@ def tile_list_sparse_code_step_kernel(
             nc.gpsimd.memset(window[:], 0.0)
             windows.append(window)
 
-        def put(b, j0, j1, bank=None, keep_first=False, wt_width=None):
-            shrink(b, j0, j1, y_tile(b, j0, j1)[:], bank or next_bank(), keep_first, wt_width)
+        def put(b, j0, j1, bank):
+            shrink(b, j0, j1, y_tile(b, j0, j1)[:], bank)
             scatter(b, j0, j1)
             if len(windows) < BLOCKS:
                 zero_window(f"y{b}_0")
 
         q1, q2, q3 = QUARTER, HALF, HALF + QUARTER
-        residual_on_vector(0)
-        residual_on_vector(SUB)
+        residual_on_vector(0, banks[0])
+        residual_on_vector(SUB, banks[1])
         quantize_h(0, SUB)
         quantize_h(SUB, q1)
         nc.tensor.transpose(banks[0][:, 0:P], thr_rows[:], ident[:])
@@ -388,38 +364,47 @@ def tile_list_sparse_code_step_kernel(
         load_wgo(1)
         zero_window("h_grouped1")
 
-        predict_out(q1)
-        put(0, 0, q1, keep_first=True, wt_width=SUB)
-        for b in range(1, 4):
-            put(b, 0, q1)
-        sum_turned(q1)
-        sum_turned(q1 + SUB)
-        put(4, 0, q1)
-        seventh = next_bank()
-        put(5, 0, q1, bank=seventh)
-        turn_back(q1, seventh)
+        predict_out(q1, banks[2:4])
+        y = y_tile(0, 0, q1)
+        for j0, bank in ((0, banks[4]), (SUB, banks[5])):
+            shrink(0, j0, j0 + SUB, y[:, j0 : j0 + SUB], bank, keep_first=True)
+        scatter(0, 0, q1)
+        zero_window("y0_0")
+        put(1, 0, q1, banks[6])
+        put(2, 0, q1, banks[7])
+        put(3, 0, q1, banks[0])
+        sum_turned(q1, banks[1])
+        sum_turned(q1 + SUB, banks[2])
+        predict_out(q2, banks[3:5])
+        put(4, 0, q1, banks[5])
+        put(5, 0, q1, banks[6])
+        turn_back(q1, banks[6])
         quantize_h(q1, q2)
-        put(6, 0, q1, bank=seventh)
-        put(7, 0, q1, bank=seventh)
-        predict_out(q2)
-        sum_turned(q2)
-        sum_turned(q2 + SUB)
-        predicted = predict_out(q3)
-        put(0, q1, q2, bank=predicted)
-        turned = turn_back(q2)
-        sum_turned(q3)
-        put(1, q1, q2, bank=turned)
-        summed = sum_turned(q3 + SUB)
-        last = turn_back(q3)
-        quantize_h(q2, S)
-        put(2, q1, q2, bank=last)
+        put(6, 0, q1, banks[6])
+        put(7, 0, q1, banks[6])
+        sum_turned(q2, banks[7])
+        sum_turned(q2 + SUB, banks[0])
+        predict_out(q3, banks[1:3])
+        put(0, q1, q2, banks[0])
+        turn_back(q2, banks[3])
+        quantize_h(q2, q3)
+        sum_turned(q3, banks[4])
+        put(1, q1, q2, banks[3])
+        sum_turned(q3 + SUB, banks[5])
+        for b in range(2, BRIDGES - 1):
+            put(b, q1, q2, banks[4])
+        turn_back(q3, banks[7])
+        quantize_h(q3, S)
+        put(BRIDGES - 1, q1, q2, banks[7])
 
-        put(0, q2, S, bank=seventh, keep_first=True)
-        others = [bank for bank in banks if bank is not summed and bank is not last and bank is not seventh]
+        y = y_tile(0, q2, S)
+        shrink(0, q2, q3, y[:, 0:QUARTER], banks[5])
+        shrink(0, q3, S, y[:, QUARTER:], banks[6], keep_first=True)
+        scatter(0, q2, S)
         for b in range(BRIDGES, BLOCKS):
             y = y_tile(b, q1, S)
-            shrink(b, q2, S, y[:, QUARTER:], others[b % len(others)])
-            shrink(b, q1, q2, y[:, 0:QUARTER], summed)
+            shrink(b, q2, S, y[:, QUARTER:], banks[b % 4])
+            shrink(b, q1, q2, y[:, 0:QUARTER], banks[7])
             scatter(b, q1, S)
             if b - BRIDGES + 1 < BRIDGES:
-                put(b - BRIDGES + 1, q2, S, bank=last)
+                put(b - BRIDGES + 1, q2, S, banks[4 + b % 2])

@@ -138,8 +138,8 @@ def tile_list_sparse_code_step_kernel(
 
         nc.sync.dma_start(out=tab_s[FLAT:P, :].bitcast(I32), in_=tab_scales.rearrange("a q t -> (a q) t").bitcast(I32))
         nc.sync.dma_start(pick[:], offs)
-        nc.sync.dma_start(out=thr_rows[0:BLOCKS, :], in_=thr.rearrange("(b p) -> b p", p=P))
         load_table(0)
+        nc.sync.dma_start(out=thr_rows[0:BLOCKS, :], in_=thr.rearrange("(b p) -> b p", p=P))
         load_wt_scales(slice(0, N))
         load_w1(0)
         nc.sync.dma_start(place[:], offs2)
@@ -149,9 +149,11 @@ def tile_list_sparse_code_step_kernel(
         for a, r in carries[:4]:
             carry_scale_rows(a, r, first_half)
         load_w1(1)
-        for a, r in carries[4:]:
+        for a, r in carries[4:6]:
             carry_scale_rows(a, r, slice(0, S))
         load_table(1)
+        for a, r in carries[6:]:
+            carry_scale_rows(a, r, slice(0, S))
 
         w1_w = [held.tile([P, M], U32, name=f"w1_w{a}", align_bytes=64) for a in range(PASSES)]
         w1_s = [held.tile([P, M], U8, name=f"w1_s{a}", align_bytes=64) for a in range(PASSES)]
@@ -174,15 +176,17 @@ def tile_list_sparse_code_step_kernel(
         }
         h_turneds = {j0: held.tile([P, M], BF16, name=f"h_turned{j0}") for j0 in range(QUARTER, S, SUB)}
 
-        def group_w1(a, t0, t1, copy):
+        def group_w1(a, t0, t1, r0, r1, copy):
             copy(
-                out=w1_grouped[a][:, t0:t1, :, :].rearrange("p t r i -> p r t i"),
-                in_=w1_raw[a][:].rearrange("p i (r t) -> p r t i", t=PACK)[:, :, t0:t1, :],
+                out=w1_grouped[a][:, t0:t1, r0:r1, :].rearrange("p t r i -> p r t i"),
+                in_=w1_raw[a][:].rearrange("p i (r t) -> p r t i", t=PACK)[:, r0:r1, t0:t1, :],
             )
 
-        def quantize_w1(a):
-            group_w1(a, 0, PACK // 2, nc.scalar.copy)
-            group_w1(a, PACK // 2, PACK, nc.vector.tensor_copy)
+        def quantize_w1(a, scalar_rows):
+            group_w1(a, 0, PACK // 2, 0, scalar_rows, nc.scalar.copy)
+            group_w1(a, PACK // 2, PACK, 0, P, nc.vector.tensor_copy)
+            if scalar_rows < P:
+                group_w1(a, 0, PACK // 2, scalar_rows, P, nc.vector.tensor_copy)
             nc.vector.quantize_mx(
                 out=w1_w[a][:].bitcast(FP8X4),
                 scales=w1_s[a][:],
@@ -230,8 +234,8 @@ def tile_list_sparse_code_step_kernel(
         load_keep(0)
         load_wt(0)
         load_wgo(0)
-        quantize_w1(0)
-        quantize_w1(1)
+        quantize_w1(0, P)
+        quantize_w1(1, 3 * P // 4)
         load_keep(1)
         for a, r in carries[:4]:
             carry_scale_rows(a, r, second_half)

@@ -30,7 +30,7 @@ SUB = 128
 BLOCKS = N // P
 VECTOR_ZEROES = 1024
 FLAT = 96
-BRIDGES = 4
+BRIDGES = 5
 
 
 def tile_list_sparse_code_step_kernel(
@@ -58,10 +58,10 @@ def tile_list_sparse_code_step_kernel(
             placed(f"meas{j0}", [P, PACK, j1 - j0], F32, kib)
             for j0, j1, kib in zip(meas_cuts, meas_cuts[1:], (0, 2, 17, 25, 29))
         ]
-        keep_cuts = [0, 2 * P, 4 * P, N]
+        keep_cuts = [0, P, 2 * P, 4 * P, N]
         keep_sb = [
             placed(f"keep{n0}", [P, PASSES, n1 - n0], I32, kib)
-            for n0, n1, kib in zip(keep_cuts, keep_cuts[1:], (4, 21, 33))
+            for n0, n1, kib in zip(keep_cuts, keep_cuts[1:], (4, 5, 21, 33))
         ]
         wt_cuts = [0, N // 2, N]
         wt_sb = [placed(f"wt{n0}", [P, 2 * (n1 - n0)], U8, kib) for n0, n1, kib in zip(wt_cuts, wt_cuts[1:], (6, 23))]
@@ -234,15 +234,16 @@ def tile_list_sparse_code_step_kernel(
         load_keep(0)
         load_wt(0)
         load_wgo(0)
+        load_keep(1)
         quantize_w1(0, P)
         quantize_w1(1, 3 * P // 4)
-        load_keep(1)
+        load_keep(2)
         for a, r in carries[:4]:
             carry_scale_rows(a, r, second_half)
         load_meas(2)
         load_keep_scales(second_half)
         load_wt(1)
-        load_keep(2)
+        load_keep(3)
         load_meas(3)
         load_meas(4)
         windows.append(placed("window3", [P, T2], F32, 37))
@@ -377,26 +378,26 @@ def tile_list_sparse_code_step_kernel(
         put(1, 0, q1, banks[6])
         put(2, 0, q1, banks[7])
         put(3, 0, q1, banks[0])
-        sum_turned(q1, banks[1])
-        sum_turned(q1 + SUB, banks[2])
-        predict_out(q2, banks[3:5])
         put(4, 0, q1, banks[5])
         put(5, 0, q1, banks[6])
+        sum_turned(q1, banks[1])
+        sum_turned(q1 + SUB, banks[2])
         turn_back(q1, banks[6])
         quantize_h(q1, q2)
         put(6, 0, q1, banks[6])
         put(7, 0, q1, banks[6])
+        predict_out(q2, banks[3:5])
         sum_turned(q2, banks[7])
         sum_turned(q2 + SUB, banks[0])
-        predict_out(q3, banks[1:3])
         put(0, q1, q2, banks[0])
+        predict_out(q3, banks[1:3])
+        put(1, q1, q2, banks[0])
         turn_back(q2, banks[3])
         quantize_h(q2, q3)
         sum_turned(q3, banks[4])
-        put(1, q1, q2, banks[3])
+        put(2, q1, q2, banks[3])
         sum_turned(q3 + SUB, banks[5])
-        for b in range(2, BRIDGES - 1):
-            put(b, q1, q2, banks[4])
+        put(3, q1, q2, banks[4])
         turn_back(q3, banks[7])
         quantize_h(q3, S)
         put(BRIDGES - 1, q1, q2, banks[7])
@@ -410,5 +411,5 @@ def tile_list_sparse_code_step_kernel(
             shrink(b, q2, S, y[:, QUARTER:], banks[b % 4])
             shrink(b, q1, q2, y[:, 0:QUARTER], banks[7])
             scatter(b, q1, S)
-            if b - BRIDGES + 1 < BRIDGES:
-                put(b - BRIDGES + 1, q2, S, banks[4 + b % 2])
+            put(b - BRIDGES + 1, q2, S, banks[4 + b % 2])
+        put(BRIDGES - 1, q2, S, banks[4])

@@ -31,6 +31,7 @@ BLOCKS = N // P
 VECTOR_ZEROES = 1024
 FLAT = 96
 BRIDGES = 5
+LINE = 256
 
 
 def tile_list_sparse_code_step_kernel(
@@ -44,7 +45,7 @@ def tile_list_sparse_code_step_kernel(
         shared = ctx.enter_context(tc.tile_pool(name="shared", bufs=1))
 
         def placed(name, shape, dtype, kib):
-            return shared.tile(shape, dtype, name=name, offset=kib * 1024, align_bytes=64)
+            return shared.tile(shape, dtype, name=name, offset=kib * 1024, align_bytes=LINE)
 
         pick = held.tile([P, S // 16], U16, name="pick")
         place = held.tile([P, S // 16], U16, name="place")
@@ -67,13 +68,13 @@ def tile_list_sparse_code_step_kernel(
         wt_sb = [placed(f"wt{n0}", [P, 2 * (n1 - n0)], U8, kib) for n0, n1, kib in zip(wt_cuts, wt_cuts[1:], (6, 23))]
         wgo_cuts = [0, QUARTER, S]
         wgo_sb = [placed(f"wgo{j0}", [P, j1 - j0], F32, kib) for j0, j1, kib in zip(wgo_cuts, wgo_cuts[1:], (7, 10))]
-        wt_s = held.tile([P, N], U8, name="wt_s", align_bytes=64)
-        v_flat = held.tile([P, S], U8, name="v_flat", align_bytes=64)
-        v_s = [held.tile([P, S], U8, name=f"v_s{a}", align_bytes=64) for a in range(PASSES)]
-        thr_rows = held.tile([P, P], F32, name="thr_rows")
+        wt_s = held.tile([P, N], U8, name="wt_s", align_bytes=LINE)
+        v_flat = held.tile([P, S], U8, name="v_flat", align_bytes=LINE)
+        v_s = [held.tile([P, S], U8, name=f"v_s{a}", align_bytes=LINE) for a in range(PASSES)]
+        thr_rows = held.tile([P, P], F32, name="thr_rows", align_bytes=LINE)
         ident = held.tile([P, P], F32, name="ident")
         neg_thr = held.tile([P, BLOCKS], F32, name="neg_thr")
-        windows = [held.tile([P, T2], F32, name=f"window{i}") for i in range(3)]
+        windows = [held.tile([P, T2], F32, name=f"window{i}", align_bytes=LINE) for i in range(3)]
 
         def zero_on_vector(words):
             count = words.shape[1]
@@ -155,20 +156,20 @@ def tile_list_sparse_code_step_kernel(
         for a, r in carries[6:]:
             carry_scale_rows(a, r, slice(0, S))
 
-        w1_w = [held.tile([P, M], U32, name=f"w1_w{a}", align_bytes=64) for a in range(PASSES)]
-        w1_s = [held.tile([P, M], U8, name=f"w1_s{a}", align_bytes=64) for a in range(PASSES)]
+        w1_w = [held.tile([P, M], U32, name=f"w1_w{a}", align_bytes=LINE) for a in range(PASSES)]
+        w1_s = [held.tile([P, M], U8, name=f"w1_s{a}", align_bytes=LINE) for a in range(PASSES)]
         v_w = {
-            (0, 0): held.tile([P, HALF], U32, name="v_w00", align_bytes=64),
-            (0, 1): held.tile([P, HALF], U32, name="v_w01", align_bytes=64),
-            (1, 0): held.tile([P, HALF], U32, name="v_w10", align_bytes=64),
+            (0, 0): held.tile([P, HALF], U32, name="v_w00", align_bytes=LINE),
+            (0, 1): held.tile([P, HALF], U32, name="v_w01", align_bytes=LINE),
+            (1, 0): held.tile([P, HALF], U32, name="v_w10", align_bytes=LINE),
         }
         h_cuts = [0, SUB, QUARTER, HALF, HALF + QUARTER, S]
         h_grouped = [
-            held.tile([P, (j1 - j0) * PACK], BF16, name=f"h_grouped{u}", tag=f"h_grouped{u}", align_bytes=64)
+            held.tile([P, (j1 - j0) * PACK], BF16, name=f"h_grouped{u}", tag=f"h_grouped{u}", align_bytes=LINE)
             for u, (j0, j1) in enumerate(zip(h_cuts, h_cuts[1:]))
         ]
-        h_w = held.tile([P, S], U32, name="h_w", align_bytes=64)
-        h_s = held.tile([P, S], U8, name="h_s", align_bytes=64)
+        h_w = held.tile([P, S], U32, name="h_w", align_bytes=LINE)
+        h_s = held.tile([P, S], U8, name="h_s", align_bytes=LINE)
         neg_preds = {
             (q0, u): held.tile([P, BANK], F32, name=f"neg_pred{q0}_{u}")
             for q0 in range(QUARTER, S, QUARTER)
@@ -315,7 +316,7 @@ def tile_list_sparse_code_step_kernel(
         ys = {}
 
         def y_tile(b, j0, j1):
-            ys[b, j0] = held.tile([P, j1 - j0], F32, name=f"y{b}_{j0}", tag=f"y{b}_{j0}", align_bytes=64)
+            ys[b, j0] = held.tile([P, j1 - j0], F32, name=f"y{b}_{j0}", tag=f"y{b}_{j0}", align_bytes=LINE)
             return ys[b, j0]
 
         def shrink(b, j0, j1, y, bank, keep_first=False):
@@ -347,7 +348,7 @@ def tile_list_sparse_code_step_kernel(
                 nc.sync.dma_start(out=out[b * P : (b + 1) * P, :], in_=windows[b][:])
 
         def zero_window(after):
-            window = held.tile([P, T2], F32, name=f"window{len(windows)}", tag=after, align_bytes=64)
+            window = held.tile([P, T2], F32, name=f"window{len(windows)}", tag=after, align_bytes=LINE)
             nc.gpsimd.memset(window[:], 0.0)
             windows.append(window)
 
@@ -364,7 +365,7 @@ def tile_list_sparse_code_step_kernel(
         quantize_h(SUB, q1)
         nc.tensor.transpose(banks[0][:, 0:P], thr_rows[:], ident[:])
         nc.scalar.mul(neg_thr[:], banks[0][:, 0:BLOCKS], -1.0)
-        v_w[1, 1] = held.tile([P, HALF], U32, name="v_w11", tag="h_grouped0", align_bytes=64)
+        v_w[1, 1] = held.tile([P, HALF], U32, name="v_w11", tag="h_grouped0", align_bytes=LINE)
         gather_words(1, HALF, S)
         load_wgo(1)
         zero_window("h_grouped1")

@@ -29,6 +29,8 @@ QUARTER = S // 4
 SUB = 128
 BLOCKS = N // P
 VECTOR_ZEROES = 1024
+PLANE = 8
+THR_ROW = 16
 FLAT = 96
 BRIDGES = 5
 LINE = 256
@@ -120,7 +122,7 @@ def tile_list_sparse_code_step_kernel(
 
         def carry_scale_rows(a, r, cols):
             nc.sync.dma_start(
-                out=v_s[a][4 * a + r : P : 32, cols].bitcast(I32),
+                out=v_s[a][PLANE + 4 * a + r : P : 32, cols].bitcast(I32),
                 in_=v_flat[FLAT + 16 * a + r : FLAT + 16 * a + 16 : 4, cols].bitcast(I32),
             )
 
@@ -131,7 +133,7 @@ def tile_list_sparse_code_step_kernel(
         def load_keep_scales(cols):
             for q in range(QUADRANTS):
                 nc.sync.dma_start(
-                    out=keep_s[32 * q : 32 * q + 8, cols].bitcast(I32),
+                    out=keep_s[32 * q + PLANE : 32 * q + PLANE + 8, cols].bitcast(I32),
                     in_=keep_scales[:, 4 * q : 4 * q + 4, cols].bitcast(I32),
                 )
 
@@ -140,7 +142,7 @@ def tile_list_sparse_code_step_kernel(
         nc.sync.dma_start(out=tab_s[FLAT:P, :].bitcast(I32), in_=tab_scales.rearrange("a q t -> (a q) t").bitcast(I32))
         nc.sync.dma_start(pick[:], offs)
         load_table(0)
-        nc.sync.dma_start(out=thr_rows[0:BLOCKS, :], in_=thr.rearrange("(b p) -> b p", p=P))
+        nc.sync.dma_start(out=thr_rows[THR_ROW : THR_ROW + BLOCKS, :], in_=thr.rearrange("(b p) -> b p", p=P))
         load_wt_scales(slice(0, N))
         load_w1(0)
         nc.sync.dma_start(place[:], offs2)
@@ -263,7 +265,7 @@ def tile_list_sparse_code_step_kernel(
                         lhsT=w1_w[a][:, ms].bitcast(FP8X4),
                         lhsT_scale=w1_s[a][:, ms],
                         rhs=v_cols(a, j0, j1).bitcast(FP8X4),
-                        rhs_scale=v_s[a][4 * a :, j0:j1],
+                        rhs_scale=v_s[a][PLANE + 4 * a :, j0:j1],
                         start=(a == 0 and t == t0),
                         stop=(a == PASSES - 1 and t == t1 - 1),
                     )
@@ -323,7 +325,7 @@ def tile_list_sparse_code_step_kernel(
             ns = slice(b * P, (b + 1) * P)
             width = j1 - j0
             keep_passes = [
-                (keep_cols(a, b).bitcast(FP8X4), keep_s[4 * a :, ns], v_cols(a, j0, j1), v_s[a][4 * a :, j0:j1])
+                (keep_cols(a, b).bitcast(FP8X4), keep_s[PLANE + 4 * a :, ns], v_cols(a, j0, j1), v_s[a][PLANE + 4 * a :, j0:j1])
                 for a in reversed(range(PASSES))
             ]
             wt_passes = [(wt_cols(b).bitcast(FP4X4), wt_s[:, ns], h_w[:, j0:j1], h_s[:, j0:j1])]
@@ -364,7 +366,7 @@ def tile_list_sparse_code_step_kernel(
         quantize_h(0, SUB)
         quantize_h(SUB, q1)
         nc.tensor.transpose(banks[0][:, 0:P], thr_rows[:], ident[:])
-        nc.scalar.mul(neg_thr[:], banks[0][:, 0:BLOCKS], -1.0)
+        nc.scalar.mul(neg_thr[:], banks[0][:, THR_ROW : THR_ROW + BLOCKS], -1.0)
         v_w[1, 1] = held.tile([P, HALF], U32, name="v_w11", tag="h_grouped0", align_bytes=LINE)
         gather_words(1, HALF, S)
         load_wgo(1)

@@ -238,7 +238,7 @@ def tile_list_sparse_code_step_kernel(
         load_wt(0)
         load_wgo(0)
         load_keep(1)
-        quantize_w1(0, P)
+        quantize_w1(0, 3 * P // 4)
         quantize_w1(1, 3 * P // 4)
         load_keep(2)
         for a, r in carries[:4]:

from contextlib import ExitStack

import concourse.mybir as mybir
from concourse.masks import make_identity

K, T, S, M, N, T2 = 1024, 2048, 1024, 512, 1024, 2048
FLOPS = 2 * S * (K * M + K * N + M * N)

F32 = mybir.dt.float32
BF16 = mybir.dt.bfloat16
I32 = mybir.dt.int32
U32 = mybir.dt.uint32
U16 = mybir.dt.uint16
U8 = mybir.dt.uint8
FP8X4 = mybir.dt.float8_e4m3fn_x4
FP4X4 = mybir.dt.float4_e2m1fn_x4
ALU = mybir.AluOpType
ACT = mybir.ActivationFunctionType

P = 128
PACK = 4
PASS = P * PACK
PASSES = K // PASS
QUADRANTS = 4
BANK = 512
BANKS = 8
HALF = S // 2
QUARTER = S // 4
SUB = 128
BLOCKS = N // P
VECTOR_ZEROES = 1024
PLANE = 8
THR_ROW = 16
FLAT = 96
BRIDGES = 5
LINE = 256


def tile_list_sparse_code_step_kernel(
    tc, tab_words, tab_scales, offs, w1, meas, wt_words, wt_scales, keep_words, keep_scales, thr, wgo, offs2, out
):
    nc = tc.nc
    with ExitStack() as ctx:
        held = ctx.enter_context(tc.tile_pool(name="held", bufs=1))
        psum = ctx.enter_context(tc.psum_pool(name="psum", bufs=1))
        banks = [psum.tile([P, BANK], F32, name=f"bank{i}") for i in range(BANKS)]
        shared = ctx.enter_context(tc.tile_pool(name="shared", bufs=1))

        def placed(name, shape, dtype, kib):
            return shared.tile(shape, dtype, name=name, offset=kib * 1024, align_bytes=LINE)

        pick = held.tile([P, S // 16], U16, name="pick")
        place = held.tile([P, S // 16], U16, name="place")
        tab_w = [placed("tab_w0", [P, T], I32, 0), placed("tab_w1", [P, T], I32, 9)]
        tab_s = placed("tab_s", [P, T], U8, 8)
        keep_s = placed("keep_s", [P, N], U8, 8)
        w1_raw = [placed(f"w1_raw{a}", [P, PACK, M], F32, 17 + 8 * a) for a in range(PASSES)]
        w1_grouped = [placed(f"w1_grouped{a}", [P, PACK, P, PACK], BF16, 33 + 4 * a) for a in range(PASSES)]
        meas_cuts = [0, SUB, QUARTER, HALF, HALF + QUARTER, S]
        meas_sb = [
            placed(f"meas{j0}", [P, PACK, j1 - j0], F32, kib)
            for j0, j1, kib in zip(meas_cuts, meas_cuts[1:], (0, 2, 17, 25, 29))
        ]
        keep_cuts = [0, P, 2 * P, 4 * P, N]
        keep_sb = [
            placed(f"keep{n0}", [P, PASSES, n1 - n0], I32, kib)
            for n0, n1, kib in zip(keep_cuts, keep_cuts[1:], (4, 5, 21, 33))
        ]
        wt_cuts = [0, N // 2, N]
        wt_sb = [placed(f"wt{n0}", [P, 2 * (n1 - n0)], U8, kib) for n0, n1, kib in zip(wt_cuts, wt_cuts[1:], (6, 23))]
        wgo_cuts = [0, QUARTER, S]
        wgo_sb = [placed(f"wgo{j0}", [P, j1 - j0], F32, kib) for j0, j1, kib in zip(wgo_cuts, wgo_cuts[1:], (7, 10))]
        wt_s = held.tile([P, N], U8, name="wt_s", align_bytes=LINE)
        v_flat = held.tile([P, S], U8, name="v_flat", align_bytes=LINE)
        v_s = [held.tile([P, S], U8, name=f"v_s{a}", align_bytes=LINE) for a in range(PASSES)]
        thr_rows = held.tile([P, P], F32, name="thr_rows", align_bytes=LINE)
        ident = held.tile([P, P], F32, name="ident")
        neg_thr = held.tile([P, BLOCKS], F32, name="neg_thr")
        windows = [held.tile([P, T2], F32, name=f"window{i}", align_bytes=LINE) for i in range(3)]

        def zero_on_vector(words):
            count = words.shape[1]
            nc.vector.memset(words[:, 0 : count - 1], 0)
            nc.vector.memset(words[:, count - 1 : count], 0)

        for plane in [wt_s] + v_s:
            zero_on_vector(plane[:].bitcast(I32))
        zero_on_vector(windows[0][:, 0:VECTOR_ZEROES])
        nc.gpsimd.memset(thr_rows[:], 0.0)
        nc.gpsimd.memset(tab_s[0:FLAT, :].bitcast(I32), 0)
        make_identity(nc, ident[:])
        nc.gpsimd.memset(windows[0][:, VECTOR_ZEROES:T2], 0.0)
        nc.gpsimd.memset(windows[1][:], 0.0)
        nc.gpsimd.memset(windows[2][:], 0.0)

        keep_view = keep_words.rearrange("a p c i -> p a (c i)")
        meas_view = meas.rearrange("(p t) j -> p t j", t=PACK)

        def load_table(a):
            nc.sync.dma_start(out=tab_w[a][:], in_=tab_words[a].rearrange("p t i -> p (t i)").bitcast(I32))

        def load_meas(u):
            nc.sync.dma_start(out=meas_sb[u][:], in_=meas_view[:, :, meas_cuts[u] : meas_cuts[u + 1]])

        def load_keep(u):
            nc.sync.dma_start(
                out=keep_sb[u][:], in_=keep_view[:, :, PACK * keep_cuts[u] : PACK * keep_cuts[u + 1]].bitcast(I32)
            )

        def load_wt(u):
            nc.sync.dma_start(
                out=wt_sb[u][:].bitcast(I32), in_=wt_words[0][:, 2 * wt_cuts[u] : 2 * wt_cuts[u + 1]].bitcast(I32)
            )

        def load_wgo(u):
            nc.sync.dma_start(out=wgo_sb[u][:], in_=wgo[:, wgo_cuts[u] : wgo_cuts[u + 1]])

        def load_w1(a):
            nc.sync.dma_start(
                out=w1_raw[a][:], in_=w1[PASS * a : PASS * (a + 1), :].rearrange("(p i) c -> p i c", i=PACK)
            )

        def carry_scale_rows(a, r, cols):
            nc.sync.dma_start(
                out=v_s[a][PLANE + 4 * a + r : P : 32, cols].bitcast(I32),
                in_=v_flat[FLAT + 16 * a + r : FLAT + 16 * a + 16 : 4, cols].bitcast(I32),
            )

        def load_wt_scales(cols):
            for q in range(QUADRANTS):
                nc.sync.dma_start(out=wt_s[q:P:32, cols].bitcast(I32), in_=wt_scales[0, q::4, cols].bitcast(I32))

        def load_keep_scales(cols):
            for q in range(QUADRANTS):
                nc.sync.dma_start(
                    out=keep_s[32 * q + PLANE : 32 * q + PLANE + 8, cols].bitcast(I32),
                    in_=keep_scales[:, 4 * q : 4 * q + 4, cols].bitcast(I32),
                )

        first_half, second_half = slice(0, HALF), slice(HALF, S)

        nc.sync.dma_start(out=tab_s[FLAT:P, :].bitcast(I32), in_=tab_scales.rearrange("a q t -> (a q) t").bitcast(I32))
        nc.sync.dma_start(pick[:], offs)
        load_table(0)
        nc.sync.dma_start(out=thr_rows[THR_ROW : THR_ROW + BLOCKS, :], in_=thr.rearrange("(b p) -> b p", p=P))
        load_wt_scales(slice(0, N))
        load_w1(0)
        nc.sync.dma_start(place[:], offs2)
        for j0 in (0, HALF):
            nc.vector.tensor_copy(v_flat[:, j0 : j0 + HALF], tab_s[:].indirect(pick[:, j0 // 16 : (j0 + HALF) // 16]))
        carries = [(a, r) for a in range(PASSES) for r in range(4)]
        for a, r in carries[:4]:
            carry_scale_rows(a, r, first_half)
        load_w1(1)
        for a, r in carries[4:6]:
            carry_scale_rows(a, r, slice(0, S))
        load_table(1)
        for a, r in carries[6:]:
            carry_scale_rows(a, r, slice(0, S))

        w1_w = [held.tile([P, M], U32, name=f"w1_w{a}", align_bytes=LINE) for a in range(PASSES)]
        w1_s = [held.tile([P, M], U8, name=f"w1_s{a}", align_bytes=LINE) for a in range(PASSES)]
        v_w = {
            (0, 0): held.tile([P, HALF], U32, name="v_w00", align_bytes=LINE),
            (0, 1): held.tile([P, HALF], U32, name="v_w01", align_bytes=LINE),
            (1, 0): held.tile([P, HALF], U32, name="v_w10", align_bytes=LINE),
        }
        h_cuts = [0, SUB, QUARTER, HALF, HALF + QUARTER, S]
        h_grouped = [
            held.tile([P, (j1 - j0) * PACK], BF16, name=f"h_grouped{u}", tag=f"h_grouped{u}", align_bytes=LINE)
            for u, (j0, j1) in enumerate(zip(h_cuts, h_cuts[1:]))
        ]
        h_w = held.tile([P, S], U32, name="h_w", align_bytes=LINE)
        h_s = held.tile([P, S], U8, name="h_s", align_bytes=LINE)
        neg_preds = {
            (q0, u): held.tile([P, BANK], F32, name=f"neg_pred{q0}_{u}")
            for q0 in range(QUARTER, S, QUARTER)
            for u in range(2)
        }
        h_turneds = {j0: held.tile([P, M], BF16, name=f"h_turned{j0}") for j0 in range(QUARTER, S, SUB)}

        def group_w1(a, t0, t1, r0, r1, copy):
            copy(
                out=w1_grouped[a][:, t0:t1, r0:r1, :].rearrange("p t r i -> p r t i"),
                in_=w1_raw[a][:].rearrange("p i (r t) -> p r t i", t=PACK)[:, r0:r1, t0:t1, :],
            )

        def quantize_w1(a, scalar_rows):
            group_w1(a, 0, PACK // 2, 0, scalar_rows, nc.scalar.copy)
            group_w1(a, PACK // 2, PACK, 0, P, nc.vector.tensor_copy)
            if scalar_rows < P:
                group_w1(a, 0, PACK // 2, scalar_rows, P, nc.vector.tensor_copy)
            nc.vector.quantize_mx(
                out=w1_w[a][:].bitcast(FP8X4),
                scales=w1_s[a][:],
                in_=w1_grouped[a][:].rearrange("p t r i -> p (t r i)"),
            )

        def v_cols(a, j0, j1):
            return v_w[a, j0 // HALF][:, j0 % HALF : j0 % HALF + j1 - j0]

        def gather_words(a, j0, j1):
            nc.vector.tensor_copy(v_cols(a, j0, j1), tab_w[a][:].bitcast(U32).indirect(pick[:, j0 // 16 : j1 // 16]))

        def part_of(cuts, first):
            return max(u for u, cut in enumerate(cuts) if cut <= first)

        def meas_cols(j0, j1):
            u = part_of(meas_cuts, j0)
            return meas_sb[u][:, :, j0 - meas_cuts[u] : j1 - meas_cuts[u]]

        def h_cols(j0, j1):
            u = part_of(h_cuts, j0)
            return h_grouped[u][:, PACK * (j0 - h_cuts[u]) : PACK * (j1 - h_cuts[u])]

        def keep_cols(a, b):
            u = part_of(keep_cuts, b * P)
            return keep_sb[u][:, a, b * P - keep_cuts[u] : (b + 1) * P - keep_cuts[u]]

        def wt_cols(b):
            u = part_of(wt_cuts, b * P)
            return wt_sb[u][:, 2 * (b * P - wt_cuts[u]) : 2 * ((b + 1) * P - wt_cuts[u])]

        def wgo_cols(j0, j1):
            u = part_of(wgo_cuts, j0)
            return wgo_sb[u][:, j0 - wgo_cuts[u] : j1 - wgo_cuts[u]]

        def quantize_h(j0, j1):
            nc.vector.quantize_mx(out=h_w[:, j0:j1].bitcast(FP8X4), scales=h_s[:, j0:j1], in_=h_cols(j0, j1))

        gather_words(0, 0, HALF)
        gather_words(0, HALF, S)
        load_meas(0)
        load_meas(1)
        nc.gpsimd.memset(keep_s[:].bitcast(I32), 0)
        load_keep_scales(first_half)
        load_keep(0)
        load_wt(0)
        load_wgo(0)
        load_keep(1)
        quantize_w1(0, 3 * P // 4)
        quantize_w1(1, 3 * P // 4)
        load_keep(2)
        for a, r in carries[:4]:
            carry_scale_rows(a, r, second_half)
        load_meas(2)
        load_keep_scales(second_half)
        load_wt(1)
        load_keep(3)
        load_meas(3)
        load_meas(4)
        windows.append(placed("window3", [P, T2], F32, 37))
        nc.gpsimd.memset(windows[3][:], 0.0)
        gather_words(1, 0, SUB)
        gather_words(1, SUB, QUARTER)
        gather_words(1, QUARTER, HALF)

        def predict(bank, j0, j1, t0, t1):
            width = j1 - j0
            for a in range(PASSES):
                for t in range(t0, t1):
                    ms = slice(t * P, (t + 1) * P)
                    nc.tensor.matmul_mx(
                        out=bank[:, (t - t0) * width : (t - t0 + 1) * width],
                        lhsT=w1_w[a][:, ms].bitcast(FP8X4),
                        lhsT_scale=w1_s[a][:, ms],
                        rhs=v_cols(a, j0, j1).bitcast(FP8X4),
                        rhs_scale=v_s[a][PLANE + 4 * a :, j0:j1],
                        start=(a == 0 and t == t0),
                        stop=(a == PASSES - 1 and t == t1 - 1),
                    )

        def residual_on_vector(j0, bank):
            predict(bank, j0, j0 + SUB, 0, PACK)
            nc.vector.tensor_tensor(
                h_cols(j0, j0 + SUB).rearrange("p (c e t) -> p c t e", e=2, t=PACK),
                meas_cols(j0, j0 + SUB).rearrange("p t (c e) -> p c t e", e=2),
                bank[:].rearrange("p (t c e) -> p c t e", t=PACK, e=2),
                ALU.subtract,
            )

        def predict_out(q0, pair):
            for u, bank in enumerate(pair):
                predict(bank, q0, q0 + QUARTER, 2 * u, 2 * u + 2)
                nc.scalar.mul(neg_preds[q0, u][:], bank[:], -1.0)

        def sum_turned(j0, bank):
            q0 = j0 - j0 % QUARTER
            terms = [meas_cols(j0, j0 + SUB)[:, t, :] for t in range(PACK)] + [
                neg_preds[q0, t // 2][:, (t % 2) * QUARTER + j0 - q0 : (t % 2) * QUARTER + j0 - q0 + SUB]
                for t in range(PACK)
            ]
            for u, term in enumerate(terms):
                t = u % PACK
                nc.tensor.matmul(
                    bank[:, t * P : (t + 1) * P],
                    term,
                    ident[:],
                    is_transpose=True,
                    start=(u == 0),
                    stop=(u == len(terms) - 1),
                )
            nc.scalar.copy(
                h_turneds[j0][:].rearrange("j (u p e) -> j u p e", u=2, e=2),
                bank[:].rearrange("j (u e p) -> j u p e", u=2, e=2),
            )

        def turn_back(q0, bank):
            for s in range(2):
                pairs = h_turneds[q0 + s * SUB][:].bitcast(F32)
                for u in range(2):
                    nc.tensor.transpose(bank[:, (2 * s + u) * P : (2 * s + u + 1) * P], pairs[:, u * P : (u + 1) * P], ident[:])
            nc.scalar.copy(
                h_cols(q0, q0 + QUARTER).bitcast(F32).rearrange("p (s j u) -> p s j u", s=2, u=2),
                bank[:].rearrange("p (s u j) -> p s j u", s=2, u=2),
            )

        ys = {}

        def y_tile(b, j0, j1):
            ys[b, j0] = held.tile([P, j1 - j0], F32, name=f"y{b}_{j0}", tag=f"y{b}_{j0}", align_bytes=LINE)
            return ys[b, j0]

        def shrink(b, j0, j1, y, bank, keep_first=False):
            ns = slice(b * P, (b + 1) * P)
            width = j1 - j0
            keep_passes = [
                (keep_cols(a, b).bitcast(FP8X4), keep_s[PLANE + 4 * a :, ns], v_cols(a, j0, j1), v_s[a][PLANE + 4 * a :, j0:j1])
                for a in reversed(range(PASSES))
            ]
            wt_passes = [(wt_cols(b).bitcast(FP4X4), wt_s[:, ns], h_w[:, j0:j1], h_s[:, j0:j1])]
            passes = keep_passes + wt_passes if keep_first else wt_passes + keep_passes
            for u, (lhs, lhs_scale, rhs, rhs_scale) in enumerate(passes):
                nc.tensor.matmul_mx(
                    out=bank[:, 0:width],
                    lhsT=lhs,
                    lhsT_scale=lhs_scale,
                    rhs=rhs.bitcast(FP8X4),
                    rhs_scale=rhs_scale,
                    start=(u == 0),
                    stop=(u == len(passes) - 1),
                )
            nc.scalar.activation(y, bank[:, 0:width], ACT.Relu, bias=neg_thr[:, b : b + 1])

        def scatter(b, j0, j1):
            nc.vector.tensor_tensor(
                windows[b][:].indirect(place[:, j0 // 16 : j1 // 16]), ys[b, j0][:], wgo_cols(j0, j1), ALU.mult
            )
            if j1 == S:
                nc.sync.dma_start(out=out[b * P : (b + 1) * P, :], in_=windows[b][:])

        def zero_window(after):
            window = held.tile([P, T2], F32, name=f"window{len(windows)}", tag=after, align_bytes=LINE)
            nc.gpsimd.memset(window[:], 0.0)
            windows.append(window)

        def put(b, j0, j1, bank):
            shrink(b, j0, j1, y_tile(b, j0, j1)[:], bank)
            scatter(b, j0, j1)
            if len(windows) < BLOCKS:
                zero_window(f"y{b}_0")

        q1, q2, q3 = QUARTER, HALF, HALF + QUARTER
        residual_on_vector(0, banks[0])
        residual_on_vector(SUB, banks[1])
        quantize_h(0, SUB)
        quantize_h(SUB, q1)
        nc.tensor.transpose(banks[0][:, 0:P], thr_rows[:], ident[:])
        nc.scalar.mul(neg_thr[:], banks[0][:, THR_ROW : THR_ROW + BLOCKS], -1.0)
        v_w[1, 1] = held.tile([P, HALF], U32, name="v_w11", tag="h_grouped0", align_bytes=LINE)
        gather_words(1, HALF, S)
        load_wgo(1)
        zero_window("h_grouped1")

        predict_out(q1, banks[2:4])
        y = y_tile(0, 0, q1)
        for j0, bank in ((0, banks[4]), (SUB, banks[5])):
            shrink(0, j0, j0 + SUB, y[:, j0 : j0 + SUB], bank, keep_first=True)
        scatter(0, 0, q1)
        zero_window("y0_0")
        put(1, 0, q1, banks[6])
        put(2, 0, q1, banks[7])
        put(3, 0, q1, banks[0])
        put(4, 0, q1, banks[5])
        put(5, 0, q1, banks[6])
        sum_turned(q1, banks[1])
        sum_turned(q1 + SUB, banks[2])
        turn_back(q1, banks[6])
        quantize_h(q1, q2)
        put(6, 0, q1, banks[6])
        put(7, 0, q1, banks[6])
        predict_out(q2, banks[3:5])
        sum_turned(q2, banks[7])
        sum_turned(q2 + SUB, banks[0])
        put(0, q1, q2, banks[0])
        predict_out(q3, banks[1:3])
        put(1, q1, q2, banks[0])
        turn_back(q2, banks[3])
        quantize_h(q2, q3)
        sum_turned(q3, banks[4])
        put(2, q1, q2, banks[3])
        sum_turned(q3 + SUB, banks[5])
        put(3, q1, q2, banks[4])
        turn_back(q3, banks[7])
        quantize_h(q3, S)
        put(BRIDGES - 1, q1, q2, banks[7])

        y = y_tile(0, q2, S)
        shrink(0, q2, q3, y[:, 0:QUARTER], banks[5])
        shrink(0, q3, S, y[:, QUARTER:], banks[6], keep_first=True)
        scatter(0, q2, S)
        for b in range(BRIDGES, BLOCKS):
            y = y_tile(b, q1, S)
            shrink(b, q2, S, y[:, QUARTER:], banks[b % 4])
            shrink(b, q1, q2, y[:, 0:QUARTER], banks[7])
            scatter(b, q1, S)
            put(b - BRIDGES + 1, q2, S, banks[4 + b % 2])
        put(BRIDGES - 1, q2, S, banks[4])
